import numpy as np
import ml_dtypes


def mxq(x, axis, fmt="e4m3"):
    dtype, down = {"e4m3": (ml_dtypes.float8_e4m3fn, 7), "e5m2": (ml_dtypes.float8_e5m2, 14)}[fmt]
    v = np.moveaxis(np.asarray(x, np.float32).astype(ml_dtypes.bfloat16).astype(np.float64), axis, -1)
    blocks = v.reshape(v.shape[:-1] + (-1, 32))
    amax = np.abs(blocks).max(-1, keepdims=True)
    byte = np.maximum(np.where(amax > 0, np.frexp(amax)[1] - 1 + 127, 0) - down, 1)
    scale = np.exp2(byte - 127.0)
    codes = (blocks / scale).astype(np.float32).astype(dtype).astype(np.float64)
    return np.moveaxis((codes * scale).reshape(v.shape), -1, axis)


WIDE = False


def mx_kscale(k):
    if not WIDE:
        return np.ones(k)
    levels = np.array([10, -10, 5, -5, 0])
    if k % 512:
        return np.exp2(np.random.permutation(np.resize(levels, k // 32))).repeat(32)
    a = np.empty((k // 512, 16))
    for p in range(k // 512):
        a[p, :8] = np.random.permutation(np.resize(levels, 8))
        for g in range(8):
            far = levels[np.abs(levels - a[p, g]) >= 10]
            a[p, g + 8] = far[np.random.randint(len(far))]
    return np.exp2(a.ravel()).repeat(32)


def f64(x):
    return np.asarray(x).astype(np.float64)


def striped(idx):
    return np.tile(idx.reshape(-1, 16).T, (8, 1)).astype(np.uint16)


def unstriped(offs):
    return offs[:16].T.reshape(-1).astype(np.int64)


E2M1 = np.array([0.0, 0.5, 1.0, 1.5, 2.0, 3.0, 4.0, 6.0, -0.0, -0.5, -1.0, -1.5, -2.0, -3.0, -4.0, -6.0])


def pack_weight(w, fmt):
    k, n = w.shape
    w = f64(np.asarray(w, np.float32).astype(ml_dtypes.bfloat16)).reshape(k // 32, 32, n)
    amax = np.abs(w).max(1)
    if fmt == "e4m3":
        byte = np.frexp(amax)[1] - 1 + 127 - 7
    else:
        mant, ex = np.frexp(amax / 6.0)
        byte = np.where(mant > 0.5, ex, ex - 1) + 127
    byte = np.clip(np.where(amax > 0, byte, 1), 1, 254)
    scaled = (w * np.exp2(127.0 - byte)[:, None, :]).reshape(k, n).astype(np.float32)
    by_word = np.ascontiguousarray(scaled.reshape(k // 512, 128, 4, n).transpose(0, 1, 3, 2))
    if fmt == "e4m3":
        words = by_word.astype(ml_dtypes.float8_e4m3fn).view(np.uint8)
    else:
        c = by_word.astype(ml_dtypes.float4_e2m1fn).view(np.uint8) & 0xF
        words = (c[..., 0::2] | (c[..., 1::2] << 4)).reshape(k // 512, 128, 2 * n)
    return np.ascontiguousarray(words), np.ascontiguousarray(byte.astype(np.uint8).reshape(k // 512, 16, n))


def unpack_weight(words, scales, fmt):
    g, _, n = scales.shape
    words = np.ascontiguousarray(words).reshape(g, 128, n, -1)
    if fmt == "e4m3":
        vals = words.view(ml_dtypes.float8_e4m3fn).astype(np.float64)
    else:
        nib = np.empty((g, 128, n, 4), np.uint8)
        nib[..., 0::2] = words & 0xF
        nib[..., 1::2] = words >> 4
        vals = E2M1[nib]
    vals = vals * np.repeat(np.exp2(scales.astype(np.float64) - 127.0), 8, axis=1)[..., None]
    return vals.transpose(0, 1, 3, 2).reshape(g * 512, n)


def gelu(v):
    return 0.5 * v * (1.0 + np.tanh(np.sqrt(2.0 / np.pi) * (v + 0.044715 * v**3)))


K, K2, H, N, T, T2, S, P = 1024, 512, 1024, 512, 2048, 1024, 512, 512

def setup_inputs():
    n = np.random.standard_normal
    s = mx_kscale(K)[:, None]
    s2 = mx_kscale(K2)[:, None]
    u = mx_kscale(H)[:, None]
    tab_words, tab_scales = pack_weight(n((K, T)) * s, "e4m3")
    offs = striped(np.random.permutation(T)[:P])
    base = (n((K2, T2)) * s2).astype(np.float32)
    xs = (np.round(16 * n((K2, S))) / 16 * s2).astype(np.float32)
    offs2 = striped(np.random.permutation(T2)[:S])
    offs3 = striped(np.random.permutation(T2)[:P])
    w1 = (n((K2, H)) * 0.35 / np.sqrt(K2) / s2).astype(np.float32)
    w2_words, w2_scales = pack_weight(n((K, H)) * 0.35 / np.sqrt(K) / s, "e2m1")
    gain = (np.exp(0.3 * n(H)) * u[:, 0]).astype(np.float32)
    wo = (n((H, N)) * 2.0 / np.sqrt(H) / u).astype(np.float32)
    w3_words, w3_scales = pack_weight(n((K, N)) / np.sqrt(K) / s, "e4m3")
    return {"tab_words": tab_words, "tab_scales": tab_scales, "offs": offs,
            "base": base, "xs": xs, "offs2": offs2, "offs3": offs3, "w1": w1,
            "w2_words": w2_words, "w2_scales": w2_scales, "gain": gain, "wo": wo,
            "w3_words": w3_words, "w3_scales": w3_scales}

def reference(tab_words, tab_scales, offs, base, xs, offs2, offs3, w1,
              w2_words, w2_scales, gain, wo, w3_words, w3_scales):
    v = unpack_weight(tab_words, tab_scales, "e4m3")[:, unstriped(offs)]
    w2 = unpack_weight(w2_words, w2_scales, "e2m1")
    w3 = unpack_weight(w3_words, w3_scales, "e4m3")
    page = f64(base).copy()
    page[:, unstriped(offs2)] = f64(xs)
    a = mxq(f64(w1), 0, "e4m3").T @ mxq(page, 0, "e4m3")
    b = w2.T @ v
    h = f64(gain)[:, None] * np.sin(a[:, unstriped(offs3)] + b)
    y = mxq(f64(wo), 0, "e4m3").T @ mxq(h, 0, "e4m3")
    d = w3.T @ v
    return y * d

@@ -1,0 +1,351 @@
+from contextlib import ExitStack
+
+import concourse.mybir as mybir
+from concourse.masks import make_identity
+
+K, K2, H, N, T, T2, S, J = 1024, 512, 1024, 512, 2048, 1024, 512, 512
+FLOPS = 2 * (K2 * H * T2 + K * H * J + H * N * J + K * N * J)
+
+F32 = mybir.dt.float32
+BF16 = mybir.dt.bfloat16
+I32 = mybir.dt.int32
+U32 = mybir.dt.uint32
+U16 = mybir.dt.uint16
+U8 = mybir.dt.uint8
+FP8X4 = mybir.dt.float8_e4m3fn_x4
+FP4X4 = mybir.dt.float4_e2m1fn_x4
+SIN = mybir.ActivationFunctionType.Sin
+ADD = mybir.AluOpType.add
+MULT = mybir.AluOpType.mult
+
+P = 128
+PACK = 4
+PASS = P * PACK
+BANK = 512
+
+
+def tile_list_place_context_kernel(
+    tc, tab_words, tab_scales, offs, base, xs, offs2, offs3, w1, w2_words, w2_scales, gain, wo, w3_words, w3_scales, out
+):
+    nc = tc.nc
+    with ExitStack() as ctx:
+        lists = ctx.enter_context(tc.tile_pool(name="lists", bufs=1))
+        keep = ctx.enter_context(tc.tile_pool(name="keep", bufs=1))
+        wide = ctx.enter_context(tc.tile_pool(name="wide", bufs=4))
+        arows = ctx.enter_context(tc.tile_pool(name="arows", bufs=6))
+        args = ctx.enter_context(tc.tile_pool(name="args", bufs=3))
+        psum = ctx.enter_context(tc.psum_pool(name="psum", bufs=4))
+
+        def mx_tiles(name, width):
+            codes = keep.tile([P, width], U32, name=name + "_codes", align_bytes=64)
+            scales = keep.tile([P, width], U8, name=name + "_scales", align_bytes=64)
+            return codes, scales
+
+        def quantize(operand, grouped):
+            codes, scales = operand
+            nc.vector.quantize_mx(out=codes[:].bitcast(FP8X4), scales=scales[:], in_=grouped)
+
+        def weave_views(grouped, planes):
+            return (
+                grouped.rearrange("p (c i t) -> p c t i", i=4, t=PACK),
+                planes.rearrange("p t (c i) -> p c t i", i=4),
+            )
+
+        idx = lists.tile([P, J // 16], U16, name="idx")
+        idx2 = lists.tile([P, S // 16], U16, name="idx2")
+        idx3 = lists.tile([P, J // 16], U16, name="idx3")
+
+        tab_sc = keep.tile([P, T], U8, name="tab_sc", align_bytes=64)
+        w2_sc_raw = keep.tile([P, 2, H], U8, name="w2_sc_raw", align_bytes=64)
+        w3_sc = keep.tile([P, 2, N], U8, name="w3_sc", align_bytes=64)
+        v_sc1 = keep.tile([P, J], U8, name="v_sc1", align_bytes=64)
+        zero = keep.tile([P, 1], F32, name="zero")
+        zero_bias = keep.tile([P, 1], F32, name="zero_bias")
+        nc.gpsimd.memset(tab_sc[:].bitcast(I32), 0)
+        nc.gpsimd.memset(w2_sc_raw[:].rearrange("p a c -> p (a c)").bitcast(I32), 0)
+        nc.vector.memset(zero[:], 0.0)
+        nc.scalar.activation(out=zero_bias[:], in_=zero[:], func=SIN)
+        nc.vector.memset(w3_sc[:].rearrange("p a c -> p (a c)").bitcast(I32), 0)
+        nc.vector.memset(v_sc1[:].bitcast(I32), 0)
+        gain_rows = keep.tile([P, PASS], F32, name="gain_rows")
+        nc.vector.memset(gain_rows[:], 0.0)
+        identity = keep.tile([P, P], F32, name="identity")
+        make_identity(nc, identity[:])
+
+        page = [keep.tile([P, T2], F32, name="page%d" % t) for t in range(PACK)]
+        fresh_first = keep.tile([P, S], F32, name="fresh_first")
+        fresh_rest = keep.tile([P, PACK - 1, S], F32, name="fresh_rest")
+        fresh = [fresh_first[:]] + [fresh_rest[:, t, :] for t in range(PACK - 1)]
+        base_rows = base.rearrange("(p t) c -> t p c", t=PACK)
+        xs_rows = xs.rearrange("(p t) c -> p t c", t=PACK)
+        page_bf = [keep.tile([P, PACK, BANK], BF16, name="page_bf%d" % h, align_bytes=64) for h in range(2)]
+
+        def load_plane(t):
+            nc.sync.dma_start(out=page[t][:], in_=base_rows[t])
+            if t == 0:
+                nc.sync.dma_start(out=fresh_first[:], in_=xs_rows[:, 0, :])
+            if t == 1:
+                nc.sync.dma_start(out=fresh_rest[:], in_=xs_rows[:, 1:PACK, :])
+
+        def scatter_plane(t):
+            nc.vector.tensor_copy(page[t][:].indirect(idx2[:]), fresh[t])
+
+        def round_plane(t):
+            for h in (1, 0):
+                src = page[t][:, h * BANK : (h + 1) * BANK]
+                if t == PACK - 1:
+                    nc.vector.tensor_copy(out=page_bf[h][:, t, :], in_=src)
+                else:
+                    nc.scalar.copy(out=page_bf[h][:, t, :], in_=src)
+
+        def load_scale_rows(tile, dram):
+            for q in range(4):
+                nc.sync.dma_start(
+                    out=tile[32 * q : 32 * q + 4, :, :].bitcast(I32),
+                    in_=dram[:, 4 * q : 4 * q + 4, :].rearrange("a r c -> r a c").bitcast(I32),
+                )
+
+        w1_raw = []
+        w1_q = [mx_tiles("w1_%d" % b, PASS) for b in range(2)]
+
+        def load_w1(b):
+            raw = wide.tile([P, PACK, PASS], F32, name="w1_raw", tag="wide")
+            nc.sync.dma_start(out=raw[:], in_=w1[:, b * PASS : (b + 1) * PASS].rearrange("(p j) r -> p j r", j=PACK))
+            w1_raw.append(raw)
+
+        def quantize_w1(b):
+            grouped = keep.tile([P, PASS * PACK], BF16, name="w1_bf%d" % b, align_bytes=64)
+            copy = nc.scalar.copy if b == 0 else nc.vector.tensor_copy
+            copy(
+                out=grouped[:].rearrange("p (t q e j) -> p t q j e", t=4, e=4, j=4),
+                in_=w1_raw[b][:].rearrange("p j (q t e) -> p t q j e", t=4, e=4),
+            )
+            quantize(w1_q[b], grouped[:])
+
+        nc.sync.dma_start(idx2[:], offs2)
+        load_plane(0)
+        for q in range(4):
+            nc.sync.dma_start(
+                out=tab_sc[32 * q : 32 * q + 8, :].bitcast(I32), in_=tab_scales[:, 4 * q : 4 * q + 4, :].bitcast(I32)
+            )
+        nc.sync.dma_start(idx[:], offs)
+        tab = [keep.tile([P, T], I32, name="tab%d" % a) for a in range(2)]
+        for a in range(2):
+            nc.sync.dma_start(out=tab[a][:], in_=tab_words[a].rearrange("p t i -> p (t i)").bitcast(I32))
+        w2_raw = keep.tile([P, 2, 2 * H], U8, name="w2_raw", align_bytes=64)
+        nc.sync.dma_start(out=w2_raw[:].bitcast(I32), in_=w2_words.rearrange("a p c -> p a c").bitcast(I32))
+        load_scale_rows(w2_sc_raw, w2_scales)
+        load_plane(1)
+        nc.sync.dma_start(out=gain_rows[0:2, :], in_=gain.rearrange("(b r) -> b r", b=2))
+        load_w1(0)
+        load_plane(2)
+        load_plane(3)
+        nc.sync.dma_start(idx3[:], offs3)
+        w3_codes = keep.tile([P, 2, N], I32, name="w3_codes", align_bytes=64)
+        nc.sync.dma_start(out=w3_codes[:], in_=w3_words.rearrange("a p c i -> p a (c i)").bitcast(I32))
+        load_scale_rows(w3_sc, w3_scales)
+        load_w1(1)
+        wo_raw = []
+        for b in range(2):
+            raw = wide.tile([P, PACK, N], F32, name="wo_raw", tag="wide")
+            rows = wo[b * PASS : (b + 1) * PASS, :].rearrange("(q t e) n -> t q e n", t=4, e=4)
+            for t in range(PACK):
+                nc.sync.dma_start(out=raw[:, t, :], in_=rows[t])
+            wo_raw.append(raw)
+
+        scatter_plane(0)
+        round_plane(0)
+        v_sc0 = keep.tile([P, J], U8, name="v_sc0", align_bytes=64)
+        nc.vector.tensor_copy(v_sc0[:], tab_sc[:].indirect(idx[:]))
+        for q in range(4):
+            nc.scalar.dma_start(
+                out=v_sc1[32 * q : 32 * q + 4, :].bitcast(I32), in_=v_sc0[32 * q + 4 : 32 * q + 8, :].bitcast(I32)
+            )
+        v_sc = [v_sc0, v_sc1]
+        v_codes = [keep.tile([P, J], U32, name="v_codes%d" % a, align_bytes=64) for a in range(2)]
+        for a in range(2):
+            nc.vector.tensor_copy(v_codes[a][:], tab[a][:].bitcast(U32).indirect(idx[:]))
+
+        w2_codes = keep.tile([P, 2 * 2 * H], U8, name="w2_codes", align_bytes=64)
+        w2_sc = keep.tile([P, 2 * H], U8, name="w2_sc", align_bytes=64)
+        nc.vector.tensor_copy(
+            out=w2_codes[:].bitcast(I32).rearrange("p (g t q e) -> p g t q e", t=4, q=32, e=2),
+            in_=w2_raw[:].rearrange("p a c -> p (a c)").bitcast(I32).rearrange("p (g q t e) -> p g t q e", t=4, q=32, e=2),
+        )
+        nc.vector.tensor_copy(
+            out=w2_sc[:].bitcast(I32).rearrange("p (g t q) -> p g t q", t=4, q=32),
+            in_=w2_sc_raw[:].rearrange("p a c -> p (a c)").bitcast(I32).rearrange("p (g q t) -> p g t q", t=4, q=32),
+        )
+
+        b_rows = []
+        for i in range(H // P):
+            acc = psum.tile([P, BANK], F32, name="acc", tag="acc")
+            for a in range(2):
+                col = a * H + i * P
+                nc.tensor.matmul_mx(
+                    out=acc[:],
+                    lhsT=w2_codes[:, 2 * col : 2 * (col + P)].bitcast(FP4X4),
+                    lhsT_scale=w2_sc[:, col : col + P],
+                    rhs=v_codes[a][:].bitcast(FP8X4),
+                    rhs_scale=v_sc[a][:],
+                    start=(a == 0),
+                    stop=(a == 1),
+                )
+            rows = keep.tile([P, J], F32, name="b_rows%d" % i)
+            nc.scalar.copy(out=rows[:], in_=acc[:])
+            b_rows.append(rows)
+
+        scatter_plane(1)
+        quantize_w1(0)
+        round_plane(1)
+        scatter_plane(2)
+        round_plane(2)
+
+        gain_planes = keep.tile([P, PACK, P], F32, name="gain_planes")
+        nc.scalar.copy(
+            out=gain_planes[:].rearrange("p t (q e) -> p t q e", e=4),
+            in_=gain_rows[:].rearrange("p (q t e) -> p t q e", t=4, e=4),
+        )
+        turned = psum.tile([P, PACK, P], F32, name="turned", tag="y")
+        for t in range(PACK):
+            nc.tensor.transpose(turned[:, t, :], gain_planes[:, t, :], identity[:])
+        gains = keep.tile([P, 2, PACK], F32, name="gains")
+        nc.scalar.copy(out=gains[:], in_=turned[:, :, 0:2].rearrange("p t b -> p b t"))
+
+        scatter_plane(3)
+        round_plane(3)
+        page_q = [mx_tiles("page_%d" % h, BANK) for h in range(2)]
+        page_grouped = [
+            keep.tile([P, BANK * PACK], BF16, name="page_grouped%d" % h, align_bytes=64) for h in range(2)
+        ]
+        share = 384
+        for copy, h, c0, c1 in (
+            (nc.scalar.copy, 1, 0, share),
+            (nc.vector.tensor_copy, 0, 0, BANK),
+            (nc.vector.tensor_copy, 1, share, BANK),
+        ):
+            dst, src = weave_views(page_grouped[h][:, c0 * PACK : c1 * PACK], page_bf[h][:, :, c0:c1])
+            copy(out=dst, in_=src)
+        for h in range(2):
+            quantize(page_q[h], page_grouped[h][:])
+
+        def project(i):
+            b, t = divmod(i, PACK)
+            rows = arows.tile([P, T2], F32, name="a_rows")
+            for h in range(2):
+                acc = psum.tile([P, BANK], F32, name="acc", tag="acc")
+                nc.tensor.matmul_mx(
+                    out=acc[:],
+                    lhsT=w1_q[b][0][:, t * P : (t + 1) * P].bitcast(FP8X4),
+                    lhsT_scale=w1_q[b][1][:, t * P : (t + 1) * P],
+                    rhs=page_q[h][0][:].bitcast(FP8X4),
+                    rhs_scale=page_q[h][1][:],
+                    start=True,
+                    stop=True,
+                )
+                nc.scalar.copy(out=rows[:, h * BANK : (h + 1) * BANK], in_=acc[:])
+            return rows
+
+        sines = [wide.tile([P, PACK, J], F32, name="sines", tag="wide") for b in range(2)]
+
+        def sine(i, rows, j0, j1):
+            b, t = divmod(i, PACK)
+            arg = args.tile([P, J], F32, name="arg")
+            nc.vector.tensor_tensor(
+                arg[:, 0 : j1 - j0], rows[:].indirect(idx3[:, j0 // 16 : j1 // 16]), b_rows[i][:, j0:j1], ADD
+            )
+            nc.scalar.activation(out=sines[b][:, t, j0:j1], in_=arg[:, 0 : j1 - j0], func=SIN, bias=zero_bias[:])
+
+        def quantize_h(b, j0, j1):
+            width = j1 - j0
+            grouped = keep.tile([P, width * PACK], BF16, name="h_bf%d_%d" % (b, j0), align_bytes=64)
+            dst, src = weave_views(grouped[:], sines[b][:, :, j0:j1])
+            factor = gains[:, b, :].unsqueeze(1).unsqueeze(3).to_broadcast([P, width // 4, PACK, 4])
+            nc.vector.tensor_tensor(dst, src, factor, MULT)
+            operand = mx_tiles("h_%d_%d" % (b, j0), width)
+            quantize(operand, grouped[:])
+            return operand
+
+        wo_q = [mx_tiles("wo_%d" % b, N) for b in range(2)]
+
+        def round_wo(b):
+            grouped = keep.tile([P, N * PACK], BF16, name="wo_bf%d" % b, align_bytes=64)
+            for n0 in range(0, N, 256):
+                dst, src = weave_views(grouped[:, n0 * PACK : (n0 + 256) * PACK], wo_raw[b][:, :, n0 : n0 + 256])
+                copy = nc.vector.tensor_copy if b == 0 else nc.scalar.copy
+                copy(out=dst, in_=src)
+            return grouped
+
+        a_rows = [project(0), project(1)]
+        quantize_w1(1)
+        for i in range(PACK):
+            sine(i, a_rows[i], 0, J)
+            a_rows.append(project(i + 2))
+        wo_bf0 = round_wo(0)
+        half = J // 2
+        sine(4, a_rows[4], 0, half)
+        a_rows.append(project(6))
+        h0 = quantize_h(0, 0, J)
+        sine(5, a_rows[5], 0, half)
+        a_rows.append(project(7))
+        quantize(wo_q[0], wo_bf0[:])
+        wo_bf1 = round_wo(1)
+        sine(6, a_rows[6], 0, half)
+        sine(7, a_rows[7], 0, half)
+        quantize(wo_q[1], wo_bf1[:])
+
+        d_rows = []
+        for nt in range(N // P):
+            acc = psum.tile([P, BANK], F32, name="d_acc", tag="y")
+            for a in range(2):
+                nc.tensor.matmul_mx(
+                    out=acc[:],
+                    lhsT=w3_codes[:, a, nt * P : (nt + 1) * P].bitcast(FP8X4),
+                    lhsT_scale=w3_sc[:, a, nt * P : (nt + 1) * P],
+                    rhs=v_codes[a][:].bitcast(FP8X4),
+                    rhs_scale=v_sc[a][:],
+                    start=(a == 0),
+                    stop=(a == 1),
+                )
+            rows = keep.tile([P, J], F32, name="d_rows%d" % nt)
+            nc.scalar.copy(out=rows[:], in_=acc[:])
+            d_rows.append(rows)
+
+        def y_pass(acc, nt, b, operand, cols):
+            nc.tensor.matmul_mx(
+                out=acc[:],
+                lhsT=wo_q[b][0][:, nt * P : (nt + 1) * P].bitcast(FP8X4),
+                lhsT_scale=wo_q[b][1][:, nt * P : (nt + 1) * P],
+                rhs=operand[0][:, cols].bitcast(FP8X4),
+                rhs_scale=operand[1][:, cols],
+                start=(b == 0),
+                stop=(b == 1),
+            )
+
+        y_acc = []
+        for c in range(2):
+            accs = [psum.tile([P, half], F32, name="y_acc", tag=("y" if c == 0 else "acc")) for nt in range(N // P)]
+            for nt in range(N // P):
+                y_pass(accs[nt], nt, 0, h0, slice(c * half, (c + 1) * half))
+            y_acc.append(accs)
+
+        out_rows = out.rearrange("(nt p) j -> p nt j", p=P)
+
+        def finish(c, h1):
+            result = keep.tile([P, N // P, half], F32, name="result%d" % c)
+            cols = slice(c * half, (c + 1) * half)
+            for nt in range(N // P):
+                y_pass(y_acc[c][nt], nt, 1, h1, slice(0, half))
+            for nt in range(N // P):
+                nc.vector.tensor_tensor(result[:, nt, :], y_acc[c][nt][:], d_rows[nt][:, cols], MULT)
+                if nt % 2 == 1:
+                    nc.sync.dma_start(out=out_rows[:, nt - 1 : nt + 1, cols], in_=result[:, nt - 1 : nt + 1, :])
+
+        sine(4, a_rows[4], half, J)
+        sine(5, a_rows[5], half, J)
+        h1a = quantize_h(1, 0, half)
+        sine(6, a_rows[6], half, J)
+        sine(7, a_rows[7], half, J)
+        finish(0, h1a)
+        h1b = quantize_h(1, half, J)
+        finish(1, h1b)

@@ -31,19 +31,20 @@ def tile_list_place_context_kernel(
     with ExitStack() as ctx:
         lists = ctx.enter_context(tc.tile_pool(name="lists", bufs=1))
         keep = ctx.enter_context(tc.tile_pool(name="keep", bufs=1))
-        wide = ctx.enter_context(tc.tile_pool(name="wide", bufs=4))
+        wide = ctx.enter_context(tc.tile_pool(name="wide", bufs=3))
         arows = ctx.enter_context(tc.tile_pool(name="arows", bufs=6))
-        args = ctx.enter_context(tc.tile_pool(name="args", bufs=3))
-        psum = ctx.enter_context(tc.psum_pool(name="psum", bufs=4))
+        args = ctx.enter_context(tc.tile_pool(name="args", bufs=5))
+        psum = ctx.enter_context(tc.psum_pool(name="psum", bufs=3))
+        psum_b = ctx.enter_context(tc.psum_pool(name="psum_b", bufs=2))
 
         def mx_tiles(name, width):
             codes = keep.tile([P, width], U32, name=name + "_codes", align_bytes=64)
             scales = keep.tile([P, width], U8, name=name + "_scales", align_bytes=64)
-            return codes, scales
+            return codes[:], scales[:]
 
         def quantize(operand, grouped):
             codes, scales = operand
-            nc.vector.quantize_mx(out=codes[:].bitcast(FP8X4), scales=scales[:], in_=grouped)
+            nc.vector.quantize_mx(out=codes.bitcast(FP8X4), scales=scales, in_=grouped)
 
         def weave_views(grouped, planes):
             return (
@@ -61,107 +62,145 @@ def tile_list_place_context_kernel(
         v_sc1 = keep.tile([P, J], U8, name="v_sc1", align_bytes=64)
         zero = keep.tile([P, 1], F32, name="zero")
         zero_bias = keep.tile([P, 1], F32, name="zero_bias")
-        nc.gpsimd.memset(tab_sc[:].bitcast(I32), 0)
-        nc.gpsimd.memset(w2_sc_raw[:].rearrange("p a c -> p (a c)").bitcast(I32), 0)
+        nc.vector.memset(w2_sc_raw[:].rearrange("p a c -> p (a c)").bitcast(I32), 0)
+        nc.vector.memset(tab_sc[:].bitcast(I32), 0)
         nc.vector.memset(zero[:], 0.0)
         nc.scalar.activation(out=zero_bias[:], in_=zero[:], func=SIN)
         nc.vector.memset(w3_sc[:].rearrange("p a c -> p (a c)").bitcast(I32), 0)
         nc.vector.memset(v_sc1[:].bitcast(I32), 0)
-        gain_rows = keep.tile([P, PASS], F32, name="gain_rows")
+        gain_rows = keep.tile([P, P], F32, name="gain_rows")
         nc.vector.memset(gain_rows[:], 0.0)
         identity = keep.tile([P, P], F32, name="identity")
         make_identity(nc, identity[:])
 
-        page = [keep.tile([P, T2], F32, name="page%d" % t) for t in range(PACK)]
-        fresh_first = keep.tile([P, S], F32, name="fresh_first")
-        fresh_rest = keep.tile([P, PACK - 1, S], F32, name="fresh_rest")
-        fresh = [fresh_first[:]] + [fresh_rest[:, t, :] for t in range(PACK - 1)]
+        page = [keep.tile([P, T2], F32, name="page%d" % t, tag="page%d" % t, align_bytes=64) for t in range(PACK)]
+        fresh_early = [keep.tile([P, S], F32, name="fresh%d" % t) for t in range(2)]
+        fresh_rest = keep.tile([P, 2, S], F32, name="fresh_rest", tag="reused", align_bytes=64)
+        fresh = [fresh_early[0][:], fresh_early[1][:], fresh_rest[:, 0, :], fresh_rest[:, 1, :]]
         base_rows = base.rearrange("(p t) c -> t p c", t=PACK)
         xs_rows = xs.rearrange("(p t) c -> p t c", t=PACK)
-        page_bf = [keep.tile([P, PACK, BANK], BF16, name="page_bf%d" % h, align_bytes=64) for h in range(2)]
-
-        def load_plane(t):
-            nc.sync.dma_start(out=page[t][:], in_=base_rows[t])
-            if t == 0:
-                nc.sync.dma_start(out=fresh_first[:], in_=xs_rows[:, 0, :])
-            if t == 1:
-                nc.sync.dma_start(out=fresh_rest[:], in_=xs_rows[:, 1:PACK, :])
 
         def scatter_plane(t):
             nc.vector.tensor_copy(page[t][:].indirect(idx2[:]), fresh[t])
 
         def round_plane(t):
-            for h in (1, 0):
-                src = page[t][:, h * BANK : (h + 1) * BANK]
-                if t == PACK - 1:
-                    nc.vector.tensor_copy(out=page_bf[h][:, t, :], in_=src)
-                else:
-                    nc.scalar.copy(out=page_bf[h][:, t, :], in_=src)
+            copy = nc.vector.tensor_copy if t == PACK - 1 else nc.scalar.copy
+            copy(out=page_bf[:, t, :], in_=page[t][:])
 
-        def load_scale_rows(tile, dram):
+        def load_scale_rows(queue, tile, dram):
             for q in range(4):
-                nc.sync.dma_start(
+                queue.dma_start(
                     out=tile[32 * q : 32 * q + 4, :, :].bitcast(I32),
                     in_=dram[:, 4 * q : 4 * q + 4, :].rearrange("a r c -> r a c").bitcast(I32),
                 )
 
         w1_raw = []
-        w1_q = [mx_tiles("w1_%d" % b, PASS) for b in range(2)]
 
         def load_w1(b):
-            raw = wide.tile([P, PACK, PASS], F32, name="w1_raw", tag="wide")
+            if b == 0:
+                raw = keep.tile([P, PACK, PASS], F32, name="w1_raw", tag="page_bf", align_bytes=64)
+            else:
+                raw = wide.tile([P, PACK, PASS], F32, name="w1_raw", tag="wide")
             nc.sync.dma_start(out=raw[:], in_=w1[:, b * PASS : (b + 1) * PASS].rearrange("(p j) r -> p j r", j=PACK))
             w1_raw.append(raw)
 
-        def quantize_w1(b):
+        def round_w1(b):
             grouped = keep.tile([P, PASS * PACK], BF16, name="w1_bf%d" % b, align_bytes=64)
-            copy = nc.scalar.copy if b == 0 else nc.vector.tensor_copy
-            copy(
+            nc.scalar.copy(
                 out=grouped[:].rearrange("p (t q e j) -> p t q j e", t=4, e=4, j=4),
                 in_=w1_raw[b][:].rearrange("p j (q t e) -> p t q j e", t=4, e=4),
             )
-            quantize(w1_q[b], grouped[:])
+            return grouped
 
-        nc.sync.dma_start(idx2[:], offs2)
-        load_plane(0)
-        for q in range(4):
-            nc.sync.dma_start(
-                out=tab_sc[32 * q : 32 * q + 8, :].bitcast(I32), in_=tab_scales[:, 4 * q : 4 * q + 4, :].bitcast(I32)
-            )
-        nc.sync.dma_start(idx[:], offs)
-        tab = [keep.tile([P, T], I32, name="tab%d" % a) for a in range(2)]
-        for a in range(2):
-            nc.sync.dma_start(out=tab[a][:], in_=tab_words[a].rearrange("p t i -> p (t i)").bitcast(I32))
-        w2_raw = keep.tile([P, 2, 2 * H], U8, name="w2_raw", align_bytes=64)
-        nc.sync.dma_start(out=w2_raw[:].bitcast(I32), in_=w2_words.rearrange("a p c -> p a c").bitcast(I32))
-        load_scale_rows(w2_sc_raw, w2_scales)
-        load_plane(1)
-        nc.sync.dma_start(out=gain_rows[0:2, :], in_=gain.rearrange("(b r) -> b r", b=2))
-        load_w1(0)
-        load_plane(2)
-        load_plane(3)
-        nc.sync.dma_start(idx3[:], offs3)
-        w3_codes = keep.tile([P, 2, N], I32, name="w3_codes", align_bytes=64)
-        nc.sync.dma_start(out=w3_codes[:], in_=w3_words.rearrange("a p c i -> p a (c i)").bitcast(I32))
-        load_scale_rows(w3_sc, w3_scales)
-        load_w1(1)
         wo_raw = []
-        for b in range(2):
-            raw = wide.tile([P, PACK, N], F32, name="wo_raw", tag="wide")
+
+        def load_wo(b):
+            if b == 0:
+                raw = keep.tile([P, PACK, N], F32, name="wo_raw", tag="relay", align_bytes=64)
+            else:
+                raw = wide.tile([P, PACK, N], F32, name="wo_raw", tag="wide")
             rows = wo[b * PASS : (b + 1) * PASS, :].rearrange("(q t e) n -> t q e n", t=4, e=4)
             for t in range(PACK):
                 nc.sync.dma_start(out=raw[:, t, :], in_=rows[t])
             wo_raw.append(raw)
 
+        def round_wo(b):
+            grouped = keep.tile([P, N * PACK], BF16, name="wo_bf%d" % b, align_bytes=64)
+            for n0 in range(0, N, 256):
+                dst, src = weave_views(grouped[:, n0 * PACK : (n0 + 256) * PACK], wo_raw[b][:, :, n0 : n0 + 256])
+                copy = nc.vector.tensor_copy if b == 1 else nc.scalar.copy
+                copy(out=dst, in_=src)
+            return grouped
+
+        tab = [keep.tile([P, T], I32, name="tab%d" % a) for a in range(2)]
+        w2_raw = keep.tile([P, 2, 2 * H], U8, name="w2_raw", align_bytes=64)
+        w3_codes = keep.tile([P, 2, N], I32, name="w3_codes", align_bytes=64)
+
+        def load_table_scales(q):
+            nc.sync.dma_start(
+                out=tab_sc[32 * q : 32 * q + 8, :].bitcast(I32), in_=tab_scales[:, 4 * q : 4 * q + 4, :].bitcast(I32)
+            )
+
+        load_scale_rows(nc.gpsimd, w2_sc_raw, w2_scales)
+        nc.sync.dma_start(idx2[:], offs2)
+        for t in range(2):
+            nc.sync.dma_start(out=page[t][:], in_=base_rows[t])
+            nc.sync.dma_start(out=fresh[t], in_=xs_rows[:, t, :])
+        load_w1(0)
+        nc.sync.dma_start(out=page[2][:], in_=base_rows[2])
+        nc.sync.dma_start(out=fresh_rest[:], in_=xs_rows[:, 2:PACK, :])
+        load_w1(1)
+        nc.sync.dma_start(idx[:], offs)
+        nc.sync.dma_start(out=page[3][:], in_=base_rows[3])
+        load_wo(0)
+        for q in range(4):
+            load_table_scales(q)
+        for a in range(2):
+            nc.sync.dma_start(out=tab[a][:], in_=tab_words[a].rearrange("p t i -> p (t i)").bitcast(I32))
+        nc.sync.dma_start(out=w2_raw[:].bitcast(I32), in_=w2_words.rearrange("a p c -> p a c").bitcast(I32))
+        page_bf = keep.tile([P, PACK, T2], BF16, name="page_bf", tag="page_bf", align_bytes=64)
+
         scatter_plane(0)
+        w1_bf = [round_w1(0)]
         round_plane(0)
-        v_sc0 = keep.tile([P, J], U8, name="v_sc0", align_bytes=64)
+        scatter_plane(1)
+        round_plane(1)
+        w1_bf.append(round_w1(1))
+        scatter_plane(2)
+        round_plane(2)
+        wo_bf = [round_wo(0)]
+        scatter_plane(3)
+        round_plane(3)
+
+        page_q = mx_tiles("page", T2)
+        first_codes = keep.tile([P, PASS], U32, name="first_codes", tag="page3", align_bytes=64)
+        late_codes = keep.tile([P, 3, PASS], U32, name="late_codes", tag="page_bf", align_bytes=64)
+        scale_planes = [keep.tile([P, PASS], U8, name="scales%d" % u, align_bytes=64) for u in range(4)]
+        w1_q = [(first_codes[:], scale_planes[0][:]), (late_codes[:, 0, :], scale_planes[1][:])]
+        wo_q = [(late_codes[:, 1 + b, :], scale_planes[2 + b][:]) for b in range(2)]
+        page_grouped = keep.tile([P, T2 * PACK], BF16, name="page_grouped", tag="relay", align_bytes=64)
+        dst, src = weave_views(page_grouped[:], page_bf[:])
+        nc.scalar.copy(out=dst, in_=src)
+        quantize(page_q, page_grouped[:])
+        quantize(w1_q[0], w1_bf[0][:])
+
+        v_sc0 = keep.tile([P, J], U8, name="v_sc0", tag="reused", align_bytes=64)
         nc.vector.tensor_copy(v_sc0[:], tab_sc[:].indirect(idx[:]))
         for q in range(4):
-            nc.scalar.dma_start(
+            nc.sync.dma_start(
                 out=v_sc1[32 * q : 32 * q + 4, :].bitcast(I32), in_=v_sc0[32 * q + 4 : 32 * q + 8, :].bitcast(I32)
             )
         v_sc = [v_sc0, v_sc1]
+        nc.sync.dma_start(idx3[:], offs3)
+        load_wo(1)
+        for b in range(2):
+            nc.sync.dma_start(
+                out=gain_rows[PACK * b : PACK * (b + 1), :].rearrange("t (q e) -> t q e", e=4),
+                in_=gain[b * PASS : (b + 1) * PASS].rearrange("(q t e) -> t q e", t=4, e=4),
+            )
+        nc.sync.dma_start(out=w3_codes[:], in_=w3_words.rearrange("a p c i -> p a (c i)").bitcast(I32))
+        load_scale_rows(nc.sync, w3_sc, w3_scales)
+
         v_codes = [keep.tile([P, J], U32, name="v_codes%d" % a, align_bytes=64) for a in range(2)]
         for a in range(2):
             nc.vector.tensor_copy(v_codes[a][:], tab[a][:].bitcast(U32).indirect(idx[:]))
@@ -176,60 +215,15 @@ def tile_list_place_context_kernel(
             out=w2_sc[:].bitcast(I32).rearrange("p (g t q) -> p g t q", t=4, q=32),
             in_=w2_sc_raw[:].rearrange("p a c -> p (a c)").bitcast(I32).rearrange("p (g q t) -> p g t q", t=4, q=32),
         )
+        quantize(w1_q[1], w1_bf[1][:])
+        quantize(wo_q[0], wo_bf[0][:])
 
-        b_rows = []
-        for i in range(H // P):
-            acc = psum.tile([P, BANK], F32, name="acc", tag="acc")
-            for a in range(2):
-                col = a * H + i * P
-                nc.tensor.matmul_mx(
-                    out=acc[:],
-                    lhsT=w2_codes[:, 2 * col : 2 * (col + P)].bitcast(FP4X4),
-                    lhsT_scale=w2_sc[:, col : col + P],
-                    rhs=v_codes[a][:].bitcast(FP8X4),
-                    rhs_scale=v_sc[a][:],
-                    start=(a == 0),
-                    stop=(a == 1),
-                )
-            rows = keep.tile([P, J], F32, name="b_rows%d" % i)
-            nc.scalar.copy(out=rows[:], in_=acc[:])
-            b_rows.append(rows)
-
-        scatter_plane(1)
-        quantize_w1(0)
-        round_plane(1)
-        scatter_plane(2)
-        round_plane(2)
-
-        gain_planes = keep.tile([P, PACK, P], F32, name="gain_planes")
-        nc.scalar.copy(
-            out=gain_planes[:].rearrange("p t (q e) -> p t q e", e=4),
-            in_=gain_rows[:].rearrange("p (q t e) -> p t q e", t=4, e=4),
-        )
-        turned = psum.tile([P, PACK, P], F32, name="turned", tag="y")
-        for t in range(PACK):
-            nc.tensor.transpose(turned[:, t, :], gain_planes[:, t, :], identity[:])
+        turned = psum.tile([P, P], F32, name="turned", tag="y")
+        nc.tensor.transpose(turned[:], gain_rows[:], identity[:])
         gains = keep.tile([P, 2, PACK], F32, name="gains")
-        nc.scalar.copy(out=gains[:], in_=turned[:, :, 0:2].rearrange("p t b -> p b t"))
+        nc.scalar.copy(out=gains[:].rearrange("p b t -> p (b t)"), in_=turned[:, 0 : 2 * PACK])
 
-        scatter_plane(3)
-        round_plane(3)
-        page_q = [mx_tiles("page_%d" % h, BANK) for h in range(2)]
-        page_grouped = [
-            keep.tile([P, BANK * PACK], BF16, name="page_grouped%d" % h, align_bytes=64) for h in range(2)
-        ]
-        share = 384
-        for copy, h, c0, c1 in (
-            (nc.scalar.copy, 1, 0, share),
-            (nc.vector.tensor_copy, 0, 0, BANK),
-            (nc.vector.tensor_copy, 1, share, BANK),
-        ):
-            dst, src = weave_views(page_grouped[h][:, c0 * PACK : c1 * PACK], page_bf[h][:, :, c0:c1])
-            copy(out=dst, in_=src)
-        for h in range(2):
-            quantize(page_q[h], page_grouped[h][:])
-
-        def project(i):
+        def project_page(i):
             b, t = divmod(i, PACK)
             rows = arows.tile([P, T2], F32, name="a_rows")
             for h in range(2):
@@ -238,64 +232,77 @@ def tile_list_place_context_kernel(
                     out=acc[:],
                     lhsT=w1_q[b][0][:, t * P : (t + 1) * P].bitcast(FP8X4),
                     lhsT_scale=w1_q[b][1][:, t * P : (t + 1) * P],
-                    rhs=page_q[h][0][:].bitcast(FP8X4),
-                    rhs_scale=page_q[h][1][:],
+                    rhs=page_q[0][:, h * BANK : (h + 1) * BANK].bitcast(FP8X4),
+                    rhs_scale=page_q[1][:, h * BANK : (h + 1) * BANK],
                     start=True,
                     stop=True,
                 )
                 nc.scalar.copy(out=rows[:, h * BANK : (h + 1) * BANK], in_=acc[:])
             return rows
 
+        def project_objects(acc, i, j0, j1):
+            for a in range(2):
+                col = a * H + i * P
+                nc.tensor.matmul_mx(
+                    out=acc,
+                    lhsT=w2_codes[:, 2 * col : 2 * (col + P)].bitcast(FP4X4),
+                    lhsT_scale=w2_sc[:, col : col + P],
+                    rhs=v_codes[a][:, j0:j1].bitcast(FP8X4),
+                    rhs_scale=v_sc[a][:, j0:j1],
+                    start=(a == 0),
+                    stop=(a == 1),
+                )
+
         sines = [wide.tile([P, PACK, J], F32, name="sines", tag="wide") for b in range(2)]
+        a_rows = []
 
-        def sine(i, rows, j0, j1):
-            b, t = divmod(i, PACK)
+        b_rows = {}
+
+        def stage_objects(i):
+            acc = psum_b.tile([P, BANK], F32, name="b_acc")
+            project_objects(acc[:], i, 0, J)
+            rows = keep.tile([P, J], F32, name="b_rows%d" % i)
+            copy = nc.vector.tensor_copy if 0 < i < PACK else nc.scalar.copy
+            copy(out=rows[:], in_=acc[:])
+            b_rows[i] = rows
+
+        def gather(tiles, j0, j1):
+            width = j1 - j0
             arg = args.tile([P, J], F32, name="arg")
-            nc.vector.tensor_tensor(
-                arg[:, 0 : j1 - j0], rows[:].indirect(idx3[:, j0 // 16 : j1 // 16]), b_rows[i][:, j0:j1], ADD
-            )
-            nc.scalar.activation(out=sines[b][:, t, j0:j1], in_=arg[:, 0 : j1 - j0], func=SIN, bias=zero_bias[:])
+            for u, i in enumerate(tiles):
+                nc.vector.tensor_tensor(
+                    arg[:, u * width : (u + 1) * width],
+                    a_rows[i][:].indirect(idx3[:, j0 // 16 : j1 // 16]),
+                    b_rows[i][:, j0:j1],
+                    ADD,
+                )
+            return arg, tiles, j0, j1
 
-        def quantize_h(b, j0, j1):
+        def sine(arg, tiles, j0, j1):
+            b, t = divmod(tiles[0], PACK)
+            nc.scalar.activation(
+                out=sines[b][:, t : t + len(tiles), j0:j1],
+                in_=arg[:].rearrange("p (u j) -> p u j", j=j1 - j0),
+                func=SIN,
+                bias=zero_bias[:],
+            )
+
+        def weigh(b, j0, j1):
             width = j1 - j0
             grouped = keep.tile([P, width * PACK], BF16, name="h_bf%d_%d" % (b, j0), align_bytes=64)
             dst, src = weave_views(grouped[:], sines[b][:, :, j0:j1])
             factor = gains[:, b, :].unsqueeze(1).unsqueeze(3).to_broadcast([P, width // 4, PACK, 4])
             nc.vector.tensor_tensor(dst, src, factor, MULT)
-            operand = mx_tiles("h_%d_%d" % (b, j0), width)
+            return grouped
+
+        def quantize_h(name, grouped, width):
+            operand = mx_tiles(name, width)
             quantize(operand, grouped[:])
             return operand
 
-        wo_q = [mx_tiles("wo_%d" % b, N) for b in range(2)]
+        d_rows = keep.tile([P, N // P, J], F32, name="d_rows")
 
-        def round_wo(b):
-            grouped = keep.tile([P, N * PACK], BF16, name="wo_bf%d" % b, align_bytes=64)
-            for n0 in range(0, N, 256):
-                dst, src = weave_views(grouped[:, n0 * PACK : (n0 + 256) * PACK], wo_raw[b][:, :, n0 : n0 + 256])
-                copy = nc.vector.tensor_copy if b == 0 else nc.scalar.copy
-                copy(out=dst, in_=src)
-            return grouped
-
-        a_rows = [project(0), project(1)]
-        quantize_w1(1)
-        for i in range(PACK):
-            sine(i, a_rows[i], 0, J)
-            a_rows.append(project(i + 2))
-        wo_bf0 = round_wo(0)
-        half = J // 2
-        sine(4, a_rows[4], 0, half)
-        a_rows.append(project(6))
-        h0 = quantize_h(0, 0, J)
-        sine(5, a_rows[5], 0, half)
-        a_rows.append(project(7))
-        quantize(wo_q[0], wo_bf0[:])
-        wo_bf1 = round_wo(1)
-        sine(6, a_rows[6], 0, half)
-        sine(7, a_rows[7], 0, half)
-        quantize(wo_q[1], wo_bf1[:])
-
-        d_rows = []
-        for nt in range(N // P):
+        def modulation(nt):
             acc = psum.tile([P, BANK], F32, name="d_acc", tag="y")
             for a in range(2):
                 nc.tensor.matmul_mx(
@@ -307,13 +314,42 @@ def tile_list_place_context_kernel(
                     start=(a == 0),
                     stop=(a == 1),
                 )
-            rows = keep.tile([P, J], F32, name="d_rows%d" % nt)
-            nc.scalar.copy(out=rows[:], in_=acc[:])
-            d_rows.append(rows)
+            nc.scalar.copy(out=d_rows[:, nt, :], in_=acc[:])
+
+        half = J // 2
+        sums = []
+        for i in range(PACK):
+            a_rows.append(project_page(i))
+            stage_objects(i)
+            sums.append(gather([i], 0, J))
+        wo_bf.append(round_wo(1))
+        quantize(wo_q[1], wo_bf[1][:])
+        for i in range(2):
+            sine(*sums[i])
+            a_rows.append(project_page(PACK + i))
+            stage_objects(PACK + i)
+        sine(*sums[2])
+        sine(*sums[3])
+        low_first = gather([4, 5], 0, half)
+        h0_bf = weigh(0, 0, J)
+        for i in range(6, 8):
+            a_rows.append(project_page(i))
+            stage_objects(i)
+        low_last = gather([4, 5], half, J)
+        h0 = quantize_h("h0", h0_bf, J)
+        high_first = gather([6, 7], 0, half)
+        high_last = gather([6, 7], half, J)
+        sine(*low_first)
+        sine(*low_last)
+        sine(*high_first)
+        modulation(0)
+        sine(*high_last)
+        for nt in range(1, N // P):
+            modulation(nt)
 
         def y_pass(acc, nt, b, operand, cols):
             nc.tensor.matmul_mx(
-                out=acc[:],
+                out=acc,
                 lhsT=wo_q[b][0][:, nt * P : (nt + 1) * P].bitcast(FP8X4),
                 lhsT_scale=wo_q[b][1][:, nt * P : (nt + 1) * P],
                 rhs=operand[0][:, cols].bitcast(FP8X4),
@@ -322,30 +358,32 @@ def tile_list_place_context_kernel(
                 stop=(b == 1),
             )
 
-        y_acc = []
-        for c in range(2):
-            accs = [psum.tile([P, half], F32, name="y_acc", tag=("y" if c == 0 else "acc")) for nt in range(N // P)]
-            for nt in range(N // P):
-                y_pass(accs[nt], nt, 0, h0, slice(c * half, (c + 1) * half))
-            y_acc.append(accs)
-
         out_rows = out.rearrange("(nt p) j -> p nt j", p=P)
+        first, last = slice(0, half), slice(half, J)
 
-        def finish(c, h1):
-            result = keep.tile([P, N // P, half], F32, name="result%d" % c)
-            cols = slice(c * half, (c + 1) * half)
-            for nt in range(N // P):
-                y_pass(y_acc[c][nt], nt, 1, h1, slice(0, half))
-            for nt in range(N // P):
-                nc.vector.tensor_tensor(result[:, nt, :], y_acc[c][nt][:], d_rows[nt][:, cols], MULT)
-                if nt % 2 == 1:
-                    nc.sync.dma_start(out=out_rows[:, nt - 1 : nt + 1, cols], in_=result[:, nt - 1 : nt + 1, :])
+        h1a_bf = weigh(1, 0, half)
+        h1a = quantize_h("h1a", h1a_bf, half)
+        h1b_bf = weigh(1, half, J)
 
-        sine(4, a_rows[4], half, J)
-        sine(5, a_rows[5], half, J)
-        h1a = quantize_h(1, 0, half)
-        sine(6, a_rows[6], half, J)
-        sine(7, a_rows[7], half, J)
-        finish(0, h1a)
-        h1b = quantize_h(1, half, J)
-        finish(1, h1b)
+        y_last = [psum.tile([P, half], F32, name="y_last", tag=("acc" if nt < 3 else "y")) for nt in range(N // P)]
+        for nt in range(N // P):
+            y_pass(y_last[nt][:], nt, 0, h0, last)
+
+        result = keep.tile([P, N // P, half], F32, name="result_first")
+        for pair in range(2):
+            acc = psum.tile([P, 2, half], F32, name="y_first", tag="y")
+            for u in range(2):
+                y_pass(acc[:, u, :], 2 * pair + u, 0, h0, first)
+                y_pass(acc[:, u, :], 2 * pair + u, 1, h1a, first)
+            rows = slice(2 * pair, 2 * pair + 2)
+            nc.vector.tensor_tensor(result[:, rows, :], acc[:], d_rows[:, rows, first], MULT)
+        nc.sync.dma_start(out=out_rows[:, :, first], in_=result[:])
+
+        h1b = quantize_h("h1b", h1b_bf, half)
+        for nt in range(N // P):
+            y_pass(y_last[nt][:], nt, 1, h1b, first)
+        for nt in range(N // P):
+            result = keep.tile([P, half], F32, name="result_last%d" % nt)
+            nc.vector.tensor_tensor(result[:], y_last[nt][:], d_rows[:, nt, last], MULT)
+            queue = nc.sync if nt % 2 == 0 else nc.scalar
+            queue.dma_start(out=out_rows[:, nt, last], in_=result[:])

@@ -32,10 +32,10 @@ def tile_list_place_context_kernel(
         lists = ctx.enter_context(tc.tile_pool(name="lists", bufs=1))
         keep = ctx.enter_context(tc.tile_pool(name="keep", bufs=1))
         wide = ctx.enter_context(tc.tile_pool(name="wide", bufs=3))
-        arows = ctx.enter_context(tc.tile_pool(name="arows", bufs=6))
-        args = ctx.enter_context(tc.tile_pool(name="args", bufs=5))
-        psum = ctx.enter_context(tc.psum_pool(name="psum", bufs=3))
-        psum_b = ctx.enter_context(tc.psum_pool(name="psum_b", bufs=2))
+        arows = ctx.enter_context(tc.tile_pool(name="arows", bufs=7))
+        args = ctx.enter_context(tc.tile_pool(name="args", bufs=6))
+        psum = ctx.enter_context(tc.psum_pool(name="psum", bufs=2))
+        psum_b = ctx.enter_context(tc.psum_pool(name="psum_b", bufs=4))
 
         def mx_tiles(name, width):
             codes = keep.tile([P, width], U32, name=name + "_codes", align_bytes=64)
@@ -128,12 +128,11 @@ def tile_list_place_context_kernel(
             grouped = keep.tile([P, N * PACK], BF16, name="wo_bf%d" % b, align_bytes=64)
             for n0 in range(0, N, 256):
                 dst, src = weave_views(grouped[:, n0 * PACK : (n0 + 256) * PACK], wo_raw[b][:, :, n0 : n0 + 256])
-                copy = nc.vector.tensor_copy if b == 1 else nc.scalar.copy
-                copy(out=dst, in_=src)
+                nc.scalar.copy(out=dst, in_=src)
             return grouped
 
         tab = [keep.tile([P, T], I32, name="tab%d" % a) for a in range(2)]
-        w2_raw = keep.tile([P, 2, 2 * H], U8, name="w2_raw", align_bytes=64)
+        w2_raw = keep.tile([P, 2, 2 * H], U8, name="w2_raw", tag="w2_raw", align_bytes=64)
         w3_codes = keep.tile([P, 2, N], I32, name="w3_codes", align_bytes=64)
 
         def load_table_scales(q):
@@ -155,6 +154,7 @@ def tile_list_place_context_kernel(
         load_wo(0)
         for q in range(4):
             load_table_scales(q)
+        load_wo(1)
         for a in range(2):
             nc.sync.dma_start(out=tab[a][:], in_=tab_words[a].rearrange("p t i -> p (t i)").bitcast(I32))
         nc.sync.dma_start(out=w2_raw[:].bitcast(I32), in_=w2_words.rearrange("a p c -> p a c").bitcast(I32))
@@ -172,16 +172,18 @@ def tile_list_place_context_kernel(
         scatter_plane(3)
         round_plane(3)
 
-        page_q = mx_tiles("page", T2)
+        page_q = [mx_tiles("page%d" % h, BANK) for h in range(2)]
         first_codes = keep.tile([P, PASS], U32, name="first_codes", tag="page3", align_bytes=64)
         late_codes = keep.tile([P, 3, PASS], U32, name="late_codes", tag="page_bf", align_bytes=64)
         scale_planes = [keep.tile([P, PASS], U8, name="scales%d" % u, align_bytes=64) for u in range(4)]
         w1_q = [(first_codes[:], scale_planes[0][:]), (late_codes[:, 0, :], scale_planes[1][:])]
         wo_q = [(late_codes[:, 1 + b, :], scale_planes[2 + b][:]) for b in range(2)]
         page_grouped = keep.tile([P, T2 * PACK], BF16, name="page_grouped", tag="relay", align_bytes=64)
-        dst, src = weave_views(page_grouped[:], page_bf[:])
-        nc.scalar.copy(out=dst, in_=src)
-        quantize(page_q, page_grouped[:])
+        for h in range(2):
+            grouped = page_grouped[:, h * BANK * PACK : (h + 1) * BANK * PACK]
+            dst, src = weave_views(grouped, page_bf[:, :, h * BANK : (h + 1) * BANK])
+            nc.scalar.copy(out=dst, in_=src)
+            quantize(page_q[h], grouped)
         quantize(w1_q[0], w1_bf[0][:])
 
         v_sc0 = keep.tile([P, J], U8, name="v_sc0", tag="reused", align_bytes=64)
@@ -192,7 +194,6 @@ def tile_list_place_context_kernel(
             )
         v_sc = [v_sc0, v_sc1]
         nc.sync.dma_start(idx3[:], offs3)
-        load_wo(1)
         for b in range(2):
             nc.sync.dma_start(
                 out=gain_rows[PACK * b : PACK * (b + 1), :].rearrange("t (q e) -> t q e", e=4),
@@ -218,7 +219,7 @@ def tile_list_place_context_kernel(
         quantize(w1_q[1], w1_bf[1][:])
         quantize(wo_q[0], wo_bf[0][:])
 
-        turned = psum.tile([P, P], F32, name="turned", tag="y")
+        turned = psum.tile([P, P], F32, name="turned", tag="y", bufs=2)
         nc.tensor.transpose(turned[:], gain_rows[:], identity[:])
         gains = keep.tile([P, 2, PACK], F32, name="gains")
         nc.scalar.copy(out=gains[:].rearrange("p b t -> p (b t)"), in_=turned[:, 0 : 2 * PACK])
@@ -232,8 +233,8 @@ def tile_list_place_context_kernel(
                     out=acc[:],
                     lhsT=w1_q[b][0][:, t * P : (t + 1) * P].bitcast(FP8X4),
                     lhsT_scale=w1_q[b][1][:, t * P : (t + 1) * P],
-                    rhs=page_q[0][:, h * BANK : (h + 1) * BANK].bitcast(FP8X4),
-                    rhs_scale=page_q[1][:, h * BANK : (h + 1) * BANK],
+                    rhs=page_q[h][0].bitcast(FP8X4),
+                    rhs_scale=page_q[h][1],
                     start=True,
                     stop=True,
                 )
@@ -259,12 +260,21 @@ def tile_list_place_context_kernel(
         b_rows = {}
 
         def stage_objects(i):
-            acc = psum_b.tile([P, BANK], F32, name="b_acc")
+            acc = psum_b.tile([P, BANK], F32, name="b_acc", tag="b")
             project_objects(acc[:], i, 0, J)
             rows = keep.tile([P, J], F32, name="b_rows%d" % i)
-            copy = nc.vector.tensor_copy if 0 < i < PACK else nc.scalar.copy
+            copy = nc.vector.tensor_copy if i == 9 else nc.scalar.copy
             copy(out=rows[:], in_=acc[:])
             b_rows[i] = rows
+
+        def gather_then_add(i):
+            acc = psum_b.tile([P, BANK], F32, name="b_acc", tag="b")
+            project_objects(acc[:], i, 0, J)
+            picked = keep.tile([P, J], F32, name="picked%d" % i)
+            arg = args.tile([P, J], F32, name="arg")
+            nc.vector.tensor_copy(picked[:], a_rows[i][:].indirect(idx3[:]))
+            nc.vector.tensor_tensor(arg[:], acc[:], picked[:], ADD)
+            return arg, [i], 0, J
 
         def gather(tiles, j0, j1):
             width = j1 - j0
@@ -303,7 +313,7 @@ def tile_list_place_context_kernel(
         d_rows = keep.tile([P, N // P, J], F32, name="d_rows")
 
         def modulation(nt):
-            acc = psum.tile([P, BANK], F32, name="d_acc", tag="y")
+            acc = psum.tile([P, BANK], F32, name="d_acc", tag="y", bufs=2)
             for a in range(2):
                 nc.tensor.matmul_mx(
                     out=acc[:],
@@ -320,32 +330,34 @@ def tile_list_place_context_kernel(
         sums = []
         for i in range(PACK):
             a_rows.append(project_page(i))
+            if i < 2:
+                sums.append(gather_then_add(i))
+            else:
+                stage_objects(i)
+                sums.append(gather([i], 0, J))
+        for i in range(4, 6):
+            a_rows.append(project_page(i))
             stage_objects(i)
-            sums.append(gather([i], 0, J))
-        wo_bf.append(round_wo(1))
-        quantize(wo_q[1], wo_bf[1][:])
-        for i in range(2):
+        for i in range(PACK):
             sine(*sums[i])
-            a_rows.append(project_page(PACK + i))
-            stage_objects(PACK + i)
-        sine(*sums[2])
-        sine(*sums[3])
-        low_first = gather([4, 5], 0, half)
+        low = [gather([i], 0, J) for i in range(4, 6)]
         h0_bf = weigh(0, 0, J)
         for i in range(6, 8):
             a_rows.append(project_page(i))
             stage_objects(i)
-        low_last = gather([4, 5], half, J)
         h0 = quantize_h("h0", h0_bf, J)
         high_first = gather([6, 7], 0, half)
         high_last = gather([6, 7], half, J)
-        sine(*low_first)
-        sine(*low_last)
-        sine(*high_first)
+        sine(*low[0])
+        sine(*low[1])
+        wo_bf.append(round_wo(1))
+        quantize(wo_q[1], wo_bf[1][:])
         modulation(0)
+        sine(*high_first)
+        modulation(1)
         sine(*high_last)
-        for nt in range(1, N // P):
-            modulation(nt)
+        modulation(2)
+        modulation(3)
 
         def y_pass(acc, nt, b, operand, cols):
             nc.tensor.matmul_mx(
@@ -365,19 +377,20 @@ def tile_list_place_context_kernel(
         h1a = quantize_h("h1a", h1a_bf, half)
         h1b_bf = weigh(1, half, J)
 
-        y_last = [psum.tile([P, half], F32, name="y_last", tag=("acc" if nt < 3 else "y")) for nt in range(N // P)]
+        y_last = [psum.tile([P, half], F32, name="y_last", tag="acc") for nt in range(2)]
+        y_last.extend([psum_b.tile([P, half], F32, name="y_last", tag="b") for nt in range(2)])
         for nt in range(N // P):
             y_pass(y_last[nt][:], nt, 0, h0, last)
 
         result = keep.tile([P, N // P, half], F32, name="result_first")
         for pair in range(2):
-            acc = psum.tile([P, 2, half], F32, name="y_first", tag="y")
+            acc = psum.tile([P, 2, half], F32, name="y_first", tag="y", bufs=2)
             for u in range(2):
                 y_pass(acc[:, u, :], 2 * pair + u, 0, h0, first)
                 y_pass(acc[:, u, :], 2 * pair + u, 1, h1a, first)
             rows = slice(2 * pair, 2 * pair + 2)
             nc.vector.tensor_tensor(result[:, rows, :], acc[:], d_rows[:, rows, first], MULT)
-        nc.sync.dma_start(out=out_rows[:, :, first], in_=result[:])
+            nc.sync.dma_start(out=out_rows[:, rows, first], in_=result[:, rows, :])
 
         h1b = quantize_h("h1b", h1b_bf, half)
         for nt in range(N // P):

@@ -288,6 +288,8 @@ def tile_list_place_context_kernel(
                 )
             return arg, tiles, j0, j1
 
+        h_planes = [keep.tile([P, PACK, J], BF16, name="h_planes%d" % b, align_bytes=64) for b in range(2)]
+
         def sine(arg, tiles, j0, j1):
             b, t = divmod(tiles[0], PACK)
             nc.scalar.activation(
@@ -296,13 +298,16 @@ def tile_list_place_context_kernel(
                 func=SIN,
                 bias=zero_bias[:],
             )
+            for u in range(t, t + len(tiles)):
+                nc.vector.tensor_scalar(
+                    h_planes[b][:, u, j0:j1], sines[b][:, u, j0:j1], gains[:, b, u : u + 1], None, MULT
+                )
 
         def weigh(b, j0, j1):
             width = j1 - j0
             grouped = keep.tile([P, width * PACK], BF16, name="h_bf%d_%d" % (b, j0), align_bytes=64)
-            dst, src = weave_views(grouped[:], sines[b][:, :, j0:j1])
-            factor = gains[:, b, :].unsqueeze(1).unsqueeze(3).to_broadcast([P, width // 4, PACK, 4])
-            nc.vector.tensor_tensor(dst, src, factor, MULT)
+            dst, src = weave_views(grouped[:], h_planes[b][:, :, j0:j1])
+            nc.vector.tensor_copy(out=dst, in_=src)
             return grouped
 
         def quantize_h(name, grouped, width):

@@ -22,6 +22,12 @@ P = 128
 PACK = 4
 PASS = P * PACK
 BANK = 512
+BANK_BYTES = 4 * BANK
+TILES = H // P
+HALF = J // 2
+QUARTER = H // 4
+FROM_BANK = 1
+AHEAD = 4
 
 
 def tile_list_place_context_kernel(
@@ -31,11 +37,13 @@ def tile_list_place_context_kernel(
     with ExitStack() as ctx:
         lists = ctx.enter_context(tc.tile_pool(name="lists", bufs=1))
         keep = ctx.enter_context(tc.tile_pool(name="keep", bufs=1))
-        wide = ctx.enter_context(tc.tile_pool(name="wide", bufs=3))
-        arows = ctx.enter_context(tc.tile_pool(name="arows", bufs=7))
-        args = ctx.enter_context(tc.tile_pool(name="args", bufs=6))
-        psum = ctx.enter_context(tc.psum_pool(name="psum", bufs=2))
-        psum_b = ctx.enter_context(tc.psum_pool(name="psum_b", bufs=4))
+        arows = ctx.enter_context(tc.tile_pool(name="arows", bufs=AHEAD + 1))
+        ring = ctx.enter_context(tc.tile_pool(name="ring", bufs=4))
+        shared = ctx.enter_context(tc.tile_pool(name="shared", bufs=1))
+        psum = ctx.enter_context(tc.psum_pool(name="psum", bufs=1))
+
+        def bank_tile(name, bank):
+            return psum.tile([P, BANK], F32, name=name, offset=bank * BANK_BYTES)
 
         def mx_tiles(name, width):
             codes = keep.tile([P, width], U32, name=name + "_codes", align_bytes=64)
@@ -46,10 +54,13 @@ def tile_list_place_context_kernel(
             codes, scales = operand
             nc.vector.quantize_mx(out=codes.bitcast(FP8X4), scales=scales, in_=grouped)
 
-        def weave_views(grouped, planes):
-            return (
-                grouped.rearrange("p (c i t) -> p c t i", i=4, t=PACK),
-                planes.rearrange("p t (c i) -> p c t i", i=4),
+        def pair_slot(pairs, t):
+            return pairs.rearrange("p (s c e) -> p s c e", s=2, e=2)[:, t // 2, :, t % 2]
+
+        def weave(copy, word, grouped, pairs):
+            copy(
+                out=grouped.bitcast(word).rearrange("p (c s) -> p c s", s=2),
+                in_=pairs.bitcast(word).rearrange("p (s c) -> p c s", s=2),
             )
 
         idx = lists.tile([P, J // 16], U16, name="idx")
@@ -62,255 +73,203 @@ def tile_list_place_context_kernel(
         v_sc1 = keep.tile([P, J], U8, name="v_sc1", align_bytes=64)
         zero = keep.tile([P, 1], F32, name="zero")
         zero_bias = keep.tile([P, 1], F32, name="zero_bias")
-        nc.vector.memset(w2_sc_raw[:].rearrange("p a c -> p (a c)").bitcast(I32), 0)
-        nc.vector.memset(tab_sc[:].bitcast(I32), 0)
-        nc.vector.memset(zero[:], 0.0)
-        nc.scalar.activation(out=zero_bias[:], in_=zero[:], func=SIN)
-        nc.vector.memset(w3_sc[:].rearrange("p a c -> p (a c)").bitcast(I32), 0)
-        nc.vector.memset(v_sc1[:].bitcast(I32), 0)
         gain_rows = keep.tile([P, P], F32, name="gain_rows")
-        nc.vector.memset(gain_rows[:], 0.0)
         identity = keep.tile([P, P], F32, name="identity")
+        nc.gpsimd.memset(tab_sc[:].bitcast(I32), 0)
+        nc.vector.memset(zero[:], 0.0)
+        nc.vector.memset(v_sc1[:].bitcast(I32), 0)
+        nc.vector.memset(w2_sc_raw[:].rearrange("p a c -> p (a c)").bitcast(I32), 0)
+        nc.vector.memset(w3_sc[:].rearrange("p a c -> p (a c)").bitcast(I32), 0)
+        nc.vector.memset(gain_rows[:], 0.0)
         make_identity(nc, identity[:])
 
-        page = [keep.tile([P, T2], F32, name="page%d" % t, tag="page%d" % t, align_bytes=64) for t in range(PACK)]
-        fresh_early = [keep.tile([P, S], F32, name="fresh%d" % t) for t in range(2)]
-        fresh_rest = keep.tile([P, 2, S], F32, name="fresh_rest", tag="reused", align_bytes=64)
-        fresh = [fresh_early[0][:], fresh_early[1][:], fresh_rest[:, 0, :], fresh_rest[:, 1, :]]
-        base_rows = base.rearrange("(p t) c -> t p c", t=PACK)
-        xs_rows = xs.rearrange("(p t) c -> p t c", t=PACK)
-
-        def scatter_plane(t):
-            nc.vector.tensor_copy(page[t][:].indirect(idx2[:]), fresh[t])
-
-        def round_plane(t):
-            copy = nc.vector.tensor_copy if t == PACK - 1 else nc.scalar.copy
-            copy(out=page_bf[:, t, :], in_=page[t][:])
-
-        def load_scale_rows(queue, tile, dram):
+        def load_scale_rows(tile, dram):
             for q in range(4):
-                queue.dma_start(
+                nc.sync.dma_start(
                     out=tile[32 * q : 32 * q + 4, :, :].bitcast(I32),
                     in_=dram[:, 4 * q : 4 * q + 4, :].rearrange("a r c -> r a c").bitcast(I32),
                 )
 
-        w1_raw = []
-
-        def load_w1(b):
-            if b == 0:
-                raw = keep.tile([P, PACK, PASS], F32, name="w1_raw", tag="page_bf", align_bytes=64)
-            else:
-                raw = wide.tile([P, PACK, PASS], F32, name="w1_raw", tag="wide")
-            nc.sync.dma_start(out=raw[:], in_=w1[:, b * PASS : (b + 1) * PASS].rearrange("(p j) r -> p j r", j=PACK))
-            w1_raw.append(raw)
-
-        def round_w1(b):
-            grouped = keep.tile([P, PASS * PACK], BF16, name="w1_bf%d" % b, align_bytes=64)
-            nc.scalar.copy(
-                out=grouped[:].rearrange("p (t q e j) -> p t q j e", t=4, e=4, j=4),
-                in_=w1_raw[b][:].rearrange("p j (q t e) -> p t q j e", t=4, e=4),
-            )
-            return grouped
-
-        wo_raw = []
-
-        def load_wo(b):
-            if b == 0:
-                raw = keep.tile([P, PACK, N], F32, name="wo_raw", tag="relay", align_bytes=64)
-            else:
-                raw = wide.tile([P, PACK, N], F32, name="wo_raw", tag="wide")
-            rows = wo[b * PASS : (b + 1) * PASS, :].rearrange("(q t e) n -> t q e n", t=4, e=4)
-            for t in range(PACK):
-                nc.sync.dma_start(out=raw[:, t, :], in_=rows[t])
-            wo_raw.append(raw)
-
-        def round_wo(b):
-            grouped = keep.tile([P, N * PACK], BF16, name="wo_bf%d" % b, align_bytes=64)
-            for n0 in range(0, N, 256):
-                dst, src = weave_views(grouped[:, n0 * PACK : (n0 + 256) * PACK], wo_raw[b][:, :, n0 : n0 + 256])
-                nc.scalar.copy(out=dst, in_=src)
-            return grouped
-
-        tab = [keep.tile([P, T], I32, name="tab%d" % a) for a in range(2)]
-        w2_raw = keep.tile([P, 2, 2 * H], U8, name="w2_raw", tag="w2_raw", align_bytes=64)
-        w3_codes = keep.tile([P, 2, N], I32, name="w3_codes", align_bytes=64)
-
-        def load_table_scales(q):
-            nc.sync.dma_start(
+        nc.sync.dma_start(idx[:], offs)
+        nc.sync.dma_start(idx2[:], offs2)
+        for q in range(4):
+            nc.scalar.dma_start(
                 out=tab_sc[32 * q : 32 * q + 8, :].bitcast(I32), in_=tab_scales[:, 4 * q : 4 * q + 4, :].bitcast(I32)
             )
-
-        load_scale_rows(nc.gpsimd, w2_sc_raw, w2_scales)
-        nc.sync.dma_start(idx2[:], offs2)
-        for t in range(2):
-            nc.sync.dma_start(out=page[t][:], in_=base_rows[t])
-            nc.sync.dma_start(out=fresh[t], in_=xs_rows[:, t, :])
-        load_w1(0)
-        nc.sync.dma_start(out=page[2][:], in_=base_rows[2])
-        nc.sync.dma_start(out=fresh_rest[:], in_=xs_rows[:, 2:PACK, :])
-        load_w1(1)
-        nc.sync.dma_start(idx[:], offs)
-        nc.sync.dma_start(out=page[3][:], in_=base_rows[3])
-        load_wo(0)
-        for q in range(4):
-            load_table_scales(q)
-        load_wo(1)
-        for a in range(2):
-            nc.sync.dma_start(out=tab[a][:], in_=tab_words[a].rearrange("p t i -> p (t i)").bitcast(I32))
-        nc.sync.dma_start(out=w2_raw[:].bitcast(I32), in_=w2_words.rearrange("a p c -> p a c").bitcast(I32))
-        page_bf = keep.tile([P, PACK, T2], BF16, name="page_bf", tag="page_bf", align_bytes=64)
-
-        scatter_plane(0)
-        w1_bf = [round_w1(0)]
-        round_plane(0)
-        scatter_plane(1)
-        round_plane(1)
-        w1_bf.append(round_w1(1))
-        scatter_plane(2)
-        round_plane(2)
-        wo_bf = [round_wo(0)]
-        scatter_plane(3)
-        round_plane(3)
-
-        page_q = [mx_tiles("page%d" % h, BANK) for h in range(2)]
-        first_codes = keep.tile([P, PASS], U32, name="first_codes", tag="page3", align_bytes=64)
-        late_codes = keep.tile([P, 3, PASS], U32, name="late_codes", tag="page_bf", align_bytes=64)
-        scale_planes = [keep.tile([P, PASS], U8, name="scales%d" % u, align_bytes=64) for u in range(4)]
-        w1_q = [(first_codes[:], scale_planes[0][:]), (late_codes[:, 0, :], scale_planes[1][:])]
-        wo_q = [(late_codes[:, 1 + b, :], scale_planes[2 + b][:]) for b in range(2)]
-        page_grouped = keep.tile([P, T2 * PACK], BF16, name="page_grouped", tag="relay", align_bytes=64)
-        for h in range(2):
-            grouped = page_grouped[:, h * BANK * PACK : (h + 1) * BANK * PACK]
-            dst, src = weave_views(grouped, page_bf[:, :, h * BANK : (h + 1) * BANK])
-            nc.scalar.copy(out=dst, in_=src)
-            quantize(page_q[h], grouped)
-        quantize(w1_q[0], w1_bf[0][:])
-
-        v_sc0 = keep.tile([P, J], U8, name="v_sc0", tag="reused", align_bytes=64)
+        nc.scalar.activation(out=zero_bias[:], in_=zero[:], func=SIN)
+        v_sc0 = keep.tile([P, J], U8, name="v_sc0", align_bytes=64)
         nc.vector.tensor_copy(v_sc0[:], tab_sc[:].indirect(idx[:]))
-        for q in range(4):
-            nc.sync.dma_start(
-                out=v_sc1[32 * q : 32 * q + 4, :].bitcast(I32), in_=v_sc0[32 * q + 4 : 32 * q + 8, :].bitcast(I32)
-            )
         v_sc = [v_sc0, v_sc1]
-        nc.sync.dma_start(idx3[:], offs3)
+
+        base_rows = base.rearrange("(p t) c -> t p c", t=PACK)
+        xs_rows = xs.rearrange("(p t) c -> t p c", t=PACK)
+        w1_bf = [keep.tile([P, PASS * PACK], BF16, name="w1_bf%d" % b, align_bytes=64) for b in range(2)]
+        page = [keep.tile([P, T2], F32, name="page%d" % t) for t in range(PACK)]
+        fresh = [keep.tile([P, S], F32, name="fresh%d" % t, tag="fresh%d" % t, align_bytes=64) for t in range(PACK)]
+
+        def load_w1(raw, c0):
+            width = raw.shape[2]
+            nc.sync.dma_start(out=raw[:], in_=w1[:, c0 : c0 + width].rearrange("(p j) r -> p j r", j=PACK))
+            b, q0 = c0 // PASS, c0 % PASS // 16
+            nc.scalar.copy(
+                out=w1_bf[b][:].rearrange("p (t q e j) -> p t q j e", t=4, e=4, j=4)[:, :, q0 : q0 + width // 16, :, :],
+                in_=raw[:].rearrange("p j (q t e) -> p t q j e", t=4, e=4),
+            )
+
+        def place(t):
+            nc.sync.dma_start(out=fresh[t][:], in_=xs_rows[t])
+            nc.vector.tensor_copy(page[t][:].indirect(idx2[:]), fresh[t][:])
+
+        def round_plane(t):
+            for h in range(2):
+                nc.scalar.copy(out=pair_slot(page_pairs[h][:], t), in_=page[t][:, h * BANK : (h + 1) * BANK])
+
+        nc.sync.dma_start(out=page[0][:], in_=base_rows[0])
+        place(0)
+        load_w1(shared.tile([P, PACK, PASS], F32, name="w1_first", offset=0, align_bytes=64), 0)
+        page_pairs = [
+            shared.tile([P, PACK * BANK], BF16, name="page_pairs%d" % h, offset=h * PACK * BANK * 2, align_bytes=64)
+            for h in range(2)
+        ]
+        round_plane(0)
+        nc.sync.dma_start(out=page[1][:], in_=base_rows[1])
+        place(1)
         for b in range(2):
             nc.sync.dma_start(
                 out=gain_rows[PACK * b : PACK * (b + 1), :].rearrange("t (q e) -> t q e", e=4),
                 in_=gain[b * PASS : (b + 1) * PASS].rearrange("(q t e) -> t q e", t=4, e=4),
             )
+        turned = bank_tile("turned", 7)
+        nc.tensor.transpose(turned[:, 0:P], gain_rows[:], identity[:])
+        gains = keep.tile([P, TILES], F32, name="gains")
+        nc.scalar.copy(out=gains[:], in_=turned[:, 0:TILES])
+        round_plane(1)
+        for t in range(2, PACK):
+            nc.sync.dma_start(out=page[t][:], in_=base_rows[t])
+            load_w1(keep.tile([P, PACK, QUARTER], F32, name="w1_raw%d" % t), t * QUARTER)
+            place(t)
+            round_plane(t)
+
+        def load_wo(b):
+            raw = keep.tile([P, PACK, N], F32, name="wo_raw%d" % b)
+            rows = wo[b * PASS : (b + 1) * PASS, :].rearrange("(q t e) n -> t q e n", t=4, e=4)
+            for t in range(PACK):
+                nc.sync.dma_start(out=raw[:, t, :], in_=rows[t])
+            return raw
+
+        def round_wo(b, raw):
+            grouped = keep.tile([P, N * PACK], BF16, name="wo_bf%d" % b, align_bytes=64)
+            for n0 in range(0, N, HALF):
+                nc.scalar.copy(
+                    out=grouped[:, n0 * PACK : (n0 + HALF) * PACK].rearrange("p (c i t) -> p c t i", i=4, t=PACK),
+                    in_=raw[:, :, n0 : n0 + HALF].rearrange("p t (c i) -> p c t i", i=4),
+                )
+            return grouped
+
+        wo_raw0 = load_wo(0)
+        for q in range(4):
+            nc.sync.dma_start(
+                out=v_sc1[32 * q : 32 * q + 4, :].bitcast(I32), in_=v_sc0[32 * q + 4 : 32 * q + 8, :].bitcast(I32)
+            )
+        tab = [keep.tile([P, T], I32, name="tab%d" % a, tag="tab%d" % a, align_bytes=64) for a in range(2)]
+        w2_raw = keep.tile([P, 2, 2 * H], U8, name="w2_raw", align_bytes=64)
+        w3_codes = keep.tile([P, 2, N], I32, name="w3_codes", align_bytes=64)
+        nc.sync.dma_start(out=tab[0][:], in_=tab_words[0].rearrange("p t i -> p (t i)").bitcast(I32))
+        load_scale_rows(w2_sc_raw, w2_scales)
+        nc.sync.dma_start(out=w2_raw[:].bitcast(I32), in_=w2_words.rearrange("a p c -> p a c").bitcast(I32))
+        nc.sync.dma_start(out=tab[1][:], in_=tab_words[1].rearrange("p t i -> p (t i)").bitcast(I32))
+        nc.sync.dma_start(idx3[:], offs3)
+        wo_raw1 = load_wo(1)
         nc.sync.dma_start(out=w3_codes[:], in_=w3_words.rearrange("a p c i -> p a (c i)").bitcast(I32))
-        load_scale_rows(nc.sync, w3_sc, w3_scales)
+        load_scale_rows(w3_sc, w3_scales)
+
+        first_codes = keep.tile([P, PASS], U32, name="first_codes", tag="fresh3", align_bytes=64)
+        scale_planes = [keep.tile([P, PASS], U8, name="scales%d" % u, align_bytes=64) for u in range(3)]
+        w1_q = [(first_codes[:], scale_planes[0][:])]
+        quantize(w1_q[0], w1_bf[0][:])
+        page_q = [mx_tiles("page%d" % h, BANK) for h in range(2)]
+        for h in range(2):
+            grouped = keep.tile([P, PACK * BANK], BF16, name="page_grouped%d" % h, align_bytes=64)
+            weave(nc.vector.tensor_copy, I32, grouped[:], page_pairs[h][:])
+            quantize(page_q[h], grouped[:])
+        wo_bf0 = round_wo(0, wo_raw0)
 
         v_codes = [keep.tile([P, J], U32, name="v_codes%d" % a, align_bytes=64) for a in range(2)]
-        for a in range(2):
-            nc.vector.tensor_copy(v_codes[a][:], tab[a][:].bitcast(U32).indirect(idx[:]))
-
+        nc.vector.tensor_copy(v_codes[0][:], tab[0][:].bitcast(U32).indirect(idx[:]))
         w2_codes = keep.tile([P, 2 * 2 * H], U8, name="w2_codes", align_bytes=64)
         w2_sc = keep.tile([P, 2 * H], U8, name="w2_sc", align_bytes=64)
-        nc.vector.tensor_copy(
-            out=w2_codes[:].bitcast(I32).rearrange("p (g t q e) -> p g t q e", t=4, q=32, e=2),
-            in_=w2_raw[:].rearrange("p a c -> p (a c)").bitcast(I32).rearrange("p (g q t e) -> p g t q e", t=4, q=32, e=2),
-        )
         nc.vector.tensor_copy(
             out=w2_sc[:].bitcast(I32).rearrange("p (g t q) -> p g t q", t=4, q=32),
             in_=w2_sc_raw[:].rearrange("p a c -> p (a c)").bitcast(I32).rearrange("p (g q t) -> p g t q", t=4, q=32),
         )
-        quantize(w1_q[1], w1_bf[1][:])
-        quantize(wo_q[0], wo_bf[0][:])
+        nc.vector.tensor_copy(
+            out=w2_codes[:].bitcast(I32).rearrange("p (g t q e) -> p g t q e", t=4, q=32, e=2),
+            in_=w2_raw[:].rearrange("p a c -> p (a c)").bitcast(I32).rearrange("p (g q t e) -> p g t q e", t=4, q=32, e=2),
+        )
+        nc.vector.tensor_copy(v_codes[1][:], tab[1][:].bitcast(U32).indirect(idx[:]))
+        late_codes = keep.tile([P, 2, PASS], U32, name="late_codes", tag="tab0", align_bytes=64)
+        w1_q.append((late_codes[:, 0, :], scale_planes[1][:]))
+        wo_q = [(late_codes[:, 1, :], scale_planes[2][:])]
 
-        turned = psum.tile([P, P], F32, name="turned", tag="y", bufs=2)
-        nc.tensor.transpose(turned[:], gain_rows[:], identity[:])
-        gains = keep.tile([P, 2, PACK], F32, name="gains")
-        nc.scalar.copy(out=gains[:].rearrange("p b t -> p (b t)"), in_=turned[:, 0 : 2 * PACK])
+        a_rows = {}
 
-        def project_page(i):
+        def project_page(i, h):
             b, t = divmod(i, PACK)
-            rows = arows.tile([P, T2], F32, name="a_rows")
-            for h in range(2):
-                acc = psum.tile([P, BANK], F32, name="acc", tag="acc")
-                nc.tensor.matmul_mx(
-                    out=acc[:],
-                    lhsT=w1_q[b][0][:, t * P : (t + 1) * P].bitcast(FP8X4),
-                    lhsT_scale=w1_q[b][1][:, t * P : (t + 1) * P],
-                    rhs=page_q[h][0].bitcast(FP8X4),
-                    rhs_scale=page_q[h][1],
-                    start=True,
-                    stop=True,
-                )
-                nc.scalar.copy(out=rows[:, h * BANK : (h + 1) * BANK], in_=acc[:])
-            return rows
+            if i not in a_rows:
+                a_rows[i] = arows.tile([P, T2], F32, name="a_rows")
+            acc = bank_tile("a%d_%d" % (i, h), (2 * i + h) % 3)
+            nc.tensor.matmul_mx(
+                out=acc[:],
+                lhsT=w1_q[b][0][:, t * P : (t + 1) * P].bitcast(FP8X4),
+                lhsT_scale=w1_q[b][1][:, t * P : (t + 1) * P],
+                rhs=page_q[h][0].bitcast(FP8X4),
+                rhs_scale=page_q[h][1],
+                start=True,
+                stop=True,
+            )
+            nc.scalar.copy(out=a_rows[i][:, h * BANK : (h + 1) * BANK], in_=acc[:])
 
-        def project_objects(acc, i, j0, j1):
+        def project_objects(i):
+            acc = bank_tile("b%d" % i, 3 + i % 4)
             for a in range(2):
                 col = a * H + i * P
                 nc.tensor.matmul_mx(
-                    out=acc,
+                    out=acc[:],
                     lhsT=w2_codes[:, 2 * col : 2 * (col + P)].bitcast(FP4X4),
                     lhsT_scale=w2_sc[:, col : col + P],
-                    rhs=v_codes[a][:, j0:j1].bitcast(FP8X4),
-                    rhs_scale=v_sc[a][:, j0:j1],
+                    rhs=v_codes[a][:].bitcast(FP8X4),
+                    rhs_scale=v_sc[a][:],
                     start=(a == 0),
                     stop=(a == 1),
                 )
+            if i < FROM_BANK:
+                return acc
+            rows = ring.tile([P, J], F32, name="b_rows")
+            nc.scalar.copy(out=rows[:], in_=acc[:])
+            return rows
 
-        sines = [wide.tile([P, PACK, J], F32, name="sines", tag="wide") for b in range(2)]
-        a_rows = []
+        def gather(i, b_rows, j0, j1):
+            arg = ring.tile([P, j1 - j0], F32, name="arg")
+            window = a_rows[i][:].indirect(idx3[:, j0 // 16 : j1 // 16])
+            if i < FROM_BANK:
+                picked = keep.tile([P, j1 - j0], F32, name="picked%d" % i)
+                nc.vector.tensor_copy(picked[:], window)
+                nc.vector.tensor_tensor(arg[:], b_rows[:, j0:j1], picked[:], ADD)
+            else:
+                nc.vector.tensor_tensor(arg[:], window, b_rows[:, j0:j1], ADD)
+            return arg
 
-        b_rows = {}
+        def sine(arg, width):
+            sines = ring.tile([P, width], F32, name="sines")
+            nc.scalar.activation(out=sines[:], in_=arg[:], func=SIN, bias=zero_bias[:])
+            return sines
 
-        def stage_objects(i):
-            acc = psum_b.tile([P, BANK], F32, name="b_acc", tag="b")
-            project_objects(acc[:], i, 0, J)
-            rows = keep.tile([P, J], F32, name="b_rows%d" % i)
-            copy = nc.vector.tensor_copy if i == 9 else nc.scalar.copy
-            copy(out=rows[:], in_=acc[:])
-            b_rows[i] = rows
+        def weigh(pairs, i, sines):
+            nc.vector.tensor_scalar(pair_slot(pairs[:], i % PACK), sines, gains[:, i : i + 1], None, MULT)
 
-        def gather_then_add(i):
-            acc = psum_b.tile([P, BANK], F32, name="b_acc", tag="b")
-            project_objects(acc[:], i, 0, J)
-            picked = keep.tile([P, J], F32, name="picked%d" % i)
-            arg = args.tile([P, J], F32, name="arg")
-            nc.vector.tensor_copy(picked[:], a_rows[i][:].indirect(idx3[:]))
-            nc.vector.tensor_tensor(arg[:], acc[:], picked[:], ADD)
-            return arg, [i], 0, J
-
-        def gather(tiles, j0, j1):
-            width = j1 - j0
-            arg = args.tile([P, J], F32, name="arg")
-            for u, i in enumerate(tiles):
-                nc.vector.tensor_tensor(
-                    arg[:, u * width : (u + 1) * width],
-                    a_rows[i][:].indirect(idx3[:, j0 // 16 : j1 // 16]),
-                    b_rows[i][:, j0:j1],
-                    ADD,
-                )
-            return arg, tiles, j0, j1
-
-        h_planes = [keep.tile([P, PACK, J], BF16, name="h_planes%d" % b, align_bytes=64) for b in range(2)]
-
-        def sine(arg, tiles, j0, j1):
-            b, t = divmod(tiles[0], PACK)
-            nc.scalar.activation(
-                out=sines[b][:, t : t + len(tiles), j0:j1],
-                in_=arg[:].rearrange("p (u j) -> p u j", j=j1 - j0),
-                func=SIN,
-                bias=zero_bias[:],
-            )
-            for u in range(t, t + len(tiles)):
-                nc.vector.tensor_scalar(
-                    h_planes[b][:, u, j0:j1], sines[b][:, u, j0:j1], gains[:, b, u : u + 1], None, MULT
-                )
-
-        def weigh(b, j0, j1):
-            width = j1 - j0
-            grouped = keep.tile([P, width * PACK], BF16, name="h_bf%d_%d" % (b, j0), align_bytes=64)
-            dst, src = weave_views(grouped[:], h_planes[b][:, :, j0:j1])
-            nc.vector.tensor_copy(out=dst, in_=src)
-            return grouped
-
-        def quantize_h(name, grouped, width):
+        def quantize_h(name, pairs, width, mover):
+            grouped = keep.tile([P, width * PACK], BF16, name=name + "_bf", align_bytes=64)
+            weave(*mover, grouped[:], pairs[:])
             operand = mx_tiles(name, width)
             quantize(operand, grouped[:])
             return operand
@@ -318,7 +277,7 @@ def tile_list_place_context_kernel(
         d_rows = keep.tile([P, N // P, J], F32, name="d_rows")
 
         def modulation(nt):
-            acc = psum.tile([P, BANK], F32, name="d_acc", tag="y", bufs=2)
+            acc = bank_tile("d%d" % nt, (7, 3, 4, 2)[nt])
             for a in range(2):
                 nc.tensor.matmul_mx(
                     out=acc[:],
@@ -331,77 +290,79 @@ def tile_list_place_context_kernel(
                 )
             nc.scalar.copy(out=d_rows[:, nt, :], in_=acc[:])
 
-        half = J // 2
-        sums = []
-        for i in range(PACK):
-            a_rows.append(project_page(i))
-            if i < 2:
-                sums.append(gather_then_add(i))
-            else:
-                stage_objects(i)
-                sums.append(gather([i], 0, J))
-        for i in range(4, 6):
-            a_rows.append(project_page(i))
-            stage_objects(i)
-        for i in range(PACK):
-            sine(*sums[i])
-        low = [gather([i], 0, J) for i in range(4, 6)]
-        h0_bf = weigh(0, 0, J)
-        for i in range(6, 8):
-            a_rows.append(project_page(i))
-            stage_objects(i)
-        h0 = quantize_h("h0", h0_bf, J)
-        high_first = gather([6, 7], 0, half)
-        high_last = gather([6, 7], half, J)
-        sine(*low[0])
-        sine(*low[1])
-        wo_bf.append(round_wo(1))
-        quantize(wo_q[1], wo_bf[1][:])
-        modulation(0)
-        sine(*high_first)
-        modulation(1)
-        sine(*high_last)
-        modulation(2)
-        modulation(3)
+        h0_pairs = keep.tile([P, PACK * J], BF16, name="h0_pairs", align_bytes=64)
+        h1_pairs = [keep.tile([P, PACK * HALF], BF16, name="h1_pairs%d" % u, align_bytes=64) for u in range(2)]
 
-        def y_pass(acc, nt, b, operand, cols):
-            nc.tensor.matmul_mx(
-                out=acc,
-                lhsT=wo_q[b][0][:, nt * P : (nt + 1) * P].bitcast(FP8X4),
-                lhsT_scale=wo_q[b][1][:, nt * P : (nt + 1) * P],
-                rhs=operand[0][:, cols].bitcast(FP8X4),
-                rhs_scale=operand[1][:, cols],
-                start=(b == 0),
-                stop=(b == 1),
-            )
+        def finish_tile(i, arg):
+            sines = sine(arg, J)
+            if i < PACK:
+                weigh(h0_pairs, i, sines[:])
+            else:
+                for u in range(2):
+                    weigh(h1_pairs[u], i, sines[:, u * HALF : (u + 1) * HALF])
+
+        quantize(w1_q[1], w1_bf[1][:])
+        quantize(wo_q[0], wo_bf0[:])
+        for i in range(AHEAD):
+            for h in range(2):
+                project_page(i, h)
+        whole = TILES - 2
+        later_halves = [(i, h) for i in range(AHEAD, TILES) for h in range(2)]
+        b_rows = {0: project_objects(0)}
+        args = {}
+        for i in range(TILES - 1):
+            b_rows[i + 1] = project_objects(i + 1)
+            if i < whole:
+                args[i] = gather(i, b_rows[i], 0, J)
+            if i >= 1:
+                finish_tile(i - 1, args[i - 1])
+            else:
+                project_page(*later_halves[0])
+            project_page(*later_halves[i + 1])
+            if i == PACK:
+                h0 = quantize_h("h0", h0_pairs, J, (nc.vector.tensor_copy, I32))
+        last_tiles = range(whole, TILES)
+        half_args = [[gather(i, b_rows[i], u * HALF, (u + 1) * HALF) for i in last_tiles] for u in range(2)]
+        wo_bf1 = round_wo(1, wo_raw1)
+        wo_q.append(mx_tiles("wo1", N))
+        quantize(wo_q[1], wo_bf1[:])
 
         out_rows = out.rearrange("(nt p) j -> p nt j", p=P)
-        first, last = slice(0, half), slice(half, J)
 
-        h1a_bf = weigh(1, 0, half)
-        h1a = quantize_h("h1a", h1a_bf, half)
-        h1b_bf = weigh(1, half, J)
-
-        y_last = [psum.tile([P, half], F32, name="y_last", tag="acc") for nt in range(2)]
-        y_last.extend([psum_b.tile([P, half], F32, name="y_last", tag="b") for nt in range(2)])
-        for nt in range(N // P):
-            y_pass(y_last[nt][:], nt, 0, h0, last)
-
-        result = keep.tile([P, N // P, half], F32, name="result_first")
-        for pair in range(2):
-            acc = psum.tile([P, 2, half], F32, name="y_first", tag="y", bufs=2)
+        def y_passes(acc, pair, b, operand, cols):
             for u in range(2):
-                y_pass(acc[:, u, :], 2 * pair + u, 0, h0, first)
-                y_pass(acc[:, u, :], 2 * pair + u, 1, h1a, first)
-            rows = slice(2 * pair, 2 * pair + 2)
-            nc.vector.tensor_tensor(result[:, rows, :], acc[:], d_rows[:, rows, first], MULT)
-            nc.sync.dma_start(out=out_rows[:, rows, first], in_=result[:, rows, :])
+                nt = 2 * pair + u
+                nc.tensor.matmul_mx(
+                    out=acc[:, u * HALF : (u + 1) * HALF],
+                    lhsT=wo_q[b][0][:, nt * P : (nt + 1) * P].bitcast(FP8X4),
+                    lhsT_scale=wo_q[b][1][:, nt * P : (nt + 1) * P],
+                    rhs=operand[0][:, cols].bitcast(FP8X4),
+                    rhs_scale=operand[1][:, cols],
+                    start=(b == 0 and u == 0),
+                    stop=(b == 1 and u == 1),
+                )
 
-        h1b = quantize_h("h1b", h1b_bf, half)
+        y_acc = [[bank_tile("y%d_%d" % (u, pair), (0, 5)[u] + pair) for pair in range(2)] for u in range(2)]
+        h1 = []
+        for u in range(2):
+            for i, arg in zip(last_tiles, half_args[u]):
+                weigh(h1_pairs[u], i, sine(arg, HALF)[:])
+            h1.append(quantize_h("h1_%d" % u, h1_pairs[u], HALF, (nc.vector.tensor_copy, I32)))
         for nt in range(N // P):
-            y_pass(y_last[nt][:], nt, 1, h1b, first)
-        for nt in range(N // P):
-            result = keep.tile([P, half], F32, name="result_last%d" % nt)
-            nc.vector.tensor_tensor(result[:], y_last[nt][:], d_rows[:, nt, last], MULT)
-            queue = nc.sync if nt % 2 == 0 else nc.scalar
-            queue.dma_start(out=out_rows[:, nt, last], in_=result[:])
+            modulation(nt)
+        for u in range(2):
+            for pair in range(2):
+                y_passes(y_acc[u][pair], pair, 0, h0, slice(u * HALF, (u + 1) * HALF))
+        for u in range(2):
+            cols = slice(u * HALF, (u + 1) * HALF)
+            for pair in range(2):
+                y_passes(y_acc[u][pair], pair, 1, h1[u], slice(0, HALF))
+            for pair in range(2):
+                step = 2 - u
+                for k in range(0, 2, step):
+                    rows = slice(2 * pair + k, 2 * pair + k + step)
+                    result = keep.tile([P, step, HALF], F32, name="result%d_%d" % (u, rows.start))
+                    acc = y_acc[u][pair][:].rearrange("p (u j) -> p u j", u=2)[:, k : k + step, :]
+                    nc.vector.tensor_tensor(result[:], acc, d_rows[:, rows, cols], MULT)
+                    queue = nc.sync if (pair + k) % 2 == 0 else nc.scalar
+                    queue.dma_start(out=out_rows[:, rows, cols], in_=result[:])

@@ -26,8 +26,8 @@ BANK_BYTES = 4 * BANK
 TILES = H // P
 HALF = J // 2
 QUARTER = H // 4
-FROM_BANK = 1
-AHEAD = 4
+FROM_BANK = 2
+AHEAD = 5
 
 
 def tile_list_place_context_kernel(
@@ -59,8 +59,8 @@ def tile_list_place_context_kernel(
 
         def weave(copy, word, grouped, pairs):
             copy(
-                out=grouped.bitcast(word).rearrange("p (c s) -> p c s", s=2),
-                in_=pairs.bitcast(word).rearrange("p (s c) -> p c s", s=2),
+                out=grouped.bitcast(word).rearrange("p (c i s) -> p c s i", i=4, s=2),
+                in_=pairs.bitcast(word).rearrange("p (s c i) -> p c s i", i=4, s=2),
             )
 
         idx = lists.tile([P, J // 16], U16, name="idx")
@@ -151,20 +151,18 @@ def tile_list_place_context_kernel(
             round_plane(t)
 
         def load_wo(b):
-            raw = keep.tile([P, PACK, N], F32, name="wo_raw%d" % b)
+            raw = keep.tile([P, PACK, N], F32, name="wo_raw%d" % b, tag="wo_raw%d" % b)
             rows = wo[b * PASS : (b + 1) * PASS, :].rearrange("(q t e) n -> t q e n", t=4, e=4)
             for t in range(PACK):
                 nc.sync.dma_start(out=raw[:, t, :], in_=rows[t])
             return raw
 
-        def round_wo(b, raw):
-            grouped = keep.tile([P, N * PACK], BF16, name="wo_bf%d" % b, align_bytes=64)
-            for n0 in range(0, N, HALF):
-                nc.scalar.copy(
-                    out=grouped[:, n0 * PACK : (n0 + HALF) * PACK].rearrange("p (c i t) -> p c t i", i=4, t=PACK),
-                    in_=raw[:, :, n0 : n0 + HALF].rearrange("p t (c i) -> p c t i", i=4),
-                )
-            return grouped
+        def round_wo(grouped, raw, u):
+            cols = slice(u * HALF, (u + 1) * HALF)
+            nc.scalar.copy(
+                out=grouped[:].rearrange("p (c i t) -> p c t i", i=4, t=PACK)[:, u * HALF // 4 : (u + 1) * HALF // 4],
+                in_=raw[:, :, cols].rearrange("p t (c i) -> p c t i", i=4),
+            )
 
         wo_raw0 = load_wo(0)
         for q in range(4):
@@ -183,16 +181,19 @@ def tile_list_place_context_kernel(
         nc.sync.dma_start(out=w3_codes[:], in_=w3_words.rearrange("a p c i -> p a (c i)").bitcast(I32))
         load_scale_rows(w3_sc, w3_scales)
 
-        first_codes = keep.tile([P, PASS], U32, name="first_codes", tag="fresh3", align_bytes=64)
+        w1_codes = keep.tile([P, 2, PASS], U32, name="w1_codes", tag="fresh3", align_bytes=64)
         scale_planes = [keep.tile([P, PASS], U8, name="scales%d" % u, align_bytes=64) for u in range(3)]
-        w1_q = [(first_codes[:], scale_planes[0][:])]
-        quantize(w1_q[0], w1_bf[0][:])
+        w1_q = [(w1_codes[:, b, :], scale_planes[b][:]) for b in range(2)]
+        for b in range(2):
+            quantize(w1_q[b], w1_bf[b][:])
         page_q = [mx_tiles("page%d" % h, BANK) for h in range(2)]
         for h in range(2):
             grouped = keep.tile([P, PACK * BANK], BF16, name="page_grouped%d" % h, align_bytes=64)
             weave(nc.vector.tensor_copy, I32, grouped[:], page_pairs[h][:])
             quantize(page_q[h], grouped[:])
-        wo_bf0 = round_wo(0, wo_raw0)
+        wo_bf0 = keep.tile([P, N * PACK], BF16, name="wo_bf0", align_bytes=64)
+        for u in range(2):
+            round_wo(wo_bf0, wo_raw0, u)
 
         v_codes = [keep.tile([P, J], U32, name="v_codes%d" % a, align_bytes=64) for a in range(2)]
         nc.vector.tensor_copy(v_codes[0][:], tab[0][:].bitcast(U32).indirect(idx[:]))
@@ -207,9 +208,8 @@ def tile_list_place_context_kernel(
             in_=w2_raw[:].rearrange("p a c -> p (a c)").bitcast(I32).rearrange("p (g q t e) -> p g t q e", t=4, q=32, e=2),
         )
         nc.vector.tensor_copy(v_codes[1][:], tab[1][:].bitcast(U32).indirect(idx[:]))
-        late_codes = keep.tile([P, 2, PASS], U32, name="late_codes", tag="tab0", align_bytes=64)
-        w1_q.append((late_codes[:, 0, :], scale_planes[1][:]))
-        wo_q = [(late_codes[:, 1, :], scale_planes[2][:])]
+        wo_codes = keep.tile([P, PASS], U32, name="wo_codes", tag="tab0", align_bytes=64)
+        wo_q = [(wo_codes[:], scale_planes[2][:])]
 
         a_rows = {}
 
@@ -217,7 +217,7 @@ def tile_list_place_context_kernel(
             b, t = divmod(i, PACK)
             if i not in a_rows:
                 a_rows[i] = arows.tile([P, T2], F32, name="a_rows")
-            acc = bank_tile("a%d_%d" % (i, h), (2 * i + h) % 3)
+            acc = bank_tile("a%d_%d" % (i, h), (2 * i + h) % 3 if i < AHEAD else 3 + (2 * (i - AHEAD + 1) + h) % 4)
             nc.tensor.matmul_mx(
                 out=acc[:],
                 lhsT=w1_q[b][0][:, t * P : (t + 1) * P].bitcast(FP8X4),
@@ -248,84 +248,105 @@ def tile_list_place_context_kernel(
             nc.scalar.copy(out=rows[:], in_=acc[:])
             return rows
 
-        def gather(i, b_rows, j0, j1):
-            arg = ring.tile([P, j1 - j0], F32, name="arg")
+        def gather(arg, i, b_rows, j0, j1):
             window = a_rows[i][:].indirect(idx3[:, j0 // 16 : j1 // 16])
             if i < FROM_BANK:
                 picked = keep.tile([P, j1 - j0], F32, name="picked%d" % i)
                 nc.vector.tensor_copy(picked[:], window)
-                nc.vector.tensor_tensor(arg[:], b_rows[:, j0:j1], picked[:], ADD)
+                nc.vector.tensor_tensor(arg, b_rows[:, j0:j1], picked[:], ADD)
             else:
-                nc.vector.tensor_tensor(arg[:], window, b_rows[:, j0:j1], ADD)
-            return arg
+                nc.vector.tensor_tensor(arg, window, b_rows[:, j0:j1], ADD)
 
-        def sine(arg, width):
-            sines = ring.tile([P, width], F32, name="sines")
-            nc.scalar.activation(out=sines[:], in_=arg[:], func=SIN, bias=zero_bias[:])
-            return sines
+        sines = [keep.tile([P, PACK, J], F32, name="sines%d" % b, tag="sines%d" % b, align_bytes=64) for b in range(2)]
 
-        def weigh(pairs, i, sines):
-            nc.vector.tensor_scalar(pair_slot(pairs[:], i % PACK), sines, gains[:, i : i + 1], None, MULT)
+        def sine(arg, i, count, j0, j1):
+            b, t = divmod(i, PACK)
+            nc.scalar.activation(
+                out=sines[b][:, t : t + count, j0:j1],
+                in_=arg.rearrange("p (u j) -> p u j", u=count),
+                func=SIN,
+                bias=zero_bias[:],
+            )
 
-        def quantize_h(name, pairs, width, mover):
-            grouped = keep.tile([P, width * PACK], BF16, name=name + "_bf", align_bytes=64)
-            weave(*mover, grouped[:], pairs[:])
+        def weigh(b, j0, j1):
+            width = j1 - j0
+            grouped = keep.tile([P, width * PACK], BF16, name="h_bf%d_%d" % (b, j0), align_bytes=64)
+            nc.vector.tensor_tensor(
+                grouped[:].rearrange("p (c i t) -> p c t i", i=4, t=PACK),
+                sines[b][:, :, j0:j1].rearrange("p t (c i) -> p c t i", i=4),
+                gains[:, PACK * b : PACK * (b + 1)].unsqueeze(1).unsqueeze(3).to_broadcast([P, width // 4, PACK, 4]),
+                MULT,
+            )
+            return grouped
+
+        def quantize_h(name, grouped, width):
             operand = mx_tiles(name, width)
             quantize(operand, grouped[:])
             return operand
 
-        d_rows = keep.tile([P, N // P, J], F32, name="d_rows")
+        d_rows = keep.tile([P, 2, N // P, HALF], F32, name="d_rows", tag="wo_raw1")
 
-        def modulation(nt):
-            acc = bank_tile("d%d" % nt, (7, 3, 4, 2)[nt])
-            for a in range(2):
-                nc.tensor.matmul_mx(
-                    out=acc[:],
-                    lhsT=w3_codes[:, a, nt * P : (nt + 1) * P].bitcast(FP8X4),
-                    lhsT_scale=w3_sc[:, a, nt * P : (nt + 1) * P],
-                    rhs=v_codes[a][:].bitcast(FP8X4),
-                    rhs_scale=v_sc[a][:],
-                    start=(a == 0),
-                    stop=(a == 1),
-                )
-            nc.scalar.copy(out=d_rows[:, nt, :], in_=acc[:])
+        def modulation(u, pair):
+            acc = bank_tile("d%d_%d" % (u, pair), (7, 2, 3, 4)[2 * pair + u])
+            cols = slice(u * HALF, (u + 1) * HALF)
+            for k in range(2):
+                nt = 2 * pair + k
+                for a in range(2):
+                    nc.tensor.matmul_mx(
+                        out=acc[:, k * HALF : (k + 1) * HALF],
+                        lhsT=w3_codes[:, a, nt * P : (nt + 1) * P].bitcast(FP8X4),
+                        lhsT_scale=w3_sc[:, a, nt * P : (nt + 1) * P],
+                        rhs=v_codes[a][:, cols].bitcast(FP8X4),
+                        rhs_scale=v_sc[a][:, cols],
+                        start=(a == 0),
+                        stop=(a == 1),
+                    )
+            nc.scalar.copy(
+                out=d_rows[:, u, 2 * pair : 2 * pair + 2, :], in_=acc[:].rearrange("p (k j) -> p k j", k=2)
+            )
 
-        h0_pairs = keep.tile([P, PACK * J], BF16, name="h0_pairs", align_bytes=64)
-        h1_pairs = [keep.tile([P, PACK * HALF], BF16, name="h1_pairs%d" % u, align_bytes=64) for u in range(2)]
-
-        def finish_tile(i, arg):
-            sines = sine(arg, J)
-            if i < PACK:
-                weigh(h0_pairs, i, sines[:])
-            else:
-                for u in range(2):
-                    weigh(h1_pairs[u], i, sines[:, u * HALF : (u + 1) * HALF])
-
-        quantize(w1_q[1], w1_bf[1][:])
         quantize(wo_q[0], wo_bf0[:])
         for i in range(AHEAD):
             for h in range(2):
                 project_page(i, h)
         whole = TILES - 2
-        later_halves = [(i, h) for i in range(AHEAD, TILES) for h in range(2)]
-        b_rows = {0: project_objects(0)}
-        args = {}
-        for i in range(TILES - 1):
-            b_rows[i + 1] = project_objects(i + 1)
-            if i < whole:
-                args[i] = gather(i, b_rows[i], 0, J)
-            if i >= 1:
-                finish_tile(i - 1, args[i - 1])
-            else:
-                project_page(*later_halves[0])
-            project_page(*later_halves[i + 1])
-            if i == PACK:
-                h0 = quantize_h("h0", h0_pairs, J, (nc.vector.tensor_copy, I32))
-        last_tiles = range(whole, TILES)
-        half_args = [[gather(i, b_rows[i], u * HALF, (u + 1) * HALF) for i in last_tiles] for u in range(2)]
-        wo_bf1 = round_wo(1, wo_raw1)
+        b_rows = {}
+        args = [ring.tile([P, 2 * J], F32, name="arg") for pair in range(whole // 2)]
+        for i in range(whole):
+            if i >= AHEAD:
+                for h in range(2):
+                    project_page(i, h)
+            b_rows[i] = project_objects(i)
+            gather(args[i // 2][:, i % 2 * J : (i % 2 + 1) * J], i, b_rows[i], 0, J)
+        for pair in range(2):
+            sine(args[pair][:], 2 * pair, 2, 0, J)
+        h0_bf = weigh(0, 0, J)
+        for h in range(2):
+            project_page(whole, h)
+        for i in range(whole, TILES):
+            b_rows[i] = project_objects(i)
+        for h in range(2):
+            project_page(whole + 1, h)
+        sine(args[2][:], PACK, 2, 0, J)
+        h0 = quantize_h("h0", h0_bf, J)
+        half_args = []
+        for u in range(2):
+            half_args.append(ring.tile([P, J], F32, name="half_arg"))
+            for i in range(whole, TILES):
+                cols = slice((i - whole) * HALF, (i - whole + 1) * HALF)
+                gather(half_args[u][:, cols], i, b_rows[i], u * HALF, (u + 1) * HALF)
+        wo_bf1 = keep.tile([P, N * PACK], BF16, name="wo_bf1", tag="sines0", align_bytes=64)
+        h1_bf = []
         wo_q.append(mx_tiles("wo1", N))
-        quantize(wo_q[1], wo_bf1[:])
+        for u in range(2):
+            sine(half_args[u][:], whole, 2, u * HALF, (u + 1) * HALF)
+            h1_bf.append(weigh(1, u * HALF, (u + 1) * HALF))
+            round_wo(wo_bf1, wo_raw1, u)
+        h1 = []
+        for u in range(2):
+            h1.append(quantize_h("h1_%d" % u, h1_bf[u], HALF))
+            cols = slice(u * HALF, (u + 1) * HALF)
+            quantize((wo_q[1][0][:, cols], wo_q[1][1][:, cols]), wo_bf1[:, u * HALF * PACK : (u + 1) * HALF * PACK])
 
         out_rows = out.rearrange("(nt p) j -> p nt j", p=P)
 
@@ -342,27 +363,23 @@ def tile_list_place_context_kernel(
                     stop=(b == 1 and u == 1),
                 )
 
-        y_acc = [[bank_tile("y%d_%d" % (u, pair), (0, 5)[u] + pair) for pair in range(2)] for u in range(2)]
-        h1 = []
-        for u in range(2):
-            for i, arg in zip(last_tiles, half_args[u]):
-                weigh(h1_pairs[u], i, sine(arg, HALF)[:])
-            h1.append(quantize_h("h1_%d" % u, h1_pairs[u], HALF, (nc.vector.tensor_copy, I32)))
-        for nt in range(N // P):
-            modulation(nt)
+        y_acc = [[bank_tile("y%d_%d" % (u, pair), (5, 0)[u] + pair) for pair in range(2)] for u in range(2)]
+        for pair in range(2):
+            for u in range(2):
+                modulation(u, pair)
         for u in range(2):
             for pair in range(2):
                 y_passes(y_acc[u][pair], pair, 0, h0, slice(u * HALF, (u + 1) * HALF))
-        for u in range(2):
-            cols = slice(u * HALF, (u + 1) * HALF)
-            for pair in range(2):
+        for pair in range(2):
+            for u in range(2):
                 y_passes(y_acc[u][pair], pair, 1, h1[u], slice(0, HALF))
-            for pair in range(2):
-                step = 2 - u
+            for u in range(2):
+                cols = slice(u * HALF, (u + 1) * HALF)
+                step = 1 if pair == 1 and u == 1 else 2
                 for k in range(0, 2, step):
                     rows = slice(2 * pair + k, 2 * pair + k + step)
                     result = keep.tile([P, step, HALF], F32, name="result%d_%d" % (u, rows.start))
                     acc = y_acc[u][pair][:].rearrange("p (u j) -> p u j", u=2)[:, k : k + step, :]
-                    nc.vector.tensor_tensor(result[:], acc, d_rows[:, rows, cols], MULT)
-                    queue = nc.sync if (pair + k) % 2 == 0 else nc.scalar
+                    nc.vector.tensor_tensor(result[:], acc, d_rows[:, u, rows, :], MULT)
+                    queue = nc.sync if (u + k) % 2 == 0 else nc.scalar
                     queue.dma_start(out=out_rows[:, rows, cols], in_=result[:])

@@ -70,36 +70,34 @@ def tile_list_place_context_kernel(
         tab_sc = keep.tile([P, T], U8, name="tab_sc", align_bytes=64)
         w2_sc_raw = keep.tile([P, 2, H], U8, name="w2_sc_raw", align_bytes=64)
         w3_sc = keep.tile([P, 2, N], U8, name="w3_sc", align_bytes=64)
-        v_sc1 = keep.tile([P, J], U8, name="v_sc1", align_bytes=64)
+        v_sc = [keep.tile([P, J], U8, name="v_sc%d" % a, align_bytes=64) for a in range(2)]
         zero = keep.tile([P, 1], F32, name="zero")
         zero_bias = keep.tile([P, 1], F32, name="zero_bias")
         gain_rows = keep.tile([P, P], F32, name="gain_rows")
         identity = keep.tile([P, P], F32, name="identity")
         nc.gpsimd.memset(tab_sc[:].bitcast(I32), 0)
         nc.vector.memset(zero[:], 0.0)
-        nc.vector.memset(v_sc1[:].bitcast(I32), 0)
+        for a in range(2):
+            nc.vector.memset(v_sc[a][:].bitcast(I32), 0)
         nc.vector.memset(w2_sc_raw[:].rearrange("p a c -> p (a c)").bitcast(I32), 0)
         nc.vector.memset(w3_sc[:].rearrange("p a c -> p (a c)").bitcast(I32), 0)
         nc.vector.memset(gain_rows[:], 0.0)
         make_identity(nc, identity[:])
 
-        def load_scale_rows(tile, dram):
-            for q in range(4):
-                nc.sync.dma_start(
-                    out=tile[32 * q : 32 * q + 4, :, :].bitcast(I32),
-                    in_=dram[:, 4 * q : 4 * q + 4, :].rearrange("a r c -> r a c").bitcast(I32),
-                )
-
-        nc.sync.dma_start(idx[:], offs)
-        nc.sync.dma_start(idx2[:], offs2)
-        for q in range(4):
-            nc.scalar.dma_start(
-                out=tab_sc[32 * q : 32 * q + 8, :].bitcast(I32), in_=tab_scales[:, 4 * q : 4 * q + 4, :].bitcast(I32)
+        def load_scale_rows(tile, dram, q):
+            nc.sync.dma_start(
+                out=tile[32 * q : 32 * q + 4, :, :].bitcast(I32),
+                in_=dram[:, 4 * q : 4 * q + 4, :].rearrange("a r c -> r a c").bitcast(I32),
             )
+
+        nc.sync.dma_start(
+            out=tab_sc[0:P:4, :].bitcast(I32), in_=tab_scales.rearrange("a g t -> (a g) t").bitcast(I32)
+        )
+        nc.sync.dma_start(idx[:], offs)
+        picked_sc = keep.tile([P, J], U8, name="picked_sc", align_bytes=64)
+        nc.vector.tensor_copy(picked_sc[:], tab_sc[:].indirect(idx[:]))
+        nc.sync.dma_start(idx2[:], offs2)
         nc.scalar.activation(out=zero_bias[:], in_=zero[:], func=SIN)
-        v_sc0 = keep.tile([P, J], U8, name="v_sc0", align_bytes=64)
-        nc.vector.tensor_copy(v_sc0[:], tab_sc[:].indirect(idx[:]))
-        v_sc = [v_sc0, v_sc1]
 
         base_rows = base.rearrange("(p t) c -> t p c", t=PACK)
         xs_rows = xs.rearrange("(p t) c -> t p c", t=PACK)
@@ -107,18 +105,27 @@ def tile_list_place_context_kernel(
         page = [keep.tile([P, T2], F32, name="page%d" % t) for t in range(PACK)]
         fresh = [keep.tile([P, S], F32, name="fresh%d" % t, tag="fresh%d" % t, align_bytes=64) for t in range(PACK)]
 
-        def load_w1(raw, c0):
-            width = raw.shape[2]
-            nc.sync.dma_start(out=raw[:], in_=w1[:, c0 : c0 + width].rearrange("(p j) r -> p j r", j=PACK))
-            b, q0 = c0 // PASS, c0 % PASS // 16
-            nc.scalar.copy(
-                out=w1_bf[b][:].rearrange("p (t q e j) -> p t q j e", t=4, e=4, j=4)[:, :, q0 : q0 + width // 16, :, :],
-                in_=raw[:].rearrange("p j (q t e) -> p t q j e", t=4, e=4),
+        def load_w1(raw, u):
+            nc.sync.dma_start(
+                out=raw[:], in_=w1[:, u * QUARTER : (u + 1) * QUARTER].rearrange("(p j) r -> p j r", j=PACK)
             )
+            dealt = w1_bf[u // 2][:].rearrange("p (t q e j) -> p t q j e", t=4, e=4, j=4)[:, :, 16 * (u % 2) : 16 * (u % 2 + 1)]
+            rows = raw[:].rearrange("p j (q t e) -> p t q j e", t=4, e=4)
+            if u < PACK - 1:
+                nc.scalar.copy(out=dealt, in_=rows)
+            else:
+                for t in range(PACK):
+                    nc.gpsimd.tensor_scalar(dealt[:, t], rows[:, t], 1.0, 0.0, MULT, ADD)
 
         def place(t):
             nc.sync.dma_start(out=fresh[t][:], in_=xs_rows[t])
             nc.vector.tensor_copy(page[t][:].indirect(idx2[:]), fresh[t][:])
+
+        def move_scale_rows(a, q):
+            first = 4 * (16 * a + 4 * q)
+            nc.sync.dma_start(
+                out=v_sc[a][32 * q : 32 * q + 4, :].bitcast(I32), in_=picked_sc[first : first + 16 : 4, :].bitcast(I32)
+            )
 
         def round_plane(t):
             for h in range(2):
@@ -126,7 +133,7 @@ def tile_list_place_context_kernel(
 
         nc.sync.dma_start(out=page[0][:], in_=base_rows[0])
         place(0)
-        load_w1(shared.tile([P, PACK, PASS], F32, name="w1_first", offset=0, align_bytes=64), 0)
+        load_w1(shared.tile([P, PACK, QUARTER], F32, name="w1_first", offset=2048, align_bytes=64), 0)
         page_pairs = [
             shared.tile([P, PACK * BANK], BF16, name="page_pairs%d" % h, offset=h * PACK * BANK * 2, align_bytes=64)
             for h in range(2)
@@ -134,21 +141,13 @@ def tile_list_place_context_kernel(
         round_plane(0)
         nc.sync.dma_start(out=page[1][:], in_=base_rows[1])
         place(1)
-        for b in range(2):
-            nc.sync.dma_start(
-                out=gain_rows[PACK * b : PACK * (b + 1), :].rearrange("t (q e) -> t q e", e=4),
-                in_=gain[b * PASS : (b + 1) * PASS].rearrange("(q t e) -> t q e", t=4, e=4),
-            )
-        turned = bank_tile("turned", 7)
-        nc.tensor.transpose(turned[:, 0:P], gain_rows[:], identity[:])
-        gains = keep.tile([P, TILES], F32, name="gains")
-        nc.scalar.copy(out=gains[:], in_=turned[:, 0:TILES])
         round_plane(1)
         for t in range(2, PACK):
             nc.sync.dma_start(out=page[t][:], in_=base_rows[t])
-            load_w1(keep.tile([P, PACK, QUARTER], F32, name="w1_raw%d" % t), t * QUARTER)
+            load_w1(keep.tile([P, PACK, QUARTER], F32, name="w1_raw%d" % t), t - 1)
             place(t)
             round_plane(t)
+        load_w1(shared.tile([P, PACK, QUARTER], F32, name="w1_last", offset=10240, align_bytes=64), PACK - 1)
 
         def load_wo(b):
             raw = keep.tile([P, PACK, N], F32, name="wo_raw%d" % b, tag="wo_raw%d" % b)
@@ -164,22 +163,32 @@ def tile_list_place_context_kernel(
                 in_=raw[:, :, cols].rearrange("p t (c i) -> p c t i", i=4),
             )
 
-        wo_raw0 = load_wo(0)
-        for q in range(4):
+        for b in range(2):
             nc.sync.dma_start(
-                out=v_sc1[32 * q : 32 * q + 4, :].bitcast(I32), in_=v_sc0[32 * q + 4 : 32 * q + 8, :].bitcast(I32)
+                out=gain_rows[PACK * b : PACK * (b + 1), :].rearrange("t (q e) -> t q e", e=4),
+                in_=gain[b * PASS : (b + 1) * PASS].rearrange("(q t e) -> t q e", t=4, e=4),
             )
+        turned = bank_tile("turned", 7)
+        nc.tensor.transpose(turned[:, 0:P], gain_rows[:], identity[:])
+        gains = keep.tile([P, TILES], F32, name="gains")
+        nc.scalar.copy(out=gains[:], in_=turned[:, 0:TILES])
+        wo_raw0 = load_wo(0)
         tab = [keep.tile([P, T], I32, name="tab%d" % a, tag="tab%d" % a, align_bytes=64) for a in range(2)]
         w2_raw = keep.tile([P, 2, 2 * H], U8, name="w2_raw", align_bytes=64)
         w3_codes = keep.tile([P, 2, N], I32, name="w3_codes", align_bytes=64)
         nc.sync.dma_start(out=tab[0][:], in_=tab_words[0].rearrange("p t i -> p (t i)").bitcast(I32))
-        load_scale_rows(w2_sc_raw, w2_scales)
         nc.sync.dma_start(out=w2_raw[:].bitcast(I32), in_=w2_words.rearrange("a p c -> p a c").bitcast(I32))
         nc.sync.dma_start(out=tab[1][:], in_=tab_words[1].rearrange("p t i -> p (t i)").bitcast(I32))
+        for q in range(4):
+            load_scale_rows(w2_sc_raw, w2_scales, q)
         nc.sync.dma_start(idx3[:], offs3)
+        for a in range(2):
+            for q in range(4):
+                move_scale_rows(a, q)
         wo_raw1 = load_wo(1)
         nc.sync.dma_start(out=w3_codes[:], in_=w3_words.rearrange("a p c i -> p a (c i)").bitcast(I32))
-        load_scale_rows(w3_sc, w3_scales)
+        for q in range(4):
+            load_scale_rows(w3_sc, w3_scales, q)
 
         w1_codes = keep.tile([P, 2, PASS], U32, name="w1_codes", tag="fresh3", align_bytes=64)
         scale_planes = [keep.tile([P, PASS], U8, name="scales%d" % u, align_bytes=64) for u in range(3)]
@@ -188,7 +197,9 @@ def tile_list_place_context_kernel(
             quantize(w1_q[b], w1_bf[b][:])
         page_q = [mx_tiles("page%d" % h, BANK) for h in range(2)]
         for h in range(2):
-            grouped = keep.tile([P, PACK * BANK], BF16, name="page_grouped%d" % h, align_bytes=64)
+            grouped = shared.tile(
+                [P, PACK * BANK], BF16, name="page_grouped%d" % h, offset=(2 + h) * PACK * BANK * 2, align_bytes=64
+            )
             weave(nc.vector.tensor_copy, I32, grouped[:], page_pairs[h][:])
             quantize(page_q[h], grouped[:])
         wo_bf0 = keep.tile([P, N * PACK], BF16, name="wo_bf0", align_bytes=64)
@@ -375,11 +386,12 @@ def tile_list_place_context_kernel(
                 y_passes(y_acc[u][pair], pair, 1, h1[u], slice(0, HALF))
             for u in range(2):
                 cols = slice(u * HALF, (u + 1) * HALF)
-                step = 1 if pair == 1 and u == 1 else 2
-                for k in range(0, 2, step):
-                    rows = slice(2 * pair + k, 2 * pair + k + step)
-                    result = keep.tile([P, step, HALF], F32, name="result%d_%d" % (u, rows.start))
-                    acc = y_acc[u][pair][:].rearrange("p (u j) -> p u j", u=2)[:, k : k + step, :]
-                    nc.vector.tensor_tensor(result[:], acc, d_rows[:, u, rows, :], MULT)
-                    queue = nc.sync if (u + k) % 2 == 0 else nc.scalar
-                    queue.dma_start(out=out_rows[:, rows, cols], in_=result[:])
+                rows = slice(2 * pair, 2 * pair + 2)
+                result = keep.tile([P, 2, HALF], F32, name="result%d_%d" % (u, pair))
+                acc = y_acc[u][pair][:].rearrange("p (k j) -> p k j", k=2)
+                nc.vector.tensor_tensor(result[:], acc, d_rows[:, u, rows, :], MULT)
+                if pair == 1 and u == 1:
+                    for k, queue in enumerate((nc.scalar, nc.sync)):
+                        queue.dma_start(out=out_rows[:, 2 * pair + k, cols], in_=result[:, k, :])
+                else:
+                    nc.sync.dma_start(out=out_rows[:, rows, cols], in_=result[:])

@@ -109,11 +109,15 @@ def tile_list_place_context_kernel(
             nc.sync.dma_start(
                 out=raw[:], in_=w1[:, u * QUARTER : (u + 1) * QUARTER].rearrange("(p j) r -> p j r", j=PACK)
             )
-            dealt = w1_bf[u // 2][:].rearrange("p (t q e j) -> p t q j e", t=4, e=4, j=4)[:, :, 16 * (u % 2) : 16 * (u % 2 + 1)]
-            rows = raw[:].rearrange("p j (q t e) -> p t q j e", t=4, e=4)
-            if u < PACK - 1:
-                nc.scalar.copy(out=dealt, in_=rows)
+            runs = slice(16 * (u % 2), 16 * (u % 2 + 1))
+            if u < 1:
+                nc.scalar.copy(
+                    out=w1_bf[u // 2][:].rearrange("p (t q e j) -> p t q j e", t=4, e=4, j=4)[:, :, runs],
+                    in_=raw[:].rearrange("p j (q t e) -> p t q j e", t=4, e=4),
+                )
             else:
+                dealt = w1_bf[u // 2][:].rearrange("p (t q e j) -> p t q e j", t=4, e=4, j=4)[:, :, runs]
+                rows = raw[:].rearrange("p j (q t e) -> p t q e j", t=4, e=4)
                 for t in range(PACK):
                     nc.gpsimd.tensor_scalar(dealt[:, t], rows[:, t], 1.0, 0.0, MULT, ADD)
 
@@ -133,21 +137,23 @@ def tile_list_place_context_kernel(
 
         nc.sync.dma_start(out=page[0][:], in_=base_rows[0])
         place(0)
-        load_w1(shared.tile([P, PACK, QUARTER], F32, name="w1_first", offset=2048, align_bytes=64), 0)
-        page_pairs = [
-            shared.tile([P, PACK * BANK], BF16, name="page_pairs%d" % h, offset=h * PACK * BANK * 2, align_bytes=64)
-            for h in range(2)
-        ]
+        page_pairs = [keep.tile([P, PACK * BANK], BF16, name="page_pairs%d" % h, align_bytes=64) for h in range(2)]
         round_plane(0)
-        nc.sync.dma_start(out=page[1][:], in_=base_rows[1])
-        place(1)
-        round_plane(1)
-        for t in range(2, PACK):
+        for t in range(1, PACK):
             nc.sync.dma_start(out=page[t][:], in_=base_rows[t])
-            load_w1(keep.tile([P, PACK, QUARTER], F32, name="w1_raw%d" % t), t - 1)
             place(t)
             round_plane(t)
-        load_w1(shared.tile([P, PACK, QUARTER], F32, name="w1_last", offset=10240, align_bytes=64), PACK - 1)
+            load_w1(keep.tile([P, PACK, QUARTER], F32, name="w1_raw%d" % t), t - 1)
+        load_w1(shared.tile([P, PACK, QUARTER], F32, name="w1_last", offset=2048, align_bytes=64), PACK - 1)
+        for b in range(2):
+            nc.sync.dma_start(
+                out=gain_rows[PACK * b : PACK * (b + 1), :].rearrange("t (q e) -> t q e", e=4),
+                in_=gain[b * PASS : (b + 1) * PASS].rearrange("(q t e) -> t q e", t=4, e=4),
+            )
+        turned = bank_tile("turned", 7)
+        nc.tensor.transpose(turned[:, 0:P], gain_rows[:], identity[:])
+        gains = keep.tile([P, TILES], F32, name="gains")
+        nc.scalar.copy(out=gains[:], in_=turned[:, 0:TILES])
 
         def load_wo(b):
             raw = keep.tile([P, PACK, N], F32, name="wo_raw%d" % b, tag="wo_raw%d" % b)
@@ -163,15 +169,6 @@ def tile_list_place_context_kernel(
                 in_=raw[:, :, cols].rearrange("p t (c i) -> p c t i", i=4),
             )
 
-        for b in range(2):
-            nc.sync.dma_start(
-                out=gain_rows[PACK * b : PACK * (b + 1), :].rearrange("t (q e) -> t q e", e=4),
-                in_=gain[b * PASS : (b + 1) * PASS].rearrange("(q t e) -> t q e", t=4, e=4),
-            )
-        turned = bank_tile("turned", 7)
-        nc.tensor.transpose(turned[:, 0:P], gain_rows[:], identity[:])
-        gains = keep.tile([P, TILES], F32, name="gains")
-        nc.scalar.copy(out=gains[:], in_=turned[:, 0:TILES])
         wo_raw0 = load_wo(0)
         tab = [keep.tile([P, T], I32, name="tab%d" % a, tag="tab%d" % a, align_bytes=64) for a in range(2)]
         w2_raw = keep.tile([P, 2, 2 * H], U8, name="w2_raw", align_bytes=64)
@@ -198,7 +195,7 @@ def tile_list_place_context_kernel(
         page_q = [mx_tiles("page%d" % h, BANK) for h in range(2)]
         for h in range(2):
             grouped = shared.tile(
-                [P, PACK * BANK], BF16, name="page_grouped%d" % h, offset=(2 + h) * PACK * BANK * 2, align_bytes=64
+                [P, PACK * BANK], BF16, name="page_grouped%d" % h, offset=h * PACK * BANK * 2, align_bytes=64
             )
             weave(nc.vector.tensor_copy, I32, grouped[:], page_pairs[h][:])
             quantize(page_q[h], grouped[:])

@@ -21,13 +21,15 @@ MULT = mybir.AluOpType.mult
 P = 128
 PACK = 4
 PASS = P * PACK
+RUN = 8
 BANK = 512
 BANK_BYTES = 4 * BANK
 TILES = H // P
 HALF = J // 2
 QUARTER = H // 4
-FROM_BANK = 2
-AHEAD = 5
+KIB = 1024
+A_BANKS = 5
+B_BANKS = 4
 
 
 def tile_list_place_context_kernel(
@@ -37,13 +39,14 @@ def tile_list_place_context_kernel(
     with ExitStack() as ctx:
         lists = ctx.enter_context(tc.tile_pool(name="lists", bufs=1))
         keep = ctx.enter_context(tc.tile_pool(name="keep", bufs=1))
-        arows = ctx.enter_context(tc.tile_pool(name="arows", bufs=AHEAD + 1))
-        ring = ctx.enter_context(tc.tile_pool(name="ring", bufs=4))
         shared = ctx.enter_context(tc.tile_pool(name="shared", bufs=1))
         psum = ctx.enter_context(tc.psum_pool(name="psum", bufs=1))
 
         def bank_tile(name, bank):
             return psum.tile([P, BANK], F32, name=name, offset=bank * BANK_BYTES)
+
+        def placed(shape, dtype, name, kib):
+            return shared.tile(shape, dtype, name=name, offset=int(kib * KIB), align_bytes=64)
 
         def mx_tiles(name, width):
             codes = keep.tile([P, width], U32, name=name + "_codes", align_bytes=64)
@@ -53,15 +56,6 @@ def tile_list_place_context_kernel(
         def quantize(operand, grouped):
             codes, scales = operand
             nc.vector.quantize_mx(out=codes.bitcast(FP8X4), scales=scales, in_=grouped)
-
-        def pair_slot(pairs, t):
-            return pairs.rearrange("p (s c e) -> p s c e", s=2, e=2)[:, t // 2, :, t % 2]
-
-        def weave(copy, word, grouped, pairs):
-            copy(
-                out=grouped.bitcast(word).rearrange("p (c i s) -> p c s i", i=4, s=2),
-                in_=pairs.bitcast(word).rearrange("p (s c i) -> p c s i", i=4, s=2),
-            )
 
         idx = lists.tile([P, J // 16], U16, name="idx")
         idx2 = lists.tile([P, S // 16], U16, name="idx2")
@@ -75,14 +69,16 @@ def tile_list_place_context_kernel(
         zero_bias = keep.tile([P, 1], F32, name="zero_bias")
         gain_rows = keep.tile([P, P], F32, name="gain_rows")
         identity = keep.tile([P, P], F32, name="identity")
-        nc.gpsimd.memset(tab_sc[:].bitcast(I32), 0)
+        nc.vector.memset(tab_sc[32:64, :].bitcast(I32), 0)
+        nc.vector.memset(tab_sc[64:P, :].bitcast(I32), 0)
         nc.vector.memset(zero[:], 0.0)
+        nc.vector.memset(w2_sc_raw[:].rearrange("p a c -> p (a c)").bitcast(I32), 0)
         for a in range(2):
             nc.vector.memset(v_sc[a][:].bitcast(I32), 0)
-        nc.vector.memset(w2_sc_raw[:].rearrange("p a c -> p (a c)").bitcast(I32), 0)
         nc.vector.memset(w3_sc[:].rearrange("p a c -> p (a c)").bitcast(I32), 0)
         nc.vector.memset(gain_rows[:], 0.0)
         make_identity(nc, identity[:])
+        nc.scalar.activation(out=zero_bias[:], in_=zero[:], func=SIN)
 
         def load_scale_rows(tile, dram, q):
             nc.sync.dma_start(
@@ -91,73 +87,131 @@ def tile_list_place_context_kernel(
             )
 
         nc.sync.dma_start(
-            out=tab_sc[0:P:4, :].bitcast(I32), in_=tab_scales.rearrange("a g t -> (a g) t").bitcast(I32)
+            out=tab_sc[0:32, :].bitcast(I32), in_=tab_scales.rearrange("a g t -> (a g) t").bitcast(I32)
         )
         nc.sync.dma_start(idx[:], offs)
+        nc.sync.dma_start(idx2[:], offs2)
         picked_sc = keep.tile([P, J], U8, name="picked_sc", align_bytes=64)
         nc.vector.tensor_copy(picked_sc[:], tab_sc[:].indirect(idx[:]))
-        nc.sync.dma_start(idx2[:], offs2)
-        nc.scalar.activation(out=zero_bias[:], in_=zero[:], func=SIN)
 
         base_rows = base.rearrange("(p t) c -> t p c", t=PACK)
         xs_rows = xs.rearrange("(p t) c -> t p c", t=PACK)
-        w1_bf = [keep.tile([P, PASS * PACK], BF16, name="w1_bf%d" % b, align_bytes=64) for b in range(2)]
-        page = [keep.tile([P, T2], F32, name="page%d" % t) for t in range(PACK)]
+        order = (2, 0, 1, 3)
+        page = [placed([P, T2], F32, "page%d" % t, 16 + 4 * order.index(t)) for t in range(PACK)]
         fresh = [keep.tile([P, S], F32, name="fresh%d" % t, tag="fresh%d" % t, align_bytes=64) for t in range(PACK)]
+        tab = [placed([P, T], I32, "tab%d" % a, 8 * a) for a in range(2)]
+        v_codes = []
+        w2_raw = keep.tile([P, 2, 2 * H], U8, name="w2_raw", align_bytes=64)
+        w2_codes = placed([P, 2 * 2 * H], U8, "w2_codes", 38)
+        w2_sc = keep.tile([P, 2 * H], U8, name="w2_sc", align_bytes=64)
+        w1_bf0 = placed([P, PASS * PACK], BF16, "w1_bf0", 32)
 
-        def load_w1(raw, u):
+        def load_plane(t):
+            nc.sync.dma_start(out=page[t][:], in_=base_rows[t])
+            nc.sync.dma_start(out=fresh[t][:], in_=xs_rows[t])
+
+        def place(t):
+            nc.vector.tensor_copy(page[t][:].indirect(idx2[:]), fresh[t][:])
+
+        def load_table(a):
+            nc.sync.dma_start(out=tab[a][:], in_=tab_words[a].rearrange("p t i -> p (t i)").bitcast(I32))
+
+        def pick_words(a):
+            v_codes.append(placed([P, J], U32, "v_codes%d" % a, (60, 16)[a]))
+            nc.vector.tensor_copy(v_codes[a][:], tab[a][:].bitcast(U32).indirect(idx[:]))
+
+        def move_scale_rows(a, q):
+            first = 16 * a + 4 * q
+            nc.sync.dma_start(
+                out=v_sc[a][32 * q : 32 * q + 4, :].bitcast(I32), in_=picked_sc[first : first + 4, :].bitcast(I32)
+            )
+
+        def round_plane(copy, t):
+            for h in range(2):
+                slot = page_pairs[h][:].rearrange("p (s c e) -> p s c e", s=2, e=2)[:, t // 2, :, t % 2]
+                copy(slot, page[t][:, h * BANK : (h + 1) * BANK])
+
+        def load_w1(u):
+            raw = keep.tile([P, PACK, QUARTER], F32, name="w1_raw%d" % u)
             nc.sync.dma_start(
                 out=raw[:], in_=w1[:, u * QUARTER : (u + 1) * QUARTER].rearrange("(p j) r -> p j r", j=PACK)
             )
-            runs = slice(16 * (u % 2), 16 * (u % 2 + 1))
-            if u < 1:
-                nc.scalar.copy(
-                    out=w1_bf[u // 2][:].rearrange("p (t q e j) -> p t q j e", t=4, e=4, j=4)[:, :, runs],
-                    in_=raw[:].rearrange("p j (q t e) -> p t q j e", t=4, e=4),
-                )
-            else:
-                dealt = w1_bf[u // 2][:].rearrange("p (t q e j) -> p t q e j", t=4, e=4, j=4)[:, :, runs]
-                rows = raw[:].rearrange("p j (q t e) -> p t q e j", t=4, e=4)
-                for t in range(PACK):
-                    nc.gpsimd.tensor_scalar(dealt[:, t], rows[:, t], 1.0, 0.0, MULT, ADD)
+            return raw
 
-        def place(t):
-            nc.sync.dma_start(out=fresh[t][:], in_=xs_rows[t])
-            nc.vector.tensor_copy(page[t][:].indirect(idx2[:]), fresh[t][:])
+        def round_w1(raw, u):
+            dealt = w1_bf0[:].rearrange("p (t g e j) -> p g t e j", t=PACK, e=RUN, j=PACK)[:, RUN * u : RUN * (u + 1)]
+            rows = raw[:].rearrange("p j (g t e) -> p g t e j", t=PACK, e=RUN)
+            nc.gpsimd.tensor_scalar(dealt, rows, 1.0, 0.0, MULT, ADD)
 
-        def move_scale_rows(a, q):
-            first = 4 * (16 * a + 4 * q)
-            nc.sync.dma_start(
-                out=v_sc[a][32 * q : 32 * q + 4, :].bitcast(I32), in_=picked_sc[first : first + 16 : 4, :].bitcast(I32)
-            )
-
-        def round_plane(t):
-            for h in range(2):
-                nc.scalar.copy(out=pair_slot(page_pairs[h][:], t), in_=page[t][:, h * BANK : (h + 1) * BANK])
-
-        nc.sync.dma_start(out=page[0][:], in_=base_rows[0])
-        place(0)
         page_pairs = [keep.tile([P, PACK * BANK], BF16, name="page_pairs%d" % h, align_bytes=64) for h in range(2)]
-        round_plane(0)
-        for t in range(1, PACK):
-            nc.sync.dma_start(out=page[t][:], in_=base_rows[t])
+        for t in order[0:2]:
+            load_plane(t)
             place(t)
-            round_plane(t)
-            load_w1(keep.tile([P, PACK, QUARTER], F32, name="w1_raw%d" % t), t - 1)
-        load_w1(shared.tile([P, PACK, QUARTER], F32, name="w1_last", offset=2048, align_bytes=64), PACK - 1)
-        for b in range(2):
-            nc.sync.dma_start(
-                out=gain_rows[PACK * b : PACK * (b + 1), :].rearrange("t (q e) -> t q e", e=4),
-                in_=gain[b * PASS : (b + 1) * PASS].rearrange("(q t e) -> t q e", t=4, e=4),
+            round_plane(nc.scalar.copy, t)
+        load_table(0)
+        pick_words(0)
+        for q in range(4):
+            load_scale_rows(w2_sc_raw, w2_scales, q)
+        nc.sync.dma_start(out=w2_raw[:].bitcast(I32), in_=w2_words.rearrange("a p c -> p a c").bitcast(I32))
+        nc.scalar.copy(
+            w2_codes[:].bitcast(U32).rearrange("p (b t g e) -> p b t g e", t=PACK, g=16, e=4),
+            w2_raw[:].rearrange("p a c -> p (a c)").bitcast(U32).rearrange("p (b g t e) -> p b t g e", t=PACK, g=16, e=4),
+        )
+        nc.scalar.copy(
+            w2_sc[:].bitcast(U32).rearrange("p (b t g e) -> p b t g e", t=PACK, g=16, e=2),
+            w2_sc_raw[:].rearrange("p a c -> p (a c)").bitcast(U32).rearrange("p (b g t e) -> p b t g e", t=PACK, g=16, e=2),
+        )
+        nc.sync.dma_start(out=page[1][:], in_=base_rows[1])
+        move_scale_rows(0, 0)
+        nc.sync.dma_start(out=fresh[1][:], in_=xs_rows[1])
+        place(1)
+        round_plane(nc.scalar.copy, 1)
+        move_scale_rows(0, 1)
+        load_table(1)
+        pick_words(1)
+        for q in range(2, 4):
+            move_scale_rows(0, q)
+        move_scale_rows(1, 0)
+        nc.sync.dma_start(out=page[3][:], in_=base_rows[3])
+        move_scale_rows(1, 1)
+        nc.sync.dma_start(out=fresh[3][:], in_=xs_rows[3])
+        place(3)
+        w1_raw = [load_w1(0)]
+        for q in range(2, 4):
+            move_scale_rows(1, q)
+        w1_raw.append(load_w1(1))
+        for u in range(2):
+            round_w1(w1_raw[u], u)
+        w1_late = keep.tile([P, PACK, PASS], F32, name="w1_late")
+        nc.sync.dma_start(out=w1_late[:], in_=w1[:, PASS:H].rearrange("(p j) r -> p j r", j=PACK))
+
+        b_acc = [bank_tile("b%d" % i, i % B_BANKS) for i in range(TILES)]
+        b_rows = [placed([P, J], F32, "b_rows%d" % i, 44 + 2 * i) for i in range(TILES)]
+
+        def object_pass(i, a):
+            col = a * H + i * P
+            nc.tensor.matmul_mx(
+                out=b_acc[i][:],
+                lhsT=w2_codes[:, 2 * col : 2 * (col + P)].bitcast(FP4X4),
+                lhsT_scale=w2_sc[:, col : col + P],
+                rhs=v_codes[a][:].bitcast(FP8X4),
+                rhs_scale=v_sc[a][:],
+                start=(a == 0),
+                stop=(a == 1),
             )
-        turned = bank_tile("turned", 7)
-        nc.tensor.transpose(turned[:, 0:P], gain_rows[:], identity[:])
-        gains = keep.tile([P, TILES], F32, name="gains")
-        nc.scalar.copy(out=gains[:], in_=turned[:, 0:TILES])
+            if a == 1:
+                nc.scalar.copy(b_rows[i][:], b_acc[i][:])
+
+        for a in range(2):
+            for i in range(B_BANKS):
+                object_pass(i, a)
+        for i in range(B_BANKS, TILES):
+            for a in range(2):
+                object_pass(i, a)
 
         def load_wo(b):
             raw = keep.tile([P, PACK, N], F32, name="wo_raw%d" % b, tag="wo_raw%d" % b)
-            rows = wo[b * PASS : (b + 1) * PASS, :].rearrange("(q t e) n -> t q e n", t=4, e=4)
+            rows = wo[b * PASS : (b + 1) * PASS, :].rearrange("(g t e) n -> t g e n", t=PACK, e=RUN)
             for t in range(PACK):
                 nc.sync.dma_start(out=raw[:, t, :], in_=rows[t])
             return raw
@@ -165,137 +219,148 @@ def tile_list_place_context_kernel(
         def round_wo(grouped, raw, u):
             cols = slice(u * HALF, (u + 1) * HALF)
             nc.scalar.copy(
-                out=grouped[:].rearrange("p (c i t) -> p c t i", i=4, t=PACK)[:, u * HALF // 4 : (u + 1) * HALF // 4],
-                in_=raw[:, :, cols].rearrange("p t (c i) -> p c t i", i=4),
+                grouped[:].rearrange("p (c i t) -> p c t i", i=4, t=PACK)[:, u * HALF // 4 : (u + 1) * HALF // 4],
+                raw[:, :, cols].rearrange("p t (c i) -> p c t i", i=4),
             )
 
-        wo_raw0 = load_wo(0)
-        tab = [keep.tile([P, T], I32, name="tab%d" % a, tag="tab%d" % a, align_bytes=64) for a in range(2)]
-        w2_raw = keep.tile([P, 2, 2 * H], U8, name="w2_raw", align_bytes=64)
-        w3_codes = keep.tile([P, 2, N], I32, name="w3_codes", align_bytes=64)
-        nc.sync.dma_start(out=tab[0][:], in_=tab_words[0].rearrange("p t i -> p (t i)").bitcast(I32))
-        nc.sync.dma_start(out=w2_raw[:].bitcast(I32), in_=w2_words.rearrange("a p c -> p a c").bitcast(I32))
-        nc.sync.dma_start(out=tab[1][:], in_=tab_words[1].rearrange("p t i -> p (t i)").bitcast(I32))
-        for q in range(4):
-            load_scale_rows(w2_sc_raw, w2_scales, q)
         nc.sync.dma_start(idx3[:], offs3)
-        for a in range(2):
-            for q in range(4):
-                move_scale_rows(a, q)
-        wo_raw1 = load_wo(1)
+        wo_raw0 = load_wo(0)
+        for b in range(2):
+            nc.sync.dma_start(
+                out=gain_rows[PACK * b : PACK * (b + 1), :].rearrange("t (g e) -> t g e", e=RUN),
+                in_=gain[b * PASS : (b + 1) * PASS].rearrange("(g t e) -> t g e", t=PACK, e=RUN),
+            )
+        w3_codes = keep.tile([P, 2, N], I32, name="w3_codes", align_bytes=64)
         nc.sync.dma_start(out=w3_codes[:], in_=w3_words.rearrange("a p c i -> p a (c i)").bitcast(I32))
         for q in range(4):
             load_scale_rows(w3_sc, w3_scales, q)
+        wo_raw1 = load_wo(1)
 
-        w1_codes = keep.tile([P, 2, PASS], U32, name="w1_codes", tag="fresh3", align_bytes=64)
-        scale_planes = [keep.tile([P, PASS], U8, name="scales%d" % u, align_bytes=64) for u in range(3)]
-        w1_q = [(w1_codes[:, b, :], scale_planes[b][:]) for b in range(2)]
-        for b in range(2):
-            quantize(w1_q[b], w1_bf[b][:])
-        page_q = [mx_tiles("page%d" % h, BANK) for h in range(2)]
+        w1_codes0 = keep.tile([P, PASS], U32, name="w1_codes0", tag="fresh3", align_bytes=64)
+        w1_sc0 = keep.tile([P, PASS], U8, name="w1_sc0", align_bytes=64)
+        quantize((w1_codes0[:], w1_sc0[:]), w1_bf0[:])
+        round_plane(nc.vector.tensor_copy, 3)
+        page_q = [
+            (keep.tile([P, BANK], U32, name="page%d_codes" % h, align_bytes=64)[:], placed([P, BANK], U8, "page%d_scales" % h, 40 + h)[:])
+            for h in range(2)
+        ]
+        grouped = [keep.tile([P, PACK * BANK], BF16, name="page_grouped%d" % h, tag="grouped%d" % h, align_bytes=64) for h in range(2)]
         for h in range(2):
-            grouped = shared.tile(
-                [P, PACK * BANK], BF16, name="page_grouped%d" % h, offset=h * PACK * BANK * 2, align_bytes=64
+            nc.vector.tensor_copy(
+                out=grouped[h][:].bitcast(I32).rearrange("p (c i s) -> p c s i", i=4, s=2),
+                in_=page_pairs[h][:].bitcast(I32).rearrange("p (s c i) -> p c s i", i=4, s=2),
             )
-            weave(nc.vector.tensor_copy, I32, grouped[:], page_pairs[h][:])
-            quantize(page_q[h], grouped[:])
-        wo_bf0 = keep.tile([P, N * PACK], BF16, name="wo_bf0", align_bytes=64)
+        for h in range(2):
+            quantize(page_q[h], grouped[h][:])
+        w1_q = [(w1_codes0[:, t * P : (t + 1) * P], w1_sc0[:, t * P : (t + 1) * P]) for t in range(PACK)]
+        late_rows = w1_late[:].rearrange("p j (g t e) -> p t g j e", t=PACK, e=RUN)
+        late_bf = []
         for u in range(2):
-            round_wo(wo_bf0, wo_raw0, u)
+            dealt = placed([P, 2 * PASS], BF16, "w1_bf1_%d" % u, (37, 41.5)[u])
+            nc.scalar.copy(dealt[:].rearrange("p (t g e j) -> p t g j e", t=2, e=RUN, j=PACK), late_rows[:, 2 * u : 2 * u + 2])
+            late_bf.append(dealt)
 
-        v_codes = [keep.tile([P, J], U32, name="v_codes%d" % a, align_bytes=64) for a in range(2)]
-        nc.vector.tensor_copy(v_codes[0][:], tab[0][:].bitcast(U32).indirect(idx[:]))
-        w2_codes = keep.tile([P, 2 * 2 * H], U8, name="w2_codes", align_bytes=64)
-        w2_sc = keep.tile([P, 2 * H], U8, name="w2_sc", align_bytes=64)
+        def quantize_late(u, codes):
+            scales = keep.tile([P, 2 * P], U8, name="w1_1_%d_scales" % u, align_bytes=64)
+            quantize((codes[:], scales[:]), late_bf[u][:])
+            w1_q.extend((codes[:, t * P : (t + 1) * P], scales[:, t * P : (t + 1) * P]) for t in range(2))
+
+        quantize_late(0, keep.tile([P, 2 * P], U32, name="w1_1_0_codes", align_bytes=64))
+        wo_bf = [
+            keep.tile([P, N * PACK], BF16, name="wo_bf%d" % b, tag=tag, align_bytes=64)
+            for b, tag in enumerate(("grouped1", "wo_bf1"))
+        ]
         nc.vector.tensor_copy(
-            out=w2_sc[:].bitcast(I32).rearrange("p (g t q) -> p g t q", t=4, q=32),
-            in_=w2_sc_raw[:].rearrange("p a c -> p (a c)").bitcast(I32).rearrange("p (g q t) -> p g t q", t=4, q=32),
+            wo_bf[0][:].rearrange("p (c i t) -> p c t i", i=4, t=PACK), wo_raw0[:].rearrange("p t (c i) -> p c t i", i=4)
         )
-        nc.vector.tensor_copy(
-            out=w2_codes[:].bitcast(I32).rearrange("p (g t q e) -> p g t q e", t=4, q=32, e=2),
-            in_=w2_raw[:].rearrange("p a c -> p (a c)").bitcast(I32).rearrange("p (g q t e) -> p g t q e", t=4, q=32, e=2),
-        )
-        nc.vector.tensor_copy(v_codes[1][:], tab[1][:].bitcast(U32).indirect(idx[:]))
-        wo_codes = keep.tile([P, PASS], U32, name="wo_codes", tag="tab0", align_bytes=64)
-        wo_q = [(wo_codes[:], scale_planes[2][:])]
 
-        a_rows = {}
+        a_rows = [keep.tile([P, T2], F32, name="a_rows%d" % i) for i in range(TILES)]
 
-        def project_page(i, h):
-            b, t = divmod(i, PACK)
-            if i not in a_rows:
-                a_rows[i] = arows.tile([P, T2], F32, name="a_rows")
-            acc = bank_tile("a%d_%d" % (i, h), (2 * i + h) % 3 if i < AHEAD else 3 + (2 * (i - AHEAD + 1) + h) % 4)
-            nc.tensor.matmul_mx(
-                out=acc[:],
-                lhsT=w1_q[b][0][:, t * P : (t + 1) * P].bitcast(FP8X4),
-                lhsT_scale=w1_q[b][1][:, t * P : (t + 1) * P],
-                rhs=page_q[h][0].bitcast(FP8X4),
-                rhs_scale=page_q[h][1],
-                start=True,
-                stop=True,
-            )
-            nc.scalar.copy(out=a_rows[i][:, h * BANK : (h + 1) * BANK], in_=acc[:])
-
-        def project_objects(i):
-            acc = bank_tile("b%d" % i, 3 + i % 4)
-            for a in range(2):
-                col = a * H + i * P
+        def project_page(i):
+            for h in range(2):
+                acc = bank_tile("a%d_%d" % (i, h), (B_BANKS + 2 * i + h) % A_BANKS)
                 nc.tensor.matmul_mx(
                     out=acc[:],
-                    lhsT=w2_codes[:, 2 * col : 2 * (col + P)].bitcast(FP4X4),
-                    lhsT_scale=w2_sc[:, col : col + P],
-                    rhs=v_codes[a][:].bitcast(FP8X4),
-                    rhs_scale=v_sc[a][:],
-                    start=(a == 0),
-                    stop=(a == 1),
+                    lhsT=w1_q[i][0].bitcast(FP8X4),
+                    lhsT_scale=w1_q[i][1],
+                    rhs=page_q[h][0].bitcast(FP8X4),
+                    rhs_scale=page_q[h][1],
+                    start=True,
+                    stop=True,
                 )
-            if i < FROM_BANK:
-                return acc
-            rows = ring.tile([P, J], F32, name="b_rows")
-            nc.scalar.copy(out=rows[:], in_=acc[:])
-            return rows
+                copy = nc.vector.tensor_copy if (i, h) == (0, 1) else nc.scalar.copy
+                copy(a_rows[i][:, h * BANK : (h + 1) * BANK], acc[:])
 
-        def gather(arg, i, b_rows, j0, j1):
-            window = a_rows[i][:].indirect(idx3[:, j0 // 16 : j1 // 16])
-            if i < FROM_BANK:
-                picked = keep.tile([P, j1 - j0], F32, name="picked%d" % i)
-                nc.vector.tensor_copy(picked[:], window)
-                nc.vector.tensor_tensor(arg, b_rows[:, j0:j1], picked[:], ADD)
-            else:
-                nc.vector.tensor_tensor(arg, window, b_rows[:, j0:j1], ADD)
+        def gather(arg, i, j0, j1):
+            nc.vector.tensor_tensor(arg, a_rows[i][:].indirect(idx3[:, j0 // 16 : j1 // 16]), b_rows[i][:, j0:j1], ADD)
 
-        sines = [keep.tile([P, PACK, J], F32, name="sines%d" % b, tag="sines%d" % b, align_bytes=64) for b in range(2)]
+        args = [placed([P, 2 * J], F32, "arg%d" % pair, 4 * pair) for pair in range(PACK)]
+        sines = [placed([P, PACK, J], F32, "sines%d" % b, 20 + 8 * b) for b in range(2)]
 
-        def sine(arg, i, count, j0, j1):
+        def gather_whole(i):
+            gather(args[i // 2][:, i % 2 * J : (i % 2 + 1) * J], i, 0, J)
+
+        def sine(arg, i, j0, j1):
             b, t = divmod(i, PACK)
             nc.scalar.activation(
-                out=sines[b][:, t : t + count, j0:j1],
-                in_=arg.rearrange("p (u j) -> p u j", u=count),
+                out=sines[b][:, t : t + 2, j0:j1],
+                in_=arg.rearrange("p (u j) -> p u j", u=2),
                 func=SIN,
                 bias=zero_bias[:],
             )
 
+        gains = keep.tile([P, TILES], F32, name="gains")
+
         def weigh(b, j0, j1):
             width = j1 - j0
-            grouped = keep.tile([P, width * PACK], BF16, name="h_bf%d_%d" % (b, j0), align_bytes=64)
+            weighed = keep.tile([P, width * PACK], BF16, name="h_bf%d_%d" % (b, j0), align_bytes=64)
             nc.vector.tensor_tensor(
-                grouped[:].rearrange("p (c i t) -> p c t i", i=4, t=PACK),
+                weighed[:].rearrange("p (c i t) -> p c t i", i=4, t=PACK),
                 sines[b][:, :, j0:j1].rearrange("p t (c i) -> p c t i", i=4),
                 gains[:, PACK * b : PACK * (b + 1)].unsqueeze(1).unsqueeze(3).to_broadcast([P, width // 4, PACK, 4]),
                 MULT,
             )
-            return grouped
+            return weighed
 
-        def quantize_h(name, grouped, width):
+        def quantize_h(name, weighed, width):
             operand = mx_tiles(name, width)
-            quantize(operand, grouped[:])
+            quantize(operand, weighed[:])
             return operand
+
+        for i in range(PACK):
+            project_page(i)
+            gather_whole(i)
+            if i == 1:
+                turned = bank_tile("turned", B_BANKS % A_BANKS)
+                nc.tensor.transpose(turned[:, 0:P], gain_rows[:], identity[:])
+                nc.scalar.copy(gains[:], turned[:, 0:TILES])
+        wo_q = [(placed([P, N], U32, "wo0_codes", 49)[:], keep.tile([P, N], U8, name="wo0_scales", align_bytes=64)[:])]
+        quantize_late(1, placed([P, 2 * P], U32, "w1_1_1_codes", 51))
+        quantize(wo_q[0], wo_bf[0][:])
+        wo_q.append(mx_tiles("wo1", N))
+        sine(args[0][:], 0, 0, J)
+        project_page(4)
+        gather_whole(4)
+        sine(args[1][:], 2, 0, J)
+        h0_bf = weigh(0, 0, J)
+        for i in range(5, TILES):
+            project_page(i)
+        gather_whole(5)
+        h0 = quantize_h("h0", h0_bf, J)
+        round_wo(wo_bf[1], wo_raw1, 0)
+        sine(args[2][:], PACK, 0, J)
+        for u in range(2):
+            for k in range(2):
+                first = u * J + k * HALF
+                gather(args[3][:, first : first + HALF], 6 + k, u * HALF, (u + 1) * HALF)
+        sine(args[3][:, 0:J], 6, 0, HALF)
+        round_wo(wo_bf[1], wo_raw1, 1)
+        sine(args[3][:, J : 2 * J], 6, HALF, J)
 
         d_rows = keep.tile([P, 2, N // P, HALF], F32, name="d_rows", tag="wo_raw1")
 
         def modulation(u, pair):
-            acc = bank_tile("d%d_%d" % (u, pair), (7, 2, 3, 4)[2 * pair + u])
+            acc = bank_tile("d%d_%d" % (u, pair), 4 + (2 * u + pair + 1) % 4)
             cols = slice(u * HALF, (u + 1) * HALF)
             for k in range(2):
                 nt = 2 * pair + k
@@ -309,52 +374,7 @@ def tile_list_place_context_kernel(
                         start=(a == 0),
                         stop=(a == 1),
                     )
-            nc.scalar.copy(
-                out=d_rows[:, u, 2 * pair : 2 * pair + 2, :], in_=acc[:].rearrange("p (k j) -> p k j", k=2)
-            )
-
-        quantize(wo_q[0], wo_bf0[:])
-        for i in range(AHEAD):
-            for h in range(2):
-                project_page(i, h)
-        whole = TILES - 2
-        b_rows = {}
-        args = [ring.tile([P, 2 * J], F32, name="arg") for pair in range(whole // 2)]
-        for i in range(whole):
-            if i >= AHEAD:
-                for h in range(2):
-                    project_page(i, h)
-            b_rows[i] = project_objects(i)
-            gather(args[i // 2][:, i % 2 * J : (i % 2 + 1) * J], i, b_rows[i], 0, J)
-        for pair in range(2):
-            sine(args[pair][:], 2 * pair, 2, 0, J)
-        h0_bf = weigh(0, 0, J)
-        for h in range(2):
-            project_page(whole, h)
-        for i in range(whole, TILES):
-            b_rows[i] = project_objects(i)
-        for h in range(2):
-            project_page(whole + 1, h)
-        sine(args[2][:], PACK, 2, 0, J)
-        h0 = quantize_h("h0", h0_bf, J)
-        half_args = []
-        for u in range(2):
-            half_args.append(ring.tile([P, J], F32, name="half_arg"))
-            for i in range(whole, TILES):
-                cols = slice((i - whole) * HALF, (i - whole + 1) * HALF)
-                gather(half_args[u][:, cols], i, b_rows[i], u * HALF, (u + 1) * HALF)
-        wo_bf1 = keep.tile([P, N * PACK], BF16, name="wo_bf1", tag="sines0", align_bytes=64)
-        h1_bf = []
-        wo_q.append(mx_tiles("wo1", N))
-        for u in range(2):
-            sine(half_args[u][:], whole, 2, u * HALF, (u + 1) * HALF)
-            h1_bf.append(weigh(1, u * HALF, (u + 1) * HALF))
-            round_wo(wo_bf1, wo_raw1, u)
-        h1 = []
-        for u in range(2):
-            h1.append(quantize_h("h1_%d" % u, h1_bf[u], HALF))
-            cols = slice(u * HALF, (u + 1) * HALF)
-            quantize((wo_q[1][0][:, cols], wo_q[1][1][:, cols]), wo_bf1[:, u * HALF * PACK : (u + 1) * HALF * PACK])
+            nc.scalar.copy(d_rows[:, u, 2 * pair : 2 * pair + 2, :], acc[:].rearrange("p (k j) -> p k j", k=2))
 
         out_rows = out.rearrange("(nt p) j -> p nt j", p=P)
 
@@ -371,24 +391,42 @@ def tile_list_place_context_kernel(
                     stop=(b == 1 and u == 1),
                 )
 
-        y_acc = [[bank_tile("y%d_%d" % (u, pair), (5, 0)[u] + pair) for pair in range(2)] for u in range(2)]
-        for pair in range(2):
-            for u in range(2):
+        y_acc = [[bank_tile("y%d_%d" % (u, pair), 2 * u + pair) for pair in range(2)] for u in range(2)]
+        for u in range(2):
+            for pair in range(2):
                 modulation(u, pair)
         for u in range(2):
             for pair in range(2):
                 y_passes(y_acc[u][pair], pair, 0, h0, slice(u * HALF, (u + 1) * HALF))
+
+        def finish(u, pair):
+            cols = slice(u * HALF, (u + 1) * HALF)
+            rows = slice(2 * pair, 2 * pair + 2)
+            result = keep.tile([P, 2, HALF], F32, name="result%d_%d" % (u, pair))
+            acc = y_acc[u][pair][:].rearrange("p (k j) -> p k j", k=2)
+            nc.vector.tensor_tensor(result[:], acc, d_rows[:, u, rows, :], MULT)
+            if pair == 1 and u == 1:
+                for k, queue in enumerate((nc.scalar, nc.sync)):
+                    queue.dma_start(out=out_rows[:, 2 * pair + k, cols], in_=result[:, k, :])
+            else:
+                nc.sync.dma_start(out=out_rows[:, rows, cols], in_=result[:])
+
+        def quantize_wo(pair):
+            cols = slice(pair * HALF, (pair + 1) * HALF)
+            rounded = wo_bf[1][:, pair * HALF * PACK : (pair + 1) * HALF * PACK]
+            quantize((wo_q[1][0][:, cols], wo_q[1][1][:, cols]), rounded)
+
+        first_half = weigh(1, 0, HALF)
+        quantize_wo(0)
+        h1 = quantize_h("h1_0", first_half, HALF)
+        y_passes(y_acc[0][0], 0, 1, h1, slice(0, HALF))
+        second_half = weigh(1, HALF, J)
+        quantize_wo(1)
+        y_passes(y_acc[0][1], 1, 1, h1, slice(0, HALF))
+        finish(0, 0)
+        h1 = quantize_h("h1_1", second_half, HALF)
         for pair in range(2):
-            for u in range(2):
-                y_passes(y_acc[u][pair], pair, 1, h1[u], slice(0, HALF))
-            for u in range(2):
-                cols = slice(u * HALF, (u + 1) * HALF)
-                rows = slice(2 * pair, 2 * pair + 2)
-                result = keep.tile([P, 2, HALF], F32, name="result%d_%d" % (u, pair))
-                acc = y_acc[u][pair][:].rearrange("p (k j) -> p k j", k=2)
-                nc.vector.tensor_tensor(result[:], acc, d_rows[:, u, rows, :], MULT)
-                if pair == 1 and u == 1:
-                    for k, queue in enumerate((nc.scalar, nc.sync)):
-                        queue.dma_start(out=out_rows[:, 2 * pair + k, cols], in_=result[:, k, :])
-                else:
-                    nc.sync.dma_start(out=out_rows[:, rows, cols], in_=result[:])
+            y_passes(y_acc[1][pair], pair, 1, h1, slice(0, HALF))
+        finish(0, 1)
+        for pair in range(2):
+            finish(1, pair)

@@ -28,8 +28,8 @@ TILES = H // P
 HALF = J // 2
 QUARTER = H // 4
 KIB = 1024
-A_BANKS = 5
-B_BANKS = 4
+B_BANKS = 3
+SHARE = 176
 
 
 def tile_list_place_context_kernel(
@@ -80,10 +80,9 @@ def tile_list_place_context_kernel(
         make_identity(nc, identity[:])
         nc.scalar.activation(out=zero_bias[:], in_=zero[:], func=SIN)
 
-        def load_scale_rows(tile, dram, q):
+        def load_scale_rows(tile, dram, r):
             nc.sync.dma_start(
-                out=tile[32 * q : 32 * q + 4, :, :].bitcast(I32),
-                in_=dram[:, 4 * q : 4 * q + 4, :].rearrange("a r c -> r a c").bitcast(I32),
+                out=tile[r:P:32, :, :].bitcast(I32), in_=dram[:, r:16:4, :].rearrange("a q c -> q a c").bitcast(I32)
             )
 
         nc.sync.dma_start(
@@ -120,10 +119,9 @@ def tile_list_place_context_kernel(
             v_codes.append(placed([P, J], U32, "v_codes%d" % a, (60, 16)[a]))
             nc.vector.tensor_copy(v_codes[a][:], tab[a][:].bitcast(U32).indirect(idx[:]))
 
-        def move_scale_rows(a, q):
-            first = 16 * a + 4 * q
+        def move_scale_rows(a, r):
             nc.sync.dma_start(
-                out=v_sc[a][32 * q : 32 * q + 4, :].bitcast(I32), in_=picked_sc[first : first + 4, :].bitcast(I32)
+                out=v_sc[a][r:P:32, :].bitcast(I32), in_=picked_sc[16 * a + r : 16 * a + 16 : 4, :].bitcast(I32)
             )
 
         def round_plane(copy, t):
@@ -216,9 +214,9 @@ def tile_list_place_context_kernel(
                 nc.sync.dma_start(out=raw[:, t, :], in_=rows[t])
             return raw
 
-        def round_wo(grouped, raw, u):
+        def round_wo(copy, grouped, raw, u):
             cols = slice(u * HALF, (u + 1) * HALF)
-            nc.scalar.copy(
+            copy(
                 grouped[:].rearrange("p (c i t) -> p c t i", i=4, t=PACK)[:, u * HALF // 4 : (u + 1) * HALF // 4],
                 raw[:, :, cols].rearrange("p t (c i) -> p c t i", i=4),
             )
@@ -266,19 +264,12 @@ def tile_list_place_context_kernel(
             w1_q.extend((codes[:, t * P : (t + 1) * P], scales[:, t * P : (t + 1) * P]) for t in range(2))
 
         quantize_late(0, keep.tile([P, 2 * P], U32, name="w1_1_0_codes", align_bytes=64))
-        wo_bf = [
-            keep.tile([P, N * PACK], BF16, name="wo_bf%d" % b, tag=tag, align_bytes=64)
-            for b, tag in enumerate(("grouped1", "wo_bf1"))
-        ]
-        nc.vector.tensor_copy(
-            wo_bf[0][:].rearrange("p (c i t) -> p c t i", i=4, t=PACK), wo_raw0[:].rearrange("p t (c i) -> p c t i", i=4)
-        )
 
         a_rows = [keep.tile([P, T2], F32, name="a_rows%d" % i) for i in range(TILES)]
 
         def project_page(i):
             for h in range(2):
-                acc = bank_tile("a%d_%d" % (i, h), (B_BANKS + 2 * i + h) % A_BANKS)
+                acc = bank_tile("a%d_%d" % (i, h), (2 - i % 2, (0, 7, 3, 4, 5, 6, 0, 3)[i])[h])
                 nc.tensor.matmul_mx(
                     out=acc[:],
                     lhsT=w1_q[i][0].bitcast(FP8X4),
@@ -309,17 +300,22 @@ def tile_list_place_context_kernel(
                 bias=zero_bias[:],
             )
 
-        gains = keep.tile([P, TILES], F32, name="gains")
-
-        def weigh(b, j0, j1):
+        def weigh(b, j0, j1, cut):
             width = j1 - j0
             weighed = keep.tile([P, width * PACK], BF16, name="h_bf%d_%d" % (b, j0), align_bytes=64)
             nc.vector.tensor_tensor(
-                weighed[:].rearrange("p (c i t) -> p c t i", i=4, t=PACK),
-                sines[b][:, :, j0:j1].rearrange("p t (c i) -> p c t i", i=4),
-                gains[:, PACK * b : PACK * (b + 1)].unsqueeze(1).unsqueeze(3).to_broadcast([P, width // 4, PACK, 4]),
+                weighed[:, 0 : cut * PACK].rearrange("p (c i t) -> p c t i", i=4, t=PACK),
+                sines[b][:, :, j0 : j0 + cut].rearrange("p t (c i) -> p c t i", i=4),
+                turned[:, PACK * b : PACK * (b + 1)].unsqueeze(1).unsqueeze(3).to_broadcast([P, cut // 4, PACK, 4]),
                 MULT,
             )
+            if cut < width:
+                nc.gpsimd.tensor_tensor(
+                    weighed[:, cut * PACK :].rearrange("p (j t) -> p j t", t=PACK),
+                    sines[b][:, :, j0 + cut : j1].rearrange("p t j -> p j t"),
+                    gains[:, PACK * b : PACK * (b + 1)].unsqueeze(1).to_broadcast([P, width - cut, PACK]),
+                    MULT,
+                )
             return weighed
 
         def quantize_h(name, weighed, width):
@@ -330,37 +326,42 @@ def tile_list_place_context_kernel(
         for i in range(PACK):
             project_page(i)
             gather_whole(i)
-            if i == 1:
-                turned = bank_tile("turned", B_BANKS % A_BANKS)
-                nc.tensor.transpose(turned[:, 0:P], gain_rows[:], identity[:])
-                nc.scalar.copy(gains[:], turned[:, 0:TILES])
-        wo_q = [(placed([P, N], U32, "wo0_codes", 49)[:], keep.tile([P, N], U8, name="wo0_scales", align_bytes=64)[:])]
-        quantize_late(1, placed([P, 2 * P], U32, "w1_1_1_codes", 51))
-        quantize(wo_q[0], wo_bf[0][:])
-        wo_q.append(mx_tiles("wo1", N))
+        turned = bank_tile("turned", 7)
+        nc.tensor.transpose(turned[:, 0:P], gain_rows[:], identity[:])
+        gains = keep.tile([P, TILES], F32, name="gains")
+        nc.scalar.copy(gains[:], turned[:, 0:TILES])
+        quantize_late(1, placed([P, 2 * P], U32, "w1_1_1_codes", 48))
+        wo_q = [mx_tiles("wo%d" % b, N) for b in range(2)]
         sine(args[0][:], 0, 0, J)
         project_page(4)
         gather_whole(4)
         sine(args[1][:], 2, 0, J)
-        h0_bf = weigh(0, 0, J)
+        h0_bf = weigh(0, 0, J, J)
+        wo_bf = [placed([P, N * PACK], BF16, "wo_bf0", 50), keep.tile([P, N * PACK], BF16, name="wo_bf1", align_bytes=64)]
+        nc.gpsimd.tensor_scalar(
+            wo_bf[0][:].rearrange("p (n t) -> p n t", t=PACK), wo_raw0[:].rearrange("p t n -> p n t"), 1.0, 0.0, MULT, ADD
+        )
         for i in range(5, TILES):
             project_page(i)
         gather_whole(5)
         h0 = quantize_h("h0", h0_bf, J)
-        round_wo(wo_bf[1], wo_raw1, 0)
+        quantize(wo_q[0], wo_bf[0][:])
+        round_wo(nc.scalar.copy, wo_bf[1], wo_raw1, 0)
         sine(args[2][:], PACK, 0, J)
         for u in range(2):
             for k in range(2):
                 first = u * J + k * HALF
                 gather(args[3][:, first : first + HALF], 6 + k, u * HALF, (u + 1) * HALF)
         sine(args[3][:, 0:J], 6, 0, HALF)
-        round_wo(wo_bf[1], wo_raw1, 1)
+        round_wo(nc.scalar.copy, wo_bf[1], wo_raw1, 1)
         sine(args[3][:, J : 2 * J], 6, HALF, J)
 
-        d_rows = keep.tile([P, 2, N // P, HALF], F32, name="d_rows", tag="wo_raw1")
+        d_first = placed([P, 2, HALF], F32, "d_first", 54)
+        d_later = keep.tile([P, 3, 2, HALF], F32, name="d_later", tag="wo_raw1")
+        d_rows = [d_first[:]] + [d_later[:, k] for k in range(3)]
 
         def modulation(u, pair):
-            acc = bank_tile("d%d_%d" % (u, pair), 4 + (2 * u + pair + 1) % 4)
+            acc = bank_tile("d%d_%d" % (u, pair), 4 + (2 * u + pair) % 3)
             cols = slice(u * HALF, (u + 1) * HALF)
             for k in range(2):
                 nt = 2 * pair + k
@@ -374,7 +375,7 @@ def tile_list_place_context_kernel(
                         start=(a == 0),
                         stop=(a == 1),
                     )
-            nc.scalar.copy(d_rows[:, u, 2 * pair : 2 * pair + 2, :], acc[:].rearrange("p (k j) -> p k j", k=2))
+            nc.scalar.copy(d_rows[2 * u + pair], acc[:].rearrange("p (k j) -> p k j", k=2))
 
         out_rows = out.rearrange("(nt p) j -> p nt j", p=P)
 
@@ -404,7 +405,7 @@ def tile_list_place_context_kernel(
             rows = slice(2 * pair, 2 * pair + 2)
             result = keep.tile([P, 2, HALF], F32, name="result%d_%d" % (u, pair))
             acc = y_acc[u][pair][:].rearrange("p (k j) -> p k j", k=2)
-            nc.vector.tensor_tensor(result[:], acc, d_rows[:, u, rows, :], MULT)
+            nc.vector.tensor_tensor(result[:], acc, d_rows[2 * u + pair], MULT)
             if pair == 1 and u == 1:
                 for k, queue in enumerate((nc.scalar, nc.sync)):
                     queue.dma_start(out=out_rows[:, 2 * pair + k, cols], in_=result[:, k, :])
@@ -416,11 +417,11 @@ def tile_list_place_context_kernel(
             rounded = wo_bf[1][:, pair * HALF * PACK : (pair + 1) * HALF * PACK]
             quantize((wo_q[1][0][:, cols], wo_q[1][1][:, cols]), rounded)
 
-        first_half = weigh(1, 0, HALF)
+        first_half = weigh(1, 0, HALF, SHARE)
         quantize_wo(0)
         h1 = quantize_h("h1_0", first_half, HALF)
         y_passes(y_acc[0][0], 0, 1, h1, slice(0, HALF))
-        second_half = weigh(1, HALF, J)
+        second_half = weigh(1, HALF, J, SHARE)
         quantize_wo(1)
         y_passes(y_acc[0][1], 1, 1, h1, slice(0, HALF))
         finish(0, 0)

@@ -29,7 +29,6 @@ HALF = J // 2
 QUARTER = H // 4
 KIB = 1024
 B_BANKS = 3
-SHARE = 176
 
 
 def tile_list_place_context_kernel(
@@ -69,19 +68,18 @@ def tile_list_place_context_kernel(
         zero_bias = keep.tile([P, 1], F32, name="zero_bias")
         gain_rows = keep.tile([P, P], F32, name="gain_rows")
         identity = keep.tile([P, P], F32, name="identity")
-        nc.vector.memset(tab_sc[32:64, :].bitcast(I32), 0)
-        nc.vector.memset(tab_sc[64:P, :].bitcast(I32), 0)
         nc.vector.memset(zero[:], 0.0)
         nc.vector.memset(w2_sc_raw[:].rearrange("p a c -> p (a c)").bitcast(I32), 0)
+        nc.vector.memset(tab_sc[32:64, :].bitcast(I32), 0)
+        nc.vector.memset(tab_sc[64:P, :].bitcast(I32), 0)
         for a in range(2):
             nc.vector.memset(v_sc[a][:].bitcast(I32), 0)
         nc.vector.memset(w3_sc[:].rearrange("p a c -> p (a c)").bitcast(I32), 0)
         nc.vector.memset(gain_rows[:], 0.0)
-        make_identity(nc, identity[:])
         nc.scalar.activation(out=zero_bias[:], in_=zero[:], func=SIN)
 
-        def load_scale_rows(tile, dram, r):
-            nc.sync.dma_start(
+        def load_scale_rows(queue, tile, dram, r):
+            queue.dma_start(
                 out=tile[r:P:32, :, :].bitcast(I32), in_=dram[:, r:16:4, :].rearrange("a q c -> q a c").bitcast(I32)
             )
 
@@ -103,7 +101,6 @@ def tile_list_place_context_kernel(
         w2_raw = keep.tile([P, 2, 2 * H], U8, name="w2_raw", align_bytes=64)
         w2_codes = placed([P, 2 * 2 * H], U8, "w2_codes", 38)
         w2_sc = keep.tile([P, 2 * H], U8, name="w2_sc", align_bytes=64)
-        w1_bf0 = placed([P, PASS * PACK], BF16, "w1_bf0", 32)
 
         def load_plane(t):
             nc.sync.dma_start(out=page[t][:], in_=base_rows[t])
@@ -120,7 +117,7 @@ def tile_list_place_context_kernel(
             nc.vector.tensor_copy(v_codes[a][:], tab[a][:].bitcast(U32).indirect(idx[:]))
 
         def move_scale_rows(a, r):
-            nc.sync.dma_start(
+            nc.gpsimd.dma_start(
                 out=v_sc[a][r:P:32, :].bitcast(I32), in_=picked_sc[16 * a + r : 16 * a + 16 : 4, :].bitcast(I32)
             )
 
@@ -129,17 +126,12 @@ def tile_list_place_context_kernel(
                 slot = page_pairs[h][:].rearrange("p (s c e) -> p s c e", s=2, e=2)[:, t // 2, :, t % 2]
                 copy(slot, page[t][:, h * BANK : (h + 1) * BANK])
 
-        def load_w1(u):
-            raw = keep.tile([P, PACK, QUARTER], F32, name="w1_raw%d" % u)
+        def load_w1(b):
+            raw = keep.tile([P, PACK, PASS], F32, name="w1_raw%d" % b)
             nc.sync.dma_start(
-                out=raw[:], in_=w1[:, u * QUARTER : (u + 1) * QUARTER].rearrange("(p j) r -> p j r", j=PACK)
+                out=raw[:], in_=w1[:, b * PASS : (b + 1) * PASS].rearrange("(p j) r -> p j r", j=PACK)
             )
             return raw
-
-        def round_w1(raw, u):
-            dealt = w1_bf0[:].rearrange("p (t g e j) -> p g t e j", t=PACK, e=RUN, j=PACK)[:, RUN * u : RUN * (u + 1)]
-            rows = raw[:].rearrange("p j (g t e) -> p g t e j", t=PACK, e=RUN)
-            nc.gpsimd.tensor_scalar(dealt, rows, 1.0, 0.0, MULT, ADD)
 
         page_pairs = [keep.tile([P, PACK * BANK], BF16, name="page_pairs%d" % h, align_bytes=64) for h in range(2)]
         for t in order[0:2]:
@@ -149,7 +141,7 @@ def tile_list_place_context_kernel(
         load_table(0)
         pick_words(0)
         for q in range(4):
-            load_scale_rows(w2_sc_raw, w2_scales, q)
+            load_scale_rows(nc.gpsimd, w2_sc_raw, w2_scales, q)
         nc.sync.dma_start(out=w2_raw[:].bitcast(I32), in_=w2_words.rearrange("a p c -> p a c").bitcast(I32))
         nc.scalar.copy(
             w2_codes[:].bitcast(U32).rearrange("p (b t g e) -> p b t g e", t=PACK, g=16, e=4),
@@ -174,15 +166,11 @@ def tile_list_place_context_kernel(
         move_scale_rows(1, 1)
         nc.sync.dma_start(out=fresh[3][:], in_=xs_rows[3])
         place(3)
-        w1_raw = [load_w1(0)]
         for q in range(2, 4):
             move_scale_rows(1, q)
-        w1_raw.append(load_w1(1))
-        for u in range(2):
-            round_w1(w1_raw[u], u)
-        w1_late = keep.tile([P, PACK, PASS], F32, name="w1_late")
-        nc.sync.dma_start(out=w1_late[:], in_=w1[:, PASS:H].rearrange("(p j) r -> p j r", j=PACK))
+        w1_raw = [load_w1(b) for b in range(2)]
 
+        make_identity(nc, identity[:])
         b_acc = [bank_tile("b%d" % i, i % B_BANKS) for i in range(TILES)]
         b_rows = [placed([P, J], F32, "b_rows%d" % i, 44 + 2 * i) for i in range(TILES)]
 
@@ -231,13 +219,31 @@ def tile_list_place_context_kernel(
         w3_codes = keep.tile([P, 2, N], I32, name="w3_codes", align_bytes=64)
         nc.sync.dma_start(out=w3_codes[:], in_=w3_words.rearrange("a p c i -> p a (c i)").bitcast(I32))
         for q in range(4):
-            load_scale_rows(w3_sc, w3_scales, q)
+            load_scale_rows(nc.sync, w3_sc, w3_scales, q)
         wo_raw1 = load_wo(1)
 
-        w1_codes0 = keep.tile([P, PASS], U32, name="w1_codes0", tag="fresh3", align_bytes=64)
-        w1_sc0 = keep.tile([P, PASS], U8, name="w1_sc0", align_bytes=64)
-        quantize((w1_codes0[:], w1_sc0[:]), w1_bf0[:])
+        w1_q = []
+
+        def round_w1(copy, dealt, u):
+            rows = w1_raw[u // 2][:].rearrange("p j (g t c i) -> p t g c j i", t=PACK, c=2, i=4)
+            for k in range(2):
+                copy(
+                    dealt[:, k * PASS : (k + 1) * PASS].rearrange("p (g c i j) -> p g c j i", c=2, i=4, j=PACK),
+                    rows[:, 2 * (u % 2) + k],
+                )
+
+        def quantize_w1(u, codes):
+            scales = keep.tile([P, 2 * P], U8, name="w1_scales%d" % u, align_bytes=64)
+            quantize((codes[:], scales[:]), w1_bf[u][:])
+            w1_q.extend((codes[:, t * P : (t + 1) * P], scales[:, t * P : (t + 1) * P]) for t in range(2))
+
         round_plane(nc.vector.tensor_copy, 3)
+        w1_bf = [
+            keep.tile([P, 2 * PASS], BF16, name="w1_bf0", tag="fresh3", align_bytes=64),
+            placed([P, 2 * PASS], BF16, "w1_bf1", 37),
+            placed([P, 2 * PASS], BF16, "w1_bf2", 41.5),
+        ]
+        round_w1(nc.vector.tensor_copy, w1_bf[0], 0)
         page_q = [
             (keep.tile([P, BANK], U32, name="page%d_codes" % h, align_bytes=64)[:], placed([P, BANK], U8, "page%d_scales" % h, 40 + h)[:])
             for h in range(2)
@@ -248,22 +254,15 @@ def tile_list_place_context_kernel(
                 out=grouped[h][:].bitcast(I32).rearrange("p (c i s) -> p c s i", i=4, s=2),
                 in_=page_pairs[h][:].bitcast(I32).rearrange("p (s c i) -> p c s i", i=4, s=2),
             )
+        quantize_w1(0, keep.tile([P, 2 * P], U32, name="w1_codes0", align_bytes=64))
         for h in range(2):
             quantize(page_q[h], grouped[h][:])
-        w1_q = [(w1_codes0[:, t * P : (t + 1) * P], w1_sc0[:, t * P : (t + 1) * P]) for t in range(PACK)]
-        late_rows = w1_late[:].rearrange("p j (g t e) -> p t g j e", t=PACK, e=RUN)
-        late_bf = []
-        for u in range(2):
-            dealt = placed([P, 2 * PASS], BF16, "w1_bf1_%d" % u, (37, 41.5)[u])
-            nc.scalar.copy(dealt[:].rearrange("p (t g e j) -> p t g j e", t=2, e=RUN, j=PACK), late_rows[:, 2 * u : 2 * u + 2])
-            late_bf.append(dealt)
-
-        def quantize_late(u, codes):
-            scales = keep.tile([P, 2 * P], U8, name="w1_1_%d_scales" % u, align_bytes=64)
-            quantize((codes[:], scales[:]), late_bf[u][:])
-            w1_q.extend((codes[:, t * P : (t + 1) * P], scales[:, t * P : (t + 1) * P]) for t in range(2))
-
-        quantize_late(0, keep.tile([P, 2 * P], U32, name="w1_1_0_codes", align_bytes=64))
+        w1_bf.append(keep.tile([P, 2 * PASS], BF16, name="w1_bf3", tag="grouped0", align_bytes=64))
+        for u in range(1, 3):
+            round_w1(nc.scalar.copy, w1_bf[u], u)
+        round_w1(nc.vector.tensor_copy, w1_bf[3], 3)
+        for u in range(1, 3):
+            quantize_w1(u, keep.tile([P, 2 * P], U32, name="w1_codes%d" % u, align_bytes=64))
 
         a_rows = [keep.tile([P, T2], F32, name="a_rows%d" % i) for i in range(TILES)]
 
@@ -300,22 +299,15 @@ def tile_list_place_context_kernel(
                 bias=zero_bias[:],
             )
 
-        def weigh(b, j0, j1, cut):
+        def weigh(b, j0, j1):
             width = j1 - j0
             weighed = keep.tile([P, width * PACK], BF16, name="h_bf%d_%d" % (b, j0), align_bytes=64)
             nc.vector.tensor_tensor(
-                weighed[:, 0 : cut * PACK].rearrange("p (c i t) -> p c t i", i=4, t=PACK),
-                sines[b][:, :, j0 : j0 + cut].rearrange("p t (c i) -> p c t i", i=4),
-                turned[:, PACK * b : PACK * (b + 1)].unsqueeze(1).unsqueeze(3).to_broadcast([P, cut // 4, PACK, 4]),
+                weighed[:].rearrange("p (c i t) -> p c t i", i=4, t=PACK),
+                sines[b][:, :, j0:j1].rearrange("p t (c i) -> p c t i", i=4),
+                gains[:, PACK * b : PACK * (b + 1)].unsqueeze(1).unsqueeze(3).to_broadcast([P, width // 4, PACK, 4]),
                 MULT,
             )
-            if cut < width:
-                nc.gpsimd.tensor_tensor(
-                    weighed[:, cut * PACK :].rearrange("p (j t) -> p j t", t=PACK),
-                    sines[b][:, :, j0 + cut : j1].rearrange("p t j -> p j t"),
-                    gains[:, PACK * b : PACK * (b + 1)].unsqueeze(1).to_broadcast([P, width - cut, PACK]),
-                    MULT,
-                )
             return weighed
 
         def quantize_h(name, weighed, width):
@@ -330,24 +322,23 @@ def tile_list_place_context_kernel(
         nc.tensor.transpose(turned[:, 0:P], gain_rows[:], identity[:])
         gains = keep.tile([P, TILES], F32, name="gains")
         nc.scalar.copy(gains[:], turned[:, 0:TILES])
-        quantize_late(1, placed([P, 2 * P], U32, "w1_1_1_codes", 48))
+        quantize_w1(3, placed([P, 2 * P], U32, "w1_codes3", 48))
         wo_q = [mx_tiles("wo%d" % b, N) for b in range(2)]
         sine(args[0][:], 0, 0, J)
         project_page(4)
         gather_whole(4)
         sine(args[1][:], 2, 0, J)
-        h0_bf = weigh(0, 0, J, J)
-        wo_bf = [placed([P, N * PACK], BF16, "wo_bf0", 50), keep.tile([P, N * PACK], BF16, name="wo_bf1", align_bytes=64)]
-        nc.gpsimd.tensor_scalar(
-            wo_bf[0][:].rearrange("p (n t) -> p n t", t=PACK), wo_raw0[:].rearrange("p t n -> p n t"), 1.0, 0.0, MULT, ADD
-        )
+        wo_bf = [placed([P, N * PACK], BF16, "wo_bf0", 44), placed([P, N * PACK], BF16, "wo_bf1", 50)]
+        round_wo(nc.vector.tensor_copy, wo_bf[0], wo_raw0, 0)
+        h0_bf = weigh(0, 0, J)
         for i in range(5, TILES):
             project_page(i)
         gather_whole(5)
         h0 = quantize_h("h0", h0_bf, J)
+        round_wo(nc.scalar.copy, wo_bf[0], wo_raw0, 1)
+        sine(args[2][:], PACK, 0, J)
         quantize(wo_q[0], wo_bf[0][:])
         round_wo(nc.scalar.copy, wo_bf[1], wo_raw1, 0)
-        sine(args[2][:], PACK, 0, J)
         for u in range(2):
             for k in range(2):
                 first = u * J + k * HALF
@@ -361,7 +352,7 @@ def tile_list_place_context_kernel(
         d_rows = [d_first[:]] + [d_later[:, k] for k in range(3)]
 
         def modulation(u, pair):
-            acc = bank_tile("d%d_%d" % (u, pair), 4 + (2 * u + pair) % 3)
+            acc = bank_tile("d%d_%d" % (u, pair), 4 + 2 * u + pair)
             cols = slice(u * HALF, (u + 1) * HALF)
             for k in range(2):
                 nt = 2 * pair + k
@@ -417,11 +408,11 @@ def tile_list_place_context_kernel(
             rounded = wo_bf[1][:, pair * HALF * PACK : (pair + 1) * HALF * PACK]
             quantize((wo_q[1][0][:, cols], wo_q[1][1][:, cols]), rounded)
 
-        first_half = weigh(1, 0, HALF, SHARE)
+        first_half = weigh(1, 0, HALF)
         quantize_wo(0)
         h1 = quantize_h("h1_0", first_half, HALF)
         y_passes(y_acc[0][0], 0, 1, h1, slice(0, HALF))
-        second_half = weigh(1, HALF, J, SHARE)
+        second_half = weigh(1, HALF, J)
         quantize_wo(1)
         y_passes(y_acc[0][1], 1, 1, h1, slice(0, HALF))
         finish(0, 0)

@@ -28,7 +28,8 @@ TILES = H // P
 HALF = J // 2
 QUARTER = H // 4
 KIB = 1024
-B_BANKS = 3
+ASIDE = 384
+A_BANKS = 4
 
 
 def tile_list_place_context_kernel(
@@ -93,8 +94,7 @@ def tile_list_place_context_kernel(
 
         base_rows = base.rearrange("(p t) c -> t p c", t=PACK)
         xs_rows = xs.rearrange("(p t) c -> t p c", t=PACK)
-        order = (2, 0, 1, 3)
-        page = [placed([P, T2], F32, "page%d" % t, 16 + 4 * order.index(t)) for t in range(PACK)]
+        page = [placed([P, T2], F32, "page%d" % t, 20 + 4 * t) for t in range(PACK)]
         fresh = [keep.tile([P, S], F32, name="fresh%d" % t, tag="fresh%d" % t, align_bytes=64) for t in range(PACK)]
         tab = [placed([P, T], I32, "tab%d" % a, 8 * a) for a in range(2)]
         v_codes = []
@@ -113,7 +113,7 @@ def tile_list_place_context_kernel(
             nc.sync.dma_start(out=tab[a][:], in_=tab_words[a].rearrange("p t i -> p (t i)").bitcast(I32))
 
         def pick_words(a):
-            v_codes.append(placed([P, J], U32, "v_codes%d" % a, (60, 16)[a]))
+            v_codes.append(placed([P, J], U32, "v_codes%d" % a, 16 + 2 * a))
             nc.vector.tensor_copy(v_codes[a][:], tab[a][:].bitcast(U32).indirect(idx[:]))
 
         def move_scale_rows(a, r):
@@ -127,21 +127,25 @@ def tile_list_place_context_kernel(
                 copy(slot, page[t][:, h * BANK : (h + 1) * BANK])
 
         def load_w1(b):
-            raw = keep.tile([P, PACK, PASS], F32, name="w1_raw%d" % b)
+            raw = placed([P, PACK, PASS], F32, "w1_raw%d" % b, 64 + 8 * b)
             nc.sync.dma_start(
                 out=raw[:], in_=w1[:, b * PASS : (b + 1) * PASS].rearrange("(p j) r -> p j r", j=PACK)
             )
             return raw
 
         page_pairs = [keep.tile([P, PACK * BANK], BF16, name="page_pairs%d" % h, align_bytes=64) for h in range(2)]
-        for t in order[0:2]:
+        for r in range(4):
+            load_scale_rows(nc.gpsimd, w2_sc_raw, w2_scales, r)
+        for a in range(2):
+            for r in range(4):
+                move_scale_rows(a, r)
+        make_identity(nc, identity[:])
+        for t in range(2):
             load_plane(t)
             place(t)
             round_plane(nc.scalar.copy, t)
         load_table(0)
         pick_words(0)
-        for q in range(4):
-            load_scale_rows(nc.gpsimd, w2_sc_raw, w2_scales, q)
         nc.sync.dma_start(out=w2_raw[:].bitcast(I32), in_=w2_words.rearrange("a p c -> p a c").bitcast(I32))
         nc.scalar.copy(
             w2_codes[:].bitcast(U32).rearrange("p (b t g e) -> p b t g e", t=PACK, g=16, e=4),
@@ -151,28 +155,29 @@ def tile_list_place_context_kernel(
             w2_sc[:].bitcast(U32).rearrange("p (b t g e) -> p b t g e", t=PACK, g=16, e=2),
             w2_sc_raw[:].rearrange("p a c -> p (a c)").bitcast(U32).rearrange("p (b g t e) -> p b t g e", t=PACK, g=16, e=2),
         )
-        nc.sync.dma_start(out=page[1][:], in_=base_rows[1])
-        move_scale_rows(0, 0)
-        nc.sync.dma_start(out=fresh[1][:], in_=xs_rows[1])
-        place(1)
-        round_plane(nc.scalar.copy, 1)
-        move_scale_rows(0, 1)
+        for t in range(2, PACK):
+            load_plane(t)
+            place(t)
+            round_plane(nc.scalar.copy, t)
+        w1_raw = [load_w1(0)]
         load_table(1)
         pick_words(1)
-        for q in range(2, 4):
-            move_scale_rows(0, q)
-        move_scale_rows(1, 0)
-        nc.sync.dma_start(out=page[3][:], in_=base_rows[3])
-        move_scale_rows(1, 1)
-        nc.sync.dma_start(out=fresh[3][:], in_=xs_rows[3])
-        place(3)
-        for q in range(2, 4):
-            move_scale_rows(1, q)
-        w1_raw = [load_w1(b) for b in range(2)]
+        w1_raw.append(load_w1(1))
 
-        make_identity(nc, identity[:])
-        b_acc = [bank_tile("b%d" % i, i % B_BANKS) for i in range(TILES)]
-        b_rows = [placed([P, J], F32, "b_rows%d" % i, 44 + 2 * i) for i in range(TILES)]
+        def round_w1_aside(dealt, b, t0, t1):
+            nc.gpsimd.tensor_scalar(
+                dealt[:].rearrange("p (t g e j) -> p g t e j", t=t1 - t0, e=RUN, j=PACK),
+                w1_raw[b][:].rearrange("p j (g t e) -> p g t e j", t=PACK, e=RUN)[:, :, t0:t1],
+                1.0,
+                0.0,
+                MULT,
+                ADD,
+            )
+
+        w1_early = placed([P, PACK * PASS], BF16, "w1_early", 56)
+        round_w1_aside(w1_early, 0, 0, PACK)
+        b_acc = [bank_tile("b%d" % i, i) for i in range(TILES)]
+        b_rows = [placed([P, J], F32, "b_rows%d" % i, 44 + 2 * i) for i in range(6)]
 
         def object_pass(i, a):
             col = a * H + i * P
@@ -185,15 +190,15 @@ def tile_list_place_context_kernel(
                 start=(a == 0),
                 stop=(a == 1),
             )
-            if a == 1:
-                nc.scalar.copy(b_rows[i][:], b_acc[i][:])
+
+        def stage(copy, i):
+            copy(b_rows[i][:], b_acc[i][:])
 
         for a in range(2):
-            for i in range(B_BANKS):
+            for i in range(TILES):
                 object_pass(i, a)
-        for i in range(B_BANKS, TILES):
-            for a in range(2):
-                object_pass(i, a)
+        for i in range(PACK):
+            stage(nc.scalar.copy, i)
 
         def load_wo(b):
             raw = keep.tile([P, PACK, N], F32, name="wo_raw%d" % b, tag="wo_raw%d" % b)
@@ -202,11 +207,10 @@ def tile_list_place_context_kernel(
                 nc.sync.dma_start(out=raw[:, t, :], in_=rows[t])
             return raw
 
-        def round_wo(copy, grouped, raw, u):
-            cols = slice(u * HALF, (u + 1) * HALF)
-            copy(
-                grouped[:].rearrange("p (c i t) -> p c t i", i=4, t=PACK)[:, u * HALF // 4 : (u + 1) * HALF // 4],
-                raw[:, :, cols].rearrange("p t (c i) -> p c t i", i=4),
+        def round_wo(grouped, raw, n0, n1):
+            nc.scalar.copy(
+                grouped[:].rearrange("p (c i t) -> p c t i", i=4, t=PACK)[:, n0 // 4 : n1 // 4],
+                raw[:, :, n0:n1].rearrange("p t (c i) -> p c t i", i=4),
             )
 
         nc.sync.dma_start(idx3[:], offs3)
@@ -222,53 +226,39 @@ def tile_list_place_context_kernel(
             load_scale_rows(nc.sync, w3_sc, w3_scales, q)
         wo_raw1 = load_wo(1)
 
-        w1_q = []
+        w1_codes = keep.tile([P, PASS], U32, name="w1_codes", tag="fresh3", align_bytes=64)
+        w1_scales = keep.tile([P, PASS], U8, name="w1_scales", align_bytes=64)
+        quantize((w1_codes[:], w1_scales[:]), w1_early[:])
+        w1_q = [(w1_codes[:, t * P : (t + 1) * P], w1_scales[:, t * P : (t + 1) * P]) for t in range(PACK)]
 
-        def round_w1(copy, dealt, u):
-            rows = w1_raw[u // 2][:].rearrange("p j (g t c i) -> p t g c j i", t=PACK, c=2, i=4)
-            for k in range(2):
-                copy(
-                    dealt[:, k * PASS : (k + 1) * PASS].rearrange("p (g c i j) -> p g c j i", c=2, i=4, j=PACK),
-                    rows[:, 2 * (u % 2) + k],
-                )
-
-        def quantize_w1(u, codes):
+        def quantize_w1(u):
+            codes = keep.tile([P, 2 * P], U32, name="w1_codes%d" % u, align_bytes=64)
             scales = keep.tile([P, 2 * P], U8, name="w1_scales%d" % u, align_bytes=64)
-            quantize((codes[:], scales[:]), w1_bf[u][:])
+            quantize((codes[:], scales[:]), w1_late[u][:])
             w1_q.extend((codes[:, t * P : (t + 1) * P], scales[:, t * P : (t + 1) * P]) for t in range(2))
 
-        round_plane(nc.vector.tensor_copy, 3)
-        w1_bf = [
-            keep.tile([P, 2 * PASS], BF16, name="w1_bf0", tag="fresh3", align_bytes=64),
-            placed([P, 2 * PASS], BF16, "w1_bf1", 37),
-            placed([P, 2 * PASS], BF16, "w1_bf2", 41.5),
-        ]
-        round_w1(nc.vector.tensor_copy, w1_bf[0], 0)
         page_q = [
-            (keep.tile([P, BANK], U32, name="page%d_codes" % h, align_bytes=64)[:], placed([P, BANK], U8, "page%d_scales" % h, 40 + h)[:])
-            for h in range(2)
+            mx_tiles("page0", BANK),
+            (placed([P, BANK], U32, "page1_codes", 56)[:], keep.tile([P, BANK], U8, name="page1_scales", align_bytes=64)[:]),
         ]
-        grouped = [keep.tile([P, PACK * BANK], BF16, name="page_grouped%d" % h, tag="grouped%d" % h, align_bytes=64) for h in range(2)]
+        grouped = [placed([P, PACK * BANK], BF16, "page_grouped%d" % h, 8 + 4 * h) for h in range(2)]
         for h in range(2):
             nc.vector.tensor_copy(
                 out=grouped[h][:].bitcast(I32).rearrange("p (c i s) -> p c s i", i=4, s=2),
                 in_=page_pairs[h][:].bitcast(I32).rearrange("p (s c i) -> p c s i", i=4, s=2),
             )
-        quantize_w1(0, keep.tile([P, 2 * P], U32, name="w1_codes0", align_bytes=64))
         for h in range(2):
             quantize(page_q[h], grouped[h][:])
-        w1_bf.append(keep.tile([P, 2 * PASS], BF16, name="w1_bf3", tag="grouped0", align_bytes=64))
-        for u in range(1, 3):
-            round_w1(nc.scalar.copy, w1_bf[u], u)
-        round_w1(nc.vector.tensor_copy, w1_bf[3], 3)
-        for u in range(1, 3):
-            quantize_w1(u, keep.tile([P, 2 * P], U32, name="w1_codes%d" % u, align_bytes=64))
+        for i in range(PACK, 6):
+            stage(nc.vector.tensor_copy, i)
+        w1_late = [placed([P, 2 * PASS], BF16, "w1_late0", 12), placed([P, 2 * PASS], BF16, "w1_late1", 50)]
+        round_w1_aside(w1_late[0], 1, 0, 2)
 
-        a_rows = [keep.tile([P, T2], F32, name="a_rows%d" % i) for i in range(TILES)]
+        a_rows = [placed([P, T2], F32, "a_rows%d" % i, 80 + 4 * i) for i in range(TILES)]
 
         def project_page(i):
             for h in range(2):
-                acc = bank_tile("a%d_%d" % (i, h), (2 - i % 2, (0, 7, 3, 4, 5, 6, 0, 3)[i])[h])
+                acc = bank_tile("a%d_%d" % (i, h), (2 * i + h) % A_BANKS)
                 nc.tensor.matmul_mx(
                     out=acc[:],
                     lhsT=w1_q[i][0].bitcast(FP8X4),
@@ -278,13 +268,12 @@ def tile_list_place_context_kernel(
                     start=True,
                     stop=True,
                 )
-                copy = nc.vector.tensor_copy if (i, h) == (0, 1) else nc.scalar.copy
-                copy(a_rows[i][:, h * BANK : (h + 1) * BANK], acc[:])
+                nc.scalar.copy(a_rows[i][:, h * BANK : (h + 1) * BANK], acc[:])
 
         def gather(arg, i, j0, j1):
             nc.vector.tensor_tensor(arg, a_rows[i][:].indirect(idx3[:, j0 // 16 : j1 // 16]), b_rows[i][:, j0:j1], ADD)
 
-        args = [placed([P, 2 * J], F32, "arg%d" % pair, 4 * pair) for pair in range(PACK)]
+        args = [placed([P, 2 * J], F32, "arg%d" % pair, (0, 4, 8, 36)[pair]) for pair in range(PACK)]
         sines = [placed([P, PACK, J], F32, "sines%d" % b, 20 + 8 * b) for b in range(2)]
 
         def gather_whole(i):
@@ -305,7 +294,7 @@ def tile_list_place_context_kernel(
             nc.vector.tensor_tensor(
                 weighed[:].rearrange("p (c i t) -> p c t i", i=4, t=PACK),
                 sines[b][:, :, j0:j1].rearrange("p t (c i) -> p c t i", i=4),
-                gains[:, PACK * b : PACK * (b + 1)].unsqueeze(1).unsqueeze(3).to_broadcast([P, width // 4, PACK, 4]),
+                turned[:, PACK * b : PACK * (b + 1)].unsqueeze(1).unsqueeze(3).to_broadcast([P, width // 4, PACK, 4]),
                 MULT,
             )
             return weighed
@@ -317,34 +306,50 @@ def tile_list_place_context_kernel(
 
         for i in range(PACK):
             project_page(i)
+            if i == 0:
+                quantize_w1(0)
             gather_whole(i)
-        turned = bank_tile("turned", 7)
+        rows = w1_raw[1][:].rearrange("p j (g t c i) -> p t g c j i", t=PACK, c=2, i=4)
+        for k in range(2):
+            nc.vector.tensor_copy(
+                w1_late[1][:, k * PASS : (k + 1) * PASS].rearrange("p (g c i j) -> p g c j i", c=2, i=4, j=PACK),
+                rows[:, 2 + k],
+            )
+        quantize_w1(1)
+        turned = bank_tile("turned", PACK)
         nc.tensor.transpose(turned[:, 0:P], gain_rows[:], identity[:])
-        gains = keep.tile([P, TILES], F32, name="gains")
-        nc.scalar.copy(gains[:], turned[:, 0:TILES])
-        quantize_w1(3, placed([P, 2 * P], U32, "w1_codes3", 48))
         wo_q = [mx_tiles("wo%d" % b, N) for b in range(2)]
         sine(args[0][:], 0, 0, J)
         project_page(4)
         gather_whole(4)
         sine(args[1][:], 2, 0, J)
-        wo_bf = [placed([P, N * PACK], BF16, "wo_bf0", 44), placed([P, N * PACK], BF16, "wo_bf1", 50)]
-        round_wo(nc.vector.tensor_copy, wo_bf[0], wo_raw0, 0)
+        wo_bf = [placed([P, N * PACK], BF16, "wo_bf0", 50), placed([P, N * PACK], BF16, "wo_bf1", 92)]
         h0_bf = weigh(0, 0, J)
+        nc.gpsimd.tensor_scalar(
+            wo_bf[0][:].rearrange("p (n t) -> p n t", t=PACK)[:, 0:ASIDE],
+            wo_raw0[:].rearrange("p t n -> p n t")[:, 0:ASIDE],
+            1.0,
+            0.0,
+            MULT,
+            ADD,
+        )
         for i in range(5, TILES):
             project_page(i)
+            if i > 5:
+                b_rows.append(placed([P, J], F32, "b_rows%d" % i, 4 + 2 * (i - 6)))
+                stage(nc.scalar.copy, i)
         gather_whole(5)
         h0 = quantize_h("h0", h0_bf, J)
-        round_wo(nc.scalar.copy, wo_bf[0], wo_raw0, 1)
+        round_wo(wo_bf[0], wo_raw0, ASIDE, N)
         sine(args[2][:], PACK, 0, J)
         quantize(wo_q[0], wo_bf[0][:])
-        round_wo(nc.scalar.copy, wo_bf[1], wo_raw1, 0)
+        round_wo(wo_bf[1], wo_raw1, 0, HALF)
         for u in range(2):
             for k in range(2):
                 first = u * J + k * HALF
                 gather(args[3][:, first : first + HALF], 6 + k, u * HALF, (u + 1) * HALF)
         sine(args[3][:, 0:J], 6, 0, HALF)
-        round_wo(nc.scalar.copy, wo_bf[1], wo_raw1, 1)
+        round_wo(wo_bf[1], wo_raw1, HALF, N)
         sine(args[3][:, J : 2 * J], 6, HALF, J)
 
         d_first = placed([P, 2, HALF], F32, "d_first", 54)
@@ -352,7 +357,7 @@ def tile_list_place_context_kernel(
         d_rows = [d_first[:]] + [d_later[:, k] for k in range(3)]
 
         def modulation(u, pair):
-            acc = bank_tile("d%d_%d" % (u, pair), 4 + 2 * u + pair)
+            acc = bank_tile("d%d_%d" % (u, pair), 5 + (2 * u + pair) % 3)
             cols = slice(u * HALF, (u + 1) * HALF)
             for k in range(2):
                 nt = 2 * pair + k

@@ -79,8 +79,8 @@ def tile_list_place_context_kernel(
         nc.vector.memset(gain_rows[:], 0.0)
         nc.scalar.activation(out=zero_bias[:], in_=zero[:], func=SIN)
 
-        def load_scale_rows(queue, tile, dram, r):
-            queue.dma_start(
+        def load_scale_rows(tile, dram, r):
+            nc.sync.dma_start(
                 out=tile[r:P:32, :, :].bitcast(I32), in_=dram[:, r:16:4, :].rearrange("a q c -> q a c").bitcast(I32)
             )
 
@@ -134,8 +134,6 @@ def tile_list_place_context_kernel(
             return raw
 
         page_pairs = [keep.tile([P, PACK * BANK], BF16, name="page_pairs%d" % h, align_bytes=64) for h in range(2)]
-        for r in range(4):
-            load_scale_rows(nc.gpsimd, w2_sc_raw, w2_scales, r)
         for a in range(2):
             for r in range(4):
                 move_scale_rows(a, r)
@@ -144,6 +142,8 @@ def tile_list_place_context_kernel(
             load_plane(t)
             place(t)
             round_plane(nc.scalar.copy, t)
+        for r in range(4):
+            load_scale_rows(w2_sc_raw, w2_scales, r)
         load_table(0)
         pick_words(0)
         nc.sync.dma_start(out=w2_raw[:].bitcast(I32), in_=w2_words.rearrange("a p c -> p a c").bitcast(I32))
@@ -223,7 +223,7 @@ def tile_list_place_context_kernel(
         w3_codes = keep.tile([P, 2, N], I32, name="w3_codes", align_bytes=64)
         nc.sync.dma_start(out=w3_codes[:], in_=w3_words.rearrange("a p c i -> p a (c i)").bitcast(I32))
         for q in range(4):
-            load_scale_rows(nc.sync, w3_sc, w3_scales, q)
+            load_scale_rows(w3_sc, w3_scales, q)
         wo_raw1 = load_wo(1)
 
         w1_codes = keep.tile([P, PASS], U32, name="w1_codes", tag="fresh3", align_bytes=64)

@@ -30,6 +30,7 @@ QUARTER = H // 4
 KIB = 1024
 ASIDE = 384
 A_BANKS = 4
+EARLY = 6
 
 
 def tile_list_place_context_kernel(
@@ -116,8 +117,8 @@ def tile_list_place_context_kernel(
             v_codes.append(placed([P, J], U32, "v_codes%d" % a, 16 + 2 * a))
             nc.vector.tensor_copy(v_codes[a][:], tab[a][:].bitcast(U32).indirect(idx[:]))
 
-        def move_scale_rows(a, r):
-            nc.gpsimd.dma_start(
+        def move_scale_rows(queue, a, r):
+            queue.dma_start(
                 out=v_sc[a][r:P:32, :].bitcast(I32), in_=picked_sc[16 * a + r : 16 * a + 16 : 4, :].bitcast(I32)
             )
 
@@ -134,9 +135,8 @@ def tile_list_place_context_kernel(
             return raw
 
         page_pairs = [keep.tile([P, PACK * BANK], BF16, name="page_pairs%d" % h, align_bytes=64) for h in range(2)]
-        for a in range(2):
-            for r in range(4):
-                move_scale_rows(a, r)
+        for r in range(4):
+            move_scale_rows(nc.gpsimd, 1, r)
         make_identity(nc, identity[:])
         for t in range(2):
             load_plane(t)
@@ -157,6 +157,8 @@ def tile_list_place_context_kernel(
         )
         for t in range(2, PACK):
             load_plane(t)
+            for r in range(2):
+                move_scale_rows(nc.sync, 0, 2 * (t - 2) + r)
             place(t)
             round_plane(nc.scalar.copy, t)
         w1_raw = [load_w1(0)]
@@ -176,7 +178,7 @@ def tile_list_place_context_kernel(
 
         w1_early = placed([P, PACK * PASS], BF16, "w1_early", 56)
         round_w1_aside(w1_early, 0, 0, PACK)
-        b_acc = [bank_tile("b%d" % i, i) for i in range(TILES)]
+        b_acc = [bank_tile("b%d" % i, i) for i in range(EARLY)]
         b_rows = [placed([P, J], F32, "b_rows%d" % i, 44 + 2 * i) for i in range(6)]
 
         def object_pass(i, a):
@@ -195,7 +197,7 @@ def tile_list_place_context_kernel(
             copy(b_rows[i][:], b_acc[i][:])
 
         for a in range(2):
-            for i in range(TILES):
+            for i in range(EARLY):
                 object_pass(i, a)
         for i in range(PACK):
             stage(nc.scalar.copy, i)
@@ -231,8 +233,7 @@ def tile_list_place_context_kernel(
         quantize((w1_codes[:], w1_scales[:]), w1_early[:])
         w1_q = [(w1_codes[:, t * P : (t + 1) * P], w1_scales[:, t * P : (t + 1) * P]) for t in range(PACK)]
 
-        def quantize_w1(u):
-            codes = keep.tile([P, 2 * P], U32, name="w1_codes%d" % u, align_bytes=64)
+        def quantize_w1(u, codes):
             scales = keep.tile([P, 2 * P], U8, name="w1_scales%d" % u, align_bytes=64)
             quantize((codes[:], scales[:]), w1_late[u][:])
             w1_q.extend((codes[:, t * P : (t + 1) * P], scales[:, t * P : (t + 1) * P]) for t in range(2))
@@ -251,14 +252,14 @@ def tile_list_place_context_kernel(
             quantize(page_q[h], grouped[h][:])
         for i in range(PACK, 6):
             stage(nc.vector.tensor_copy, i)
-        w1_late = [placed([P, 2 * PASS], BF16, "w1_late0", 12), placed([P, 2 * PASS], BF16, "w1_late1", 50)]
+        w1_late = [placed([P, 2 * PASS], BF16, "w1_late0", 12), keep.tile([P, 2 * PASS], BF16, name="w1_late1", tag="fresh3", align_bytes=64)]
         round_w1_aside(w1_late[0], 1, 0, 2)
 
         a_rows = [placed([P, T2], F32, "a_rows%d" % i, 80 + 4 * i) for i in range(TILES)]
 
         def project_page(i):
             for h in range(2):
-                acc = bank_tile("a%d_%d" % (i, h), (2 * i + h) % A_BANKS)
+                acc = bank_tile("a%d_%d" % (i, h), (2 * i + h - 2) % A_BANKS if i else EARLY + h)
                 nc.tensor.matmul_mx(
                     out=acc[:],
                     lhsT=w1_q[i][0].bitcast(FP8X4),
@@ -307,21 +308,23 @@ def tile_list_place_context_kernel(
         for i in range(PACK):
             project_page(i)
             if i == 0:
-                quantize_w1(0)
+                quantize_w1(0, keep.tile([P, 2 * P], U32, name="w1_codes0", align_bytes=64))
             gather_whole(i)
-        rows = w1_raw[1][:].rearrange("p j (g t c i) -> p t g c j i", t=PACK, c=2, i=4)
-        for k in range(2):
-            nc.vector.tensor_copy(
-                w1_late[1][:, k * PASS : (k + 1) * PASS].rearrange("p (g c i j) -> p g c j i", c=2, i=4, j=PACK),
-                rows[:, 2 + k],
-            )
-        quantize_w1(1)
+        nc.vector.tensor_copy(
+            w1_late[1][:].rearrange("p (t g e j) -> p t g j e", t=2, e=RUN, j=PACK),
+            w1_raw[1][:].rearrange("p j (g t e) -> p t g j e", t=PACK, e=RUN)[:, 2:PACK],
+        )
         turned = bank_tile("turned", PACK)
         nc.tensor.transpose(turned[:, 0:P], gain_rows[:], identity[:])
         wo_q = [mx_tiles("wo%d" % b, N) for b in range(2)]
         sine(args[0][:], 0, 0, J)
+        quantize_w1(1, placed([P, 2 * P], U32, "w1_codes1", 0))
         project_page(4)
         gather_whole(4)
+        for i in range(EARLY, TILES):
+            b_acc.append(bank_tile("b%d" % i, i))
+            for a in range(2):
+                object_pass(i, a)
         sine(args[1][:], 2, 0, J)
         wo_bf = [placed([P, N * PACK], BF16, "wo_bf0", 50), placed([P, N * PACK], BF16, "wo_bf1", 92)]
         h0_bf = weigh(0, 0, J)
@@ -343,14 +346,14 @@ def tile_list_place_context_kernel(
         round_wo(wo_bf[0], wo_raw0, ASIDE, N)
         sine(args[2][:], PACK, 0, J)
         quantize(wo_q[0], wo_bf[0][:])
-        round_wo(wo_bf[1], wo_raw1, 0, HALF)
         for u in range(2):
             for k in range(2):
                 first = u * J + k * HALF
                 gather(args[3][:, first : first + HALF], 6 + k, u * HALF, (u + 1) * HALF)
         sine(args[3][:, 0:J], 6, 0, HALF)
-        round_wo(wo_bf[1], wo_raw1, HALF, N)
+        round_wo(wo_bf[1], wo_raw1, 0, HALF)
         sine(args[3][:, J : 2 * J], 6, HALF, J)
+        round_wo(wo_bf[1], wo_raw1, HALF, N)
 
         d_first = placed([P, 2, HALF], F32, "d_first", 54)
         d_later = keep.tile([P, 3, 2, HALF], F32, name="d_later", tag="wo_raw1")

@@ -289,13 +289,13 @@ def tile_list_place_context_kernel(
                 bias=zero_bias[:],
             )
 
-        def weigh(b, j0, j1):
+        def weigh(b, j0, j1, gains):
             width = j1 - j0
             weighed = keep.tile([P, width * PACK], BF16, name="h_bf%d_%d" % (b, j0), align_bytes=64)
             nc.vector.tensor_tensor(
                 weighed[:].rearrange("p (c i t) -> p c t i", i=4, t=PACK),
                 sines[b][:, :, j0:j1].rearrange("p t (c i) -> p c t i", i=4),
-                turned[:, PACK * b : PACK * (b + 1)].unsqueeze(1).unsqueeze(3).to_broadcast([P, width // 4, PACK, 4]),
+                gains[:, PACK * b : PACK * (b + 1)].unsqueeze(1).unsqueeze(3).to_broadcast([P, width // 4, PACK, 4]),
                 MULT,
             )
             return weighed
@@ -327,7 +327,7 @@ def tile_list_place_context_kernel(
                 object_pass(i, a)
         sine(args[1][:], 2, 0, J)
         wo_bf = [placed([P, N * PACK], BF16, "wo_bf0", 50), placed([P, N * PACK], BF16, "wo_bf1", 92)]
-        h0_bf = weigh(0, 0, J)
+        h0_bf = weigh(0, 0, J, turned)
         nc.gpsimd.tensor_scalar(
             wo_bf[0][:].rearrange("p (n t) -> p n t", t=PACK)[:, 0:ASIDE],
             wo_raw0[:].rearrange("p t n -> p n t")[:, 0:ASIDE],
@@ -341,6 +341,8 @@ def tile_list_place_context_kernel(
             if i > 5:
                 b_rows.append(placed([P, J], F32, "b_rows%d" % i, 4 + 2 * (i - 6)))
                 stage(nc.scalar.copy, i)
+        gains = placed([P, TILES], F32, "gains", 46)
+        nc.scalar.copy(gains[:], turned[:, 0:TILES])
         gather_whole(5)
         h0 = quantize_h("h0", h0_bf, J)
         round_wo(wo_bf[0], wo_raw0, ASIDE, N)
@@ -360,7 +362,7 @@ def tile_list_place_context_kernel(
         d_rows = [d_first[:]] + [d_later[:, k] for k in range(3)]
 
         def modulation(u, pair):
-            acc = bank_tile("d%d_%d" % (u, pair), 5 + (2 * u + pair) % 3)
+            acc = bank_tile("d%d_%d" % (u, pair), 4 + (2 * u + pair + 1) % 4)
             cols = slice(u * HALF, (u + 1) * HALF)
             for k in range(2):
                 nt = 2 * pair + k
@@ -416,11 +418,11 @@ def tile_list_place_context_kernel(
             rounded = wo_bf[1][:, pair * HALF * PACK : (pair + 1) * HALF * PACK]
             quantize((wo_q[1][0][:, cols], wo_q[1][1][:, cols]), rounded)
 
-        first_half = weigh(1, 0, HALF)
+        first_half = weigh(1, 0, HALF, gains)
         quantize_wo(0)
         h1 = quantize_h("h1_0", first_half, HALF)
         y_passes(y_acc[0][0], 0, 1, h1, slice(0, HALF))
-        second_half = weigh(1, HALF, J)
+        second_half = weigh(1, HALF, J, gains)
         quantize_wo(1)
         y_passes(y_acc[0][1], 1, 1, h1, slice(0, HALF))
         finish(0, 0)

@@ -28,7 +28,7 @@ TILES = H // P
 HALF = J // 2
 QUARTER = H // 4
 KIB = 1024
-ASIDE = 384
+ASIDE = 352
 A_BANKS = 4
 EARLY = 6
 
@@ -229,7 +229,7 @@ def tile_list_place_context_kernel(
         wo_raw1 = load_wo(1)
 
         w1_codes = keep.tile([P, PASS], U32, name="w1_codes", tag="fresh3", align_bytes=64)
-        w1_scales = keep.tile([P, PASS], U8, name="w1_scales", align_bytes=64)
+        w1_scales = placed([P, PASS], U8, "w1_scales", 14)
         quantize((w1_codes[:], w1_scales[:]), w1_early[:])
         w1_q = [(w1_codes[:, t * P : (t + 1) * P], w1_scales[:, t * P : (t + 1) * P]) for t in range(PACK)]
 
@@ -242,7 +242,7 @@ def tile_list_place_context_kernel(
             mx_tiles("page0", BANK),
             (placed([P, BANK], U32, "page1_codes", 56)[:], keep.tile([P, BANK], U8, name="page1_scales", align_bytes=64)[:]),
         ]
-        grouped = [placed([P, PACK * BANK], BF16, "page_grouped%d" % h, 8 + 4 * h) for h in range(2)]
+        grouped = [placed([P, PACK * BANK], BF16, "page_grouped%d" % h, 6 + 4 * h) for h in range(2)]
         for h in range(2):
             nc.vector.tensor_copy(
                 out=grouped[h][:].bitcast(I32).rearrange("p (c i s) -> p c s i", i=4, s=2),
@@ -310,10 +310,12 @@ def tile_list_place_context_kernel(
             if i == 0:
                 quantize_w1(0, keep.tile([P, 2 * P], U32, name="w1_codes0", align_bytes=64))
             gather_whole(i)
-        nc.vector.tensor_copy(
-            w1_late[1][:].rearrange("p (t g e j) -> p t g j e", t=2, e=RUN, j=PACK),
-            w1_raw[1][:].rearrange("p j (g t e) -> p t g j e", t=PACK, e=RUN)[:, 2:PACK],
-        )
+        rows = w1_raw[1][:].rearrange("p j (g t c i) -> p t g c j i", t=PACK, c=2, i=4)
+        for k in range(2):
+            nc.vector.tensor_copy(
+                w1_late[1][:, k * PASS : (k + 1) * PASS].rearrange("p (g c i j) -> p g c j i", c=2, i=4, j=PACK),
+                rows[:, 2 + k],
+            )
         turned = bank_tile("turned", PACK)
         nc.tensor.transpose(turned[:, 0:P], gain_rows[:], identity[:])
         wo_q = [mx_tiles("wo%d" % b, N) for b in range(2)]

@@ -250,10 +250,19 @@ def tile_list_place_context_kernel(
             )
         for h in range(2):
             quantize(page_q[h], grouped[h][:])
-        for i in range(PACK, 6):
-            stage(nc.vector.tensor_copy, i)
+        stage(nc.vector.tensor_copy, PACK)
         w1_late = [placed([P, 2 * PASS], BF16, "w1_late0", 12), keep.tile([P, 2 * PASS], BF16, name="w1_late1", tag="fresh3", align_bytes=64)]
-        round_w1_aside(w1_late[0], 1, 0, 2)
+        late_rows = w1_raw[1][:].rearrange("p j (g t c i) -> p t g c j i", t=PACK, c=2, i=4)
+
+        def round_late(u):
+            for k in range(2):
+                nc.vector.tensor_copy(
+                    w1_late[u][:, k * PASS : (k + 1) * PASS].rearrange("p (g c i j) -> p g c j i", c=2, i=4, j=PACK),
+                    late_rows[:, 2 * u + k],
+                )
+
+        round_late(0)
+        stage(nc.vector.tensor_copy, 5)
 
         a_rows = [placed([P, T2], F32, "a_rows%d" % i, 80 + 4 * i) for i in range(TILES)]
 
@@ -310,12 +319,7 @@ def tile_list_place_context_kernel(
             if i == 0:
                 quantize_w1(0, keep.tile([P, 2 * P], U32, name="w1_codes0", align_bytes=64))
             gather_whole(i)
-        rows = w1_raw[1][:].rearrange("p j (g t c i) -> p t g c j i", t=PACK, c=2, i=4)
-        for k in range(2):
-            nc.vector.tensor_copy(
-                w1_late[1][:, k * PASS : (k + 1) * PASS].rearrange("p (g c i j) -> p g c j i", c=2, i=4, j=PACK),
-                rows[:, 2 + k],
-            )
+        round_late(1)
         turned = bank_tile("turned", PACK)
         nc.tensor.transpose(turned[:, 0:P], gain_rows[:], identity[:])
         wo_q = [mx_tiles("wo%d" % b, N) for b in range(2)]

from contextlib import ExitStack

import concourse.mybir as mybir
from concourse.masks import make_identity

K, K2, H, N, T, T2, S, J = 1024, 512, 1024, 512, 2048, 1024, 512, 512
FLOPS = 2 * (K2 * H * T2 + K * H * J + H * N * J + K * N * J)

F32 = mybir.dt.float32
BF16 = mybir.dt.bfloat16
I32 = mybir.dt.int32
U32 = mybir.dt.uint32
U16 = mybir.dt.uint16
U8 = mybir.dt.uint8
FP8X4 = mybir.dt.float8_e4m3fn_x4
FP4X4 = mybir.dt.float4_e2m1fn_x4
SIN = mybir.ActivationFunctionType.Sin
ADD = mybir.AluOpType.add
MULT = mybir.AluOpType.mult

P = 128
PACK = 4
PASS = P * PACK
RUN = 8
BANK = 512
BANK_BYTES = 4 * BANK
TILES = H // P
HALF = J // 2
QUARTER = H // 4
KIB = 1024
ASIDE = 352
A_BANKS = 4
EARLY = 6


def tile_list_place_context_kernel(
    tc, tab_words, tab_scales, offs, base, xs, offs2, offs3, w1, w2_words, w2_scales, gain, wo, w3_words, w3_scales, out
):
    nc = tc.nc
    with ExitStack() as ctx:
        lists = ctx.enter_context(tc.tile_pool(name="lists", bufs=1))
        keep = ctx.enter_context(tc.tile_pool(name="keep", bufs=1))
        shared = ctx.enter_context(tc.tile_pool(name="shared", bufs=1))
        psum = ctx.enter_context(tc.psum_pool(name="psum", bufs=1))

        def bank_tile(name, bank):
            return psum.tile([P, BANK], F32, name=name, offset=bank * BANK_BYTES)

        def placed(shape, dtype, name, kib):
            return shared.tile(shape, dtype, name=name, offset=int(kib * KIB), align_bytes=64)

        def mx_tiles(name, width):
            codes = keep.tile([P, width], U32, name=name + "_codes", align_bytes=64)
            scales = keep.tile([P, width], U8, name=name + "_scales", align_bytes=64)
            return codes[:], scales[:]

        def quantize(operand, grouped):
            codes, scales = operand
            nc.vector.quantize_mx(out=codes.bitcast(FP8X4), scales=scales, in_=grouped)

        idx = lists.tile([P, J // 16], U16, name="idx")
        idx2 = lists.tile([P, S // 16], U16, name="idx2")
        idx3 = lists.tile([P, J // 16], U16, name="idx3")

        tab_sc = keep.tile([P, T], U8, name="tab_sc", align_bytes=64)
        w2_sc_raw = keep.tile([P, 2, H], U8, name="w2_sc_raw", align_bytes=64)
        w3_sc = keep.tile([P, 2, N], U8, name="w3_sc", align_bytes=64)
        v_sc = [keep.tile([P, J], U8, name="v_sc%d" % a, align_bytes=64) for a in range(2)]
        zero = keep.tile([P, 1], F32, name="zero")
        zero_bias = keep.tile([P, 1], F32, name="zero_bias")
        gain_rows = keep.tile([P, P], F32, name="gain_rows")
        identity = keep.tile([P, P], F32, name="identity")
        nc.vector.memset(zero[:], 0.0)
        nc.vector.memset(w2_sc_raw[:].rearrange("p a c -> p (a c)").bitcast(I32), 0)
        nc.vector.memset(tab_sc[32:64, :].bitcast(I32), 0)
        nc.vector.memset(tab_sc[64:P, :].bitcast(I32), 0)
        for a in range(2):
            nc.vector.memset(v_sc[a][:].bitcast(I32), 0)
        nc.vector.memset(w3_sc[:].rearrange("p a c -> p (a c)").bitcast(I32), 0)
        nc.vector.memset(gain_rows[:], 0.0)
        nc.scalar.activation(out=zero_bias[:], in_=zero[:], func=SIN)

        def load_scale_rows(tile, dram, r):
            nc.sync.dma_start(
                out=tile[r:P:32, :, :].bitcast(I32), in_=dram[:, r:16:4, :].rearrange("a q c -> q a c").bitcast(I32)
            )

        nc.sync.dma_start(
            out=tab_sc[0:32, :].bitcast(I32), in_=tab_scales.rearrange("a g t -> (a g) t").bitcast(I32)
        )
        nc.sync.dma_start(idx[:], offs)
        nc.sync.dma_start(idx2[:], offs2)
        picked_sc = keep.tile([P, J], U8, name="picked_sc", align_bytes=64)
        nc.vector.tensor_copy(picked_sc[:], tab_sc[:].indirect(idx[:]))

        base_rows = base.rearrange("(p t) c -> t p c", t=PACK)
        xs_rows = xs.rearrange("(p t) c -> t p c", t=PACK)
        page = [placed([P, T2], F32, "page%d" % t, 20 + 4 * t) for t in range(PACK)]
        fresh = [keep.tile([P, S], F32, name="fresh%d" % t, tag="fresh%d" % t, align_bytes=64) for t in range(PACK)]
        tab = [placed([P, T], I32, "tab%d" % a, 8 * a) for a in range(2)]
        v_codes = []
        w2_raw = keep.tile([P, 2, 2 * H], U8, name="w2_raw", align_bytes=64)
        w2_codes = placed([P, 2 * 2 * H], U8, "w2_codes", 38)
        w2_sc = keep.tile([P, 2 * H], U8, name="w2_sc", align_bytes=64)

        def load_plane(t):
            nc.sync.dma_start(out=page[t][:], in_=base_rows[t])
            nc.sync.dma_start(out=fresh[t][:], in_=xs_rows[t])

        def place(t):
            nc.vector.tensor_copy(page[t][:].indirect(idx2[:]), fresh[t][:])

        def load_table(a):
            nc.sync.dma_start(out=tab[a][:], in_=tab_words[a].rearrange("p t i -> p (t i)").bitcast(I32))

        def pick_words(a):
            v_codes.append(placed([P, J], U32, "v_codes%d" % a, 16 + 2 * a))
            nc.vector.tensor_copy(v_codes[a][:], tab[a][:].bitcast(U32).indirect(idx[:]))

        def move_scale_rows(queue, a, r):
            queue.dma_start(
                out=v_sc[a][r:P:32, :].bitcast(I32), in_=picked_sc[16 * a + r : 16 * a + 16 : 4, :].bitcast(I32)
            )

        def round_plane(copy, t):
            for h in range(2):
                slot = page_pairs[h][:].rearrange("p (s c e) -> p s c e", s=2, e=2)[:, t // 2, :, t % 2]
                copy(slot, page[t][:, h * BANK : (h + 1) * BANK])

        def load_w1(b):
            raw = placed([P, PACK, PASS], F32, "w1_raw%d" % b, 64 + 8 * b)
            nc.sync.dma_start(
                out=raw[:], in_=w1[:, b * PASS : (b + 1) * PASS].rearrange("(p j) r -> p j r", j=PACK)
            )
            return raw

        page_pairs = [keep.tile([P, PACK * BANK], BF16, name="page_pairs%d" % h, align_bytes=64) for h in range(2)]
        for r in range(4):
            move_scale_rows(nc.gpsimd, 1, r)
        make_identity(nc, identity[:])
        for t in range(2):
            load_plane(t)
            place(t)
            round_plane(nc.scalar.copy, t)
        for r in range(4):
            load_scale_rows(w2_sc_raw, w2_scales, r)
        load_table(0)
        pick_words(0)
        nc.sync.dma_start(out=w2_raw[:].bitcast(I32), in_=w2_words.rearrange("a p c -> p a c").bitcast(I32))
        nc.scalar.copy(
            w2_codes[:].bitcast(U32).rearrange("p (b t g e) -> p b t g e", t=PACK, g=16, e=4),
            w2_raw[:].rearrange("p a c -> p (a c)").bitcast(U32).rearrange("p (b g t e) -> p b t g e", t=PACK, g=16, e=4),
        )
        nc.scalar.copy(
            w2_sc[:].bitcast(U32).rearrange("p (b t g e) -> p b t g e", t=PACK, g=16, e=2),
            w2_sc_raw[:].rearrange("p a c -> p (a c)").bitcast(U32).rearrange("p (b g t e) -> p b t g e", t=PACK, g=16, e=2),
        )
        for t in range(2, PACK):
            load_plane(t)
            for r in range(2):
                move_scale_rows(nc.sync, 0, 2 * (t - 2) + r)
            place(t)
            round_plane(nc.scalar.copy, t)
        w1_raw = [load_w1(0)]
        load_table(1)
        pick_words(1)
        w1_raw.append(load_w1(1))

        def round_w1_aside(dealt, b, t0, t1):
            nc.gpsimd.tensor_scalar(
                dealt[:].rearrange("p (t g e j) -> p g t e j", t=t1 - t0, e=RUN, j=PACK),
                w1_raw[b][:].rearrange("p j (g t e) -> p g t e j", t=PACK, e=RUN)[:, :, t0:t1],
                1.0,
                0.0,
                MULT,
                ADD,
            )

        w1_early = placed([P, PACK * PASS], BF16, "w1_early", 56)
        round_w1_aside(w1_early, 0, 0, PACK)
        b_acc = [bank_tile("b%d" % i, i) for i in range(EARLY)]
        b_rows = [placed([P, J], F32, "b_rows%d" % i, 44 + 2 * i) for i in range(6)]

        def object_pass(i, a):
            col = a * H + i * P
            nc.tensor.matmul_mx(
                out=b_acc[i][:],
                lhsT=w2_codes[:, 2 * col : 2 * (col + P)].bitcast(FP4X4),
                lhsT_scale=w2_sc[:, col : col + P],
                rhs=v_codes[a][:].bitcast(FP8X4),
                rhs_scale=v_sc[a][:],
                start=(a == 0),
                stop=(a == 1),
            )

        def stage(copy, i):
            copy(b_rows[i][:], b_acc[i][:])

        for a in range(2):
            for i in range(EARLY):
                object_pass(i, a)
        for i in range(PACK):
            stage(nc.scalar.copy, i)

        def load_wo(b):
            raw = keep.tile([P, PACK, N], F32, name="wo_raw%d" % b, tag="wo_raw%d" % b)
            rows = wo[b * PASS : (b + 1) * PASS, :].rearrange("(g t e) n -> t g e n", t=PACK, e=RUN)
            for t in range(PACK):
                nc.sync.dma_start(out=raw[:, t, :], in_=rows[t])
            return raw

        def round_wo(grouped, raw, n0, n1):
            nc.scalar.copy(
                grouped[:].rearrange("p (c i t) -> p c t i", i=4, t=PACK)[:, n0 // 4 : n1 // 4],
                raw[:, :, n0:n1].rearrange("p t (c i) -> p c t i", i=4),
            )

        nc.sync.dma_start(idx3[:], offs3)
        wo_raw0 = load_wo(0)
        for b in range(2):
            nc.sync.dma_start(
                out=gain_rows[PACK * b : PACK * (b + 1), :].rearrange("t (g e) -> t g e", e=RUN),
                in_=gain[b * PASS : (b + 1) * PASS].rearrange("(g t e) -> t g e", t=PACK, e=RUN),
            )
        w3_codes = keep.tile([P, 2, N], I32, name="w3_codes", align_bytes=64)
        nc.sync.dma_start(out=w3_codes[:], in_=w3_words.rearrange("a p c i -> p a (c i)").bitcast(I32))
        for q in range(4):
            load_scale_rows(w3_sc, w3_scales, q)
        wo_raw1 = load_wo(1)

        w1_codes = keep.tile([P, PASS], U32, name="w1_codes", tag="fresh3", align_bytes=64)
        w1_scales = placed([P, PASS], U8, "w1_scales", 14)
        quantize((w1_codes[:], w1_scales[:]), w1_early[:])
        w1_q = [(w1_codes[:, t * P : (t + 1) * P], w1_scales[:, t * P : (t + 1) * P]) for t in range(PACK)]

        def quantize_w1(u, codes):
            scales = keep.tile([P, 2 * P], U8, name="w1_scales%d" % u, align_bytes=64)
            quantize((codes[:], scales[:]), w1_late[u][:])
            w1_q.extend((codes[:, t * P : (t + 1) * P], scales[:, t * P : (t + 1) * P]) for t in range(2))

        page_q = [
            mx_tiles("page0", BANK),
            (placed([P, BANK], U32, "page1_codes", 56)[:], keep.tile([P, BANK], U8, name="page1_scales", align_bytes=64)[:]),
        ]
        grouped = [placed([P, PACK * BANK], BF16, "page_grouped%d" % h, 6 + 4 * h) for h in range(2)]
        for h in range(2):
            nc.vector.tensor_copy(
                out=grouped[h][:].bitcast(I32).rearrange("p (c i s) -> p c s i", i=4, s=2),
                in_=page_pairs[h][:].bitcast(I32).rearrange("p (s c i) -> p c s i", i=4, s=2),
            )
        for h in range(2):
            quantize(page_q[h], grouped[h][:])
        stage(nc.vector.tensor_copy, PACK)
        w1_late = [placed([P, 2 * PASS], BF16, "w1_late0", 12), keep.tile([P, 2 * PASS], BF16, name="w1_late1", tag="fresh3", align_bytes=64)]
        late_rows = w1_raw[1][:].rearrange("p j (g t c i) -> p t g c j i", t=PACK, c=2, i=4)

        def round_late(u):
            for k in range(2):
                nc.vector.tensor_copy(
                    w1_late[u][:, k * PASS : (k + 1) * PASS].rearrange("p (g c i j) -> p g c j i", c=2, i=4, j=PACK),
                    late_rows[:, 2 * u + k],
                )

        round_late(0)
        stage(nc.vector.tensor_copy, 5)

        a_rows = [placed([P, T2], F32, "a_rows%d" % i, 80 + 4 * i) for i in range(TILES)]

        def project_page(i):
            for h in range(2):
                acc = bank_tile("a%d_%d" % (i, h), (2 * i + h - 2) % A_BANKS if i else EARLY + h)
                nc.tensor.matmul_mx(
                    out=acc[:],
                    lhsT=w1_q[i][0].bitcast(FP8X4),
                    lhsT_scale=w1_q[i][1],
                    rhs=page_q[h][0].bitcast(FP8X4),
                    rhs_scale=page_q[h][1],
                    start=True,
                    stop=True,
                )
                nc.scalar.copy(a_rows[i][:, h * BANK : (h + 1) * BANK], acc[:])

        def gather(arg, i, j0, j1):
            nc.vector.tensor_tensor(arg, a_rows[i][:].indirect(idx3[:, j0 // 16 : j1 // 16]), b_rows[i][:, j0:j1], ADD)

        args = [placed([P, 2 * J], F32, "arg%d" % pair, (0, 4, 8, 36)[pair]) for pair in range(PACK)]
        sines = [placed([P, PACK, J], F32, "sines%d" % b, 20 + 8 * b) for b in range(2)]

        def gather_whole(i):
            gather(args[i // 2][:, i % 2 * J : (i % 2 + 1) * J], i, 0, J)

        def sine(arg, i, j0, j1):
            b, t = divmod(i, PACK)
            nc.scalar.activation(
                out=sines[b][:, t : t + 2, j0:j1],
                in_=arg.rearrange("p (u j) -> p u j", u=2),
                func=SIN,
                bias=zero_bias[:],
            )

        def weigh(b, j0, j1, gains):
            width = j1 - j0
            weighed = keep.tile([P, width * PACK], BF16, name="h_bf%d_%d" % (b, j0), align_bytes=64)
            nc.vector.tensor_tensor(
                weighed[:].rearrange("p (c i t) -> p c t i", i=4, t=PACK),
                sines[b][:, :, j0:j1].rearrange("p t (c i) -> p c t i", i=4),
                gains[:, PACK * b : PACK * (b + 1)].unsqueeze(1).unsqueeze(3).to_broadcast([P, width // 4, PACK, 4]),
                MULT,
            )
            return weighed

        def quantize_h(name, weighed, width):
            operand = mx_tiles(name, width)
            quantize(operand, weighed[:])
            return operand

        for i in range(PACK):
            project_page(i)
            if i == 0:
                quantize_w1(0, keep.tile([P, 2 * P], U32, name="w1_codes0", align_bytes=64))
            gather_whole(i)
        round_late(1)
        turned = bank_tile("turned", PACK)
        nc.tensor.transpose(turned[:, 0:P], gain_rows[:], identity[:])
        wo_q = [mx_tiles("wo%d" % b, N) for b in range(2)]
        sine(args[0][:], 0, 0, J)
        quantize_w1(1, placed([P, 2 * P], U32, "w1_codes1", 0))
        project_page(4)
        gather_whole(4)
        for i in range(EARLY, TILES):
            b_acc.append(bank_tile("b%d" % i, i))
            for a in range(2):
                object_pass(i, a)
        sine(args[1][:], 2, 0, J)
        wo_bf = [placed([P, N * PACK], BF16, "wo_bf0", 50), placed([P, N * PACK], BF16, "wo_bf1", 92)]
        h0_bf = weigh(0, 0, J, turned)
        nc.gpsimd.tensor_scalar(
            wo_bf[0][:].rearrange("p (n t) -> p n t", t=PACK)[:, 0:ASIDE],
            wo_raw0[:].rearrange("p t n -> p n t")[:, 0:ASIDE],
            1.0,
            0.0,
            MULT,
            ADD,
        )
        for i in range(5, TILES):
            project_page(i)
            if i > 5:
                b_rows.append(placed([P, J], F32, "b_rows%d" % i, 4 + 2 * (i - 6)))
                stage(nc.scalar.copy, i)
        gains = placed([P, TILES], F32, "gains", 46)
        nc.scalar.copy(gains[:], turned[:, 0:TILES])
        gather_whole(5)
        h0 = quantize_h("h0", h0_bf, J)
        round_wo(wo_bf[0], wo_raw0, ASIDE, N)
        sine(args[2][:], PACK, 0, J)
        quantize(wo_q[0], wo_bf[0][:])
        for u in range(2):
            for k in range(2):
                first = u * J + k * HALF
                gather(args[3][:, first : first + HALF], 6 + k, u * HALF, (u + 1) * HALF)
        sine(args[3][:, 0:J], 6, 0, HALF)
        round_wo(wo_bf[1], wo_raw1, 0, HALF)
        sine(args[3][:, J : 2 * J], 6, HALF, J)
        round_wo(wo_bf[1], wo_raw1, HALF, N)

        d_first = placed([P, 2, HALF], F32, "d_first", 54)
        d_later = keep.tile([P, 3, 2, HALF], F32, name="d_later", tag="wo_raw1")
        d_rows = [d_first[:]] + [d_later[:, k] for k in range(3)]

        def modulation(u, pair):
            acc = bank_tile("d%d_%d" % (u, pair), 4 + (2 * u + pair + 1) % 4)
            cols = slice(u * HALF, (u + 1) * HALF)
            for k in range(2):
                nt = 2 * pair + k
                for a in range(2):
                    nc.tensor.matmul_mx(
                        out=acc[:, k * HALF : (k + 1) * HALF],
                        lhsT=w3_codes[:, a, nt * P : (nt + 1) * P].bitcast(FP8X4),
                        lhsT_scale=w3_sc[:, a, nt * P : (nt + 1) * P],
                        rhs=v_codes[a][:, cols].bitcast(FP8X4),
                        rhs_scale=v_sc[a][:, cols],
                        start=(a == 0),
                        stop=(a == 1),
                    )
            nc.scalar.copy(d_rows[2 * u + pair], acc[:].rearrange("p (k j) -> p k j", k=2))

        out_rows = out.rearrange("(nt p) j -> p nt j", p=P)

        def y_passes(acc, pair, b, operand, cols):
            for u in range(2):
                nt = 2 * pair + u
                nc.tensor.matmul_mx(
                    out=acc[:, u * HALF : (u + 1) * HALF],
                    lhsT=wo_q[b][0][:, nt * P : (nt + 1) * P].bitcast(FP8X4),
                    lhsT_scale=wo_q[b][1][:, nt * P : (nt + 1) * P],
                    rhs=operand[0][:, cols].bitcast(FP8X4),
                    rhs_scale=operand[1][:, cols],
                    start=(b == 0 and u == 0),
                    stop=(b == 1 and u == 1),
                )

        y_acc = [[bank_tile("y%d_%d" % (u, pair), 2 * u + pair) for pair in range(2)] for u in range(2)]
        for u in range(2):
            for pair in range(2):
                modulation(u, pair)
        for u in range(2):
            for pair in range(2):
                y_passes(y_acc[u][pair], pair, 0, h0, slice(u * HALF, (u + 1) * HALF))

        def finish(u, pair):
            cols = slice(u * HALF, (u + 1) * HALF)
            rows = slice(2 * pair, 2 * pair + 2)
            result = keep.tile([P, 2, HALF], F32, name="result%d_%d" % (u, pair))
            acc = y_acc[u][pair][:].rearrange("p (k j) -> p k j", k=2)
            nc.vector.tensor_tensor(result[:], acc, d_rows[2 * u + pair], MULT)
            if pair == 1 and u == 1:
                for k, queue in enumerate((nc.scalar, nc.sync)):
                    queue.dma_start(out=out_rows[:, 2 * pair + k, cols], in_=result[:, k, :])
            else:
                nc.sync.dma_start(out=out_rows[:, rows, cols], in_=result[:])

        def quantize_wo(pair):
            cols = slice(pair * HALF, (pair + 1) * HALF)
            rounded = wo_bf[1][:, pair * HALF * PACK : (pair + 1) * HALF * PACK]
            quantize((wo_q[1][0][:, cols], wo_q[1][1][:, cols]), rounded)

        first_half = weigh(1, 0, HALF, gains)
        quantize_wo(0)
        h1 = quantize_h("h1_0", first_half, HALF)
        y_passes(y_acc[0][0], 0, 1, h1, slice(0, HALF))
        second_half = weigh(1, HALF, J, gains)
        quantize_wo(1)
        y_passes(y_acc[0][1], 1, 1, h1, slice(0, HALF))
        finish(0, 0)
        h1 = quantize_h("h1_1", second_half, HALF)
        for pair in range(2):
            y_passes(y_acc[1][pair], pair, 1, h1, slice(0, HALF))
        finish(0, 1)
        for pair in range(2):
            finish(1, pair)
